import numpy as np, ml_dtypes
CORES = [6,15,38,47]
N = 4
BF = ml_dtypes.bfloat16
W, SV, M, HOPS = 4096, 1024, 256, [1, 1, 1, 1]
RO = len(HOPS) + 1
def names(rng, power, *shape):
    return np.minimum((W * rng.random(shape) ** power).astype(np.int64), W - 1)
def pairs(rng, C, power):
    a = names(rng, power, N, 8, 16, C); b = np.take_along_axis(a, np.argsort(rng.random((N, 8, 16, C)), axis=2), 2)
    share = rng.choice(np.array([0.0, 0.15, 0.5, 1.0]), (N, 8, 1, C)); b = np.where(rng.random(b.shape) < share, b, names(rng, power, N, 8, 16, C))
    fa = rng.choice(np.array([0.05, 0.12, 0.3, 0.7, 1.0]), (N, 8, 1, C), p=[0.2, 0.25, 0.2, 0.2, 0.15])
    fb = rng.choice(np.array([0.0, 0.3, 0.7, 1.0]), (N, 8, 1, C), p=[0.05, 0.25, 0.3, 0.4])
    return np.where(rng.random(a.shape) < fa, a, -1), np.where(rng.random(b.shape) < fb, b, -1)
def parts(rng, power):
    clk = rng.integers(0, 256, (N, 8, 16, W)); z = rng.integers(0, 256, (N, 8, 16, M)); th = rng.integers(1200, 1600, (N, 8))
    sc, st = pairs(rng, SV, power); d, t = pairs(rng, M, power)
    return clk, sc, st, d, t, z, th
def pack(clk, sc, st, d, t, z, th):
    return {"clk": clk.reshape(N, 128, W).astype(np.float32).astype(BF), "sc": sc.reshape(N, 128, SV).astype(np.int32), "st": st.reshape(N, 128, SV).astype(np.int32),
            "dl": d.reshape(N, 128, M).astype(np.int32), "tl": t.reshape(N, 128, M).astype(np.int32), "z0": z.reshape(N, 128, M).astype(np.float32).astype(BF),
            "th": np.repeat(th.reshape(N, 8), 16, axis=1).reshape(N, 128, 1).astype(np.int32)}
def setup_inputs(rng):
    return pack(*parts(rng, 1))
def setup_inputs_spread(rng):
    clk, sc, st, d, t, z, th = parts(rng, 4)
    clk = np.floor(np.exp2(8 * rng.random((N, 8, 1, W))) * rng.random((N, 8, 16, W))).astype(np.int64)
    z = np.floor(np.exp2(8 * rng.random((N, 8, 1, M))) * rng.random((N, 8, 16, M))).astype(np.int64)
    th = np.minimum(np.floor(np.exp2(12 * rng.random((N, 8)))).astype(np.int64), 4080)
    return pack(np.minimum(clk, 255), sc, st, d, t, np.minimum(z, 255), th)
def setup_inputs_ends(rng):
    def rec(C):
        p = rng.choice(np.array([0.0, 0.06, 0.5, 1.0]), (N, 8, 1, C)); s = (N, 8, 16, C)
        a = np.where(rng.random(s) < p, W - 1, -1)
        o = np.where(rng.random(s) < 0.3, -1, np.where(rng.random(s) < 0.15, W - 1, rng.integers(0, W, s)))
        return np.where(rng.random((N, 8, 1, C)) < 0.6, a, o)
    def half(C):
        k = rng.integers(0, 3, (N, 8, 1, C))
        return np.where(k == 0, 0, np.where(k == 1, 255, 255 * rng.integers(0, 2, (N, 8, 16, C))))
    clk = half(W); z = half(M); sc = rec(SV); st = rec(SV); d = rec(M); t = rec(M)
    g = np.arange(8)[None, :]; q = np.arange(N)[:, None]
    clk[..., 0] = 255; clk[..., W - 1] = np.where(((g + q + N) & 1) == 0, 255, 0)[:, :, None]
    clk[..., W - 2] = 255; clk[:, :, 15, W - 2] = 254
    z[..., 0] = 255; z[..., M - 1] = 255; z[..., M - 2] = 0
    th = 4080 * ((g // 2 + q + rng.integers(0, 2, (N, 1))) & 1); th[:, 5] = 4080
    for m, lo, hi in ((M - 1, 0, W - 1), (0, W - 1, 0)):
        d[..., m] = -1; d[:, :, 15, m] = W - 1; d[:, :, 4, m] = 5; t[..., m] = -1; t[:, :, 2, m] = lo; t[:, :, 15, m] = hi
    s = slice(M - 6, M - 2); z[..., s] = 255; d[:, :, 15, s] = W - 1; t[..., s] = -1; t[:, :, 2, s] = W - 2; t[:, :, 15, s] = 0
    d[:, 5] = W - 1; t[:, 5] = W - 1; sc[:, 5] = W - 1; st[:, 5] = W - 1; z[:, 5] = z[:, 5, :1]
    return pack(clk, sc, st, d, t, z, th)
def setup_inputs_corners(rng):
    clk, sc, st, d, t, z, th = parts(rng, 1)
    clk[:, 1::2, :, 1::2] = clk[:, 1::2, :, 0::2]
    th = rng.choice(np.array([0, 1, 126, 128, 1000, 1999, 4080]), (N, 8)); th[:, 0] = 1000; th[:, 7] = 1999; th[:, 3] = 0
    th[:, 5] = 2051 + 4 * rng.integers(0, 100, N); th[:, 6] = 2052 + 4 * rng.integers(0, 100, N)
    lanes = np.array([0, 1, SV - 1, SV, W - 2, W - 1])
    for q in range(N):
        for g in range(8):
            kind = rng.permutation(M) % 10; n = np.where(rng.random(M) < 0.5, rng.choice(lanes, M), rng.integers(0, W, M)); full = rng.integers(0, W, (16, M))
            D = d[q, g]; T = t[q, g]; x = clk[q, g][:, n]; room = np.maximum(x, 255 - x)
            gap = np.maximum(int(th[q, g]) + rng.integers(-1, 2, M), 0); step = np.clip(gap[None, :] - (np.add.accumulate(room, axis=0) - room), 0, room)
            near = np.where(x < 128, x + step, x - step)
            s = kind == 0; D[:, s] = -1; T[:, s] = -1; T[15, s] = n[s]
            s = kind == 1; D[:, s] = -1; T[:, s] = -1
            s = kind == 2; D[:, s] = full[:, s]; T[:, s] = -1
            s = kind == 3; D[:, s] = full[:, s]; T[:, s] = full[::-1][:, s]
            s = kind == 4; D[:, s] = n[s]; T[:, s] = -1; T[15, s] = n[s]
            s = kind == 5; D[:, s] = full[:, s] & ~1; T[:, s] = full[::-1][:, s] | 1
            s = kind == 6; D[:, s] = -1; D[15, s] = n[s]; T[:, s] = -1; T[0, s] = n[s]
            s = kind == 7; D[:, s] = -1; D[0, s] = n[s]; T[:, s] = -1; T[15, s] = n[s] ^ 1
            s = kind == 8; D[:, s] = -1; D[7, s] = n[s]; D[8, s] = (n[s] + 5) % W; T[:, s] = -1; T[15, s] = n[s]; T[3, s] = n[s] ^ 1
            s = kind == 9; D[:, s] = n[s]; D[0, s] = n[s] ^ 1; T[:, s] = n[s]
            s = (kind == 4) | (kind == 6) | (kind == 8) | (kind == 9); z[q, g][:, s] = near[:, s]
    k = rng.integers(0, 6, (N, 8, 1, SV)); more = rng.integers(0, W, (2, N, 8, 16, SV))
    st = np.where(k == 4, sc[:, :, ::-1], st)
    sc = np.where((k == 0) | (k == 2), -1, np.where(k == 1, more[0], sc)); st = np.where((k == 0) | (k == 3), -1, np.where(k == 1, more[1], st))
    return pack(clk, sc, st, d, t, z, th)
def setup_inputs_crowd(rng):
    clk, sc, st, d, t, z, th = parts(rng, 1); h = SV >> 1
    def high(*shape):
        return h + rng.integers(0, h - 1, shape) + SV * rng.integers(0, W // SV, shape)
    for q in range(N):
        for g in (0, 1):
            keep = d[q, g, :, M - 1].copy(), z[q, g, :, M - 1].copy()
            z[q, g] = rng.permuted(np.repeat(rng.integers(0, 256, (16, 1)), M, axis=1), axis=0); t[q, g] = -1
            if g == 1: d[q, g, :, M - 1], z[q, g, :, M - 1] = keep; t[q, g, 15, M - 1] = W - 1
        for g in (2, 3):
            v = int(rng.choice(np.array([0, SV - 1, SV >> 1]))); n = v + SV * rng.integers(0, W // SV, (16, M))
            t[q, g] = np.where(rng.random((16, M)) < 0.5, n, -1); t[q, g, 9] = n[9]; d[q, g] = -1
            if g == 3: d[q, g, 15, M - 1] = (v + 1) % W
        for g in (6, 7):
            n = rng.integers(0, W, M); z[q, g] = clk[q, g][:, n]; t[q, g, 5] = n
            d[q, g] = -1; d[q, g, 15] = n
            if g == 7: d[q, g, 15, M - 1] = -1
    for g, c, lim in ((4, 20, 219), (5, 35, 212)):
        clk[:, g] = rng.integers(0, 8, (N, 16, W)); clk[:, g, :, W - 1] = c
        d[:, g] = high(N, 16, M); t[:, g] = rng.permuted(d[:, g], axis=1)
        sc[:, g, :, :h] = high(N, 16, h); st[:, g, :, :h] = rng.permuted(sc[:, g, :, :h], axis=1)
        z[:, g] = rng.integers(0, 7, (N, 16, M))
        for q in range(N):
            z[q, g, :, M - 1] = 6 + (np.arange(16) < 4 + q)
            b = (q + int(np.sum(HOPS[:-1]))) % N; sc[b, g, :, 100 + q] = W - 1; st[b, g, :, 100 + q] = W - 1
            th[(b + HOPS[-1]) % N, g] = lim - q
    d[:, 5, 15, 0] = -1
    return pack(clk, sc, st, d, t, z, th)
def check_inputs(d):
    bad = []
    for k, lo, hi in (("clk", 0, 255), ("z0", 0, 255), ("sc", -1, W - 1), ("st", -1, W - 1), ("dl", -1, W - 1), ("tl", -1, W - 1), ("th", 0, 4080)):
        a = np.asarray(d[k]).astype(np.float64)
        if not (np.min(a) >= lo and np.max(a) <= hi): bad.append("range of " + k)
        elif np.any(a != np.floor(a)): bad.append("whole numbers in " + k)
    h = np.asarray(d["th"]).reshape(-1, 16)
    if np.any(h != h[:, :1]): bad.append("th alike in a group")
    return bad
def reference(clk, sc, st, dl, tl, z0, th):
    X = clk.astype(np.float32).astype(np.int64).reshape(N, 8, 16, W); Z = z0.astype(np.float32).astype(np.int64).reshape(N, 8, 16, M)
    C = sc.astype(np.int64).reshape(N, 8, 16, SV); S = st.astype(np.int64).reshape(N, 8, 16, SV)
    D = dl.astype(np.int64).reshape(N, 8, 16, M); T = tl.astype(np.int64).reshape(N, 8, 16, M)
    base = th.astype(np.int64).reshape(N, 8, 16)[:, :, 0]; A = np.zeros((N, 8), np.int64); row = np.arange(16).reshape(1, 16, 1)
    for visit in range(RO):
        nd, nt, nz = [], [], []
        for a in range(N):
            d, t, z = D[a], T[a], Z[a]
            x = np.take_along_axis(X[a], np.maximum(d, 0).reshape(8, 1, 16 * M), 2).reshape(8, 16, 16, M)
            y = np.take_along_axis(X[a], np.maximum(t, 0).reshape(8, 1, 16 * M), 2).reshape(8, 16, 16, M)
            dist = np.sum(np.abs(x - z[:, :, None, :]), axis=1)
            score = np.where(t >= 0, np.sum(np.minimum(y, z[:, :, None, :]), axis=1), -1)
            ks = np.argmax(score, axis=1)
            has = np.any(t >= 0, axis=1); v = np.take_along_axis(t, ks[:, None, :], 1)[:, 0] & (SV - 1)
            eq = (d[:, :, None, :] == t[:, None, :, :]) & (d >= 0)[:, :, None, :]
            cd = np.any(eq, axis=2); ct = np.any(eq, axis=1)
            lim = base[a] + 8 * (A[a] & 31)
            abort = np.any(cd & (dist > lim[:, None, None]), axis=1)
            d1 = np.where(cd, -1, d); t1 = np.where(ct | (row == ks[:, None, :]), -1, t)
            left = np.any(d1 >= 0, axis=1); proof = has & ~abort & ~left; go = has & ~abort & left
            yk = np.take_along_axis(y, ks[:, None, None, :], 2)[:, :, 0]
            top = np.max(np.where((d1 >= 0)[:, None, :, :], x, 0), axis=2)
            cv = np.take_along_axis(C[a], v[:, None, :], 2); sv = np.take_along_axis(S[a], v[:, None, :], 2)
            u = np.sum(z, axis=1) & (SV - 1)
            cu = np.take_along_axis(C[a], u[:, None, :], 2); su = np.take_along_axis(S[a], u[:, None, :], 2)
            hd = np.any(cv[:, :, None, :] == d[:, None, :, :], axis=2); ht = np.any(sv[:, :, None, :] == t[:, None, :, :], axis=2)
            d2 = np.where((d1 < 0) & ~hd, cv, d1); t2 = np.where((t1 < 0) & ~ht, sv, t1)
            ab = abort[:, None, :]; on = go[:, None, :]
            nd.append(np.where(ab, cv, np.where(on, d2, cu))); nt.append(np.where(ab, sv, np.where(on, t2, su)))
            nz.append(np.where(ab, np.abs(z - yk), np.where(on, (yk + top) >> 1, z)))
            A[a] += np.sum(cd & ~ab, axis=(1, 2))
            for g in range(8):
                for m in np.nonzero(proof[g])[0]: C[a, g, :, v[g, m]] = t1[g, :, m]
        D, T, Z = np.stack(nd), np.stack(nt), np.stack(nz)
        if visit < RO - 1: D, T, Z = [np.roll(b, HOPS[visit], axis=0) for b in (D, T, Z)]
    return {"yd": D.reshape(N, 128, M).astype(np.float32), "yt": T.reshape(N, 128, M).astype(np.float32), "yz": Z.reshape(N, 128, M).astype(np.float32), "ys": C.reshape(N, 128, SV).astype(np.float32)}

@@ -1,0 +1,501 @@
+from concourse.mybir import AluOpType, ActivationFunctionType
+
+A, F = AluOpType, ActivationFunctionType
+NV = 5
+f32, f16, b16, i32, u16 = "float32", "float16", "bfloat16", "int32", "uint16"
+SCRATCH, ALIAS = {}, {}
+
+
+def _decl(text, d, lead):
+    for w in text.split():
+        n, s = w.split(":")
+        SCRATCH[n] = ("sbuf", [128] + lead + [int(x) for x in s.split(",")], d)
+
+
+_decl("tli:256 dli:256 thi:1 sci:1024 sti:1024 pidx:1 pmi:1 ai:1 a31:1", i32, [])
+_decl("tm0:256 ts0:256 stm:1024 sta:1024 stw:1024 scw:1280 pmf:1 iq:384 P1:16 on32:128 boa:128 bo32:128 id32:128 "
+      "q0i:16 q0:16 thn:1 nlim:8 asum:16 T1s:256 pr:16 dvq:16 mvq:16 PV:16 PVs:256 lm:16 dq2:16 lq:16 PLf:16 od:256 ot:256 oz:256 cst:5", f32, [])
+_decl("selm:2048 bc:2048 dM:384 tri:256 PV16:16 eqP:256", f16, [])
+_decl("clkw:4112 rst:2048 rs:128 rowc:128 k8big:128", b16, [])
+_decl("PLu:32", u16, [])
+_decl("eqA:2048 eqB:2048 eqC:2048 Dq:512 Tq:512 D1:128 KD:128 CD:128 T1a:128 CT:128 FC:128 oh:128 KT:128 T1:128 KTf:128 LMs:384 "
+      "cw:128 sw:128 hf:128 dst:128", f16, [2])
+_decl("Y:2048 GA:16,128 XG:2048 xs:2048 rl:128 OHn:128 SG:128 SA:128 ac:128 acr:128 cmA:128 cmB:128 cmC:128 ysb:128 zg:128 yg:128 "
+      "sdB:512 sdC:512 seB:512 seC:512", b16, [2])
+_decl("sk:128 sk2:128 a1:8 dvu:8 ms:8 wf:8 C1:128 C1t:128 Dm:128 Tm:128", f32, [2])
+_decl("nu:16 nv:16", i32, [2])
+_decl("D1u:128 nlu:8 wu:8", u16, [2])
+_decl("dt:128 tt:128 sd:128 stt:128", u16, [2 * NV])
+_decl("zl:128 sz:128", b16, [2 * NV])
+for _b, _l, _d in (("kh", "I16 In16 Im16 BOm16 BO16 BO128 BOm128 c2048 c2040 c16320n I8n o128h cm2047", f16),
+                   ("kb", "Ib Ibn Ibh Ib512n Ib256 Ib256n Ib4096n Ib65536 I4128n BO64b BOb c67584 cm4096 o128b", b16)):
+    _l = _l.split()
+    SCRATCH[_b] = ("sbuf", [128, len(_l), 128], _d)
+    for _i, _n in enumerate(_l):
+        ALIAS[_n] = (_b, _i)
+for _n in ("pc", "po", "pk", "r0", "r1", "r2"):
+    SCRATCH[_n] = ("psum", [128, 512], f32)
+SCRATCH["pg0"] = SCRATCH["pg1"] = ("psum", [128, 8, 64], f32)
+BK = dict(cnt="po", dist="pk", ca="po", key="r2", oh="r2", lm="pc", ll="r2", tot="pc", h="r2", cc="r2", z="pc", d="po", d2="pk")
+LOADS = ("tl", "dl", "za", "zb", "th", "clk", "st", "sc")
+SEMAPHORES = ["sv", "ss", "sp", "sg", "so", "ls"] + ["l_" + n for n in LOADS]
+SEMAPHORES += ["a%d%d%s" % (t, h, k) for t in range(1, NV) for h in (0, 1) for k in "dtz"]
+CYC, OVV, OVS, WAKE, SELF, REMOTE, LOOK = 1.0, 10.0, 20.0, 70.0, 100.0, 4000.0, 20.0
+BIAS = {"D": -5.0, "B0": 20.0, "B1": 60.0, "A1": -5.0, "C1": -5.0}
+
+
+def R(name, *ix):
+    return (ALIAS[name][0], (ALIAS[name][1],) + ix) if name in ALIAS else (name, ix)
+
+
+def S_(a, b, st=None):
+    return slice(a, b, st)
+
+
+def blk(i, n=128):
+    return slice(n * i, n * i + n)
+
+
+def get(T, x):
+    return T[x[0]][(slice(None),) + x[1] + (slice(None),) * (len(SCRATCH[x[0]][1]) - 1 - len(x[1]))]
+
+
+def span(x):
+    out = []
+    for d, n in enumerate(SCRATCH[x[0]][1][1:]):
+        i = x[1][d] if d < len(x[1]) else slice(None)
+        if isinstance(i, int):
+            out.append((i, i + 1, 1))
+        else:
+            a, b, st = i.indices(n)
+            out.append((a, b, len(range(a, b, st))))
+    return out
+
+
+def size(x):
+    n = 1
+    for s in span(x):
+        n *= s[2]
+    return n
+
+
+def psum(x):
+    return SCRATCH[x[0]][0] == "psum"
+
+
+def two(*xs):
+    return all(not psum(x) and SCRATCH[x[0]][2] in (f16, b16, u16) for x in xs)
+
+
+def program(nrem):
+    ops, rc, lab = [], [0], [""]
+
+    def add(e, dur, fn, r, w, **kw):
+        ops.append(dict(kw, g=lab[0], e=e, d=dur, fn=fn, r=[x for x in r if isinstance(x, tuple)], w=w))
+        return len(ops) - 1
+
+    def val(T, x):
+        return get(T, x) if isinstance(x, tuple) else x
+
+    def ts(o, i, s1, op0, s2=None, op1=None):
+        def fn(g, T):
+            a = (get(T, o), get(T, i), val(T, s1), val(T, s2), op0)
+            return g.vector.tensor_scalar(*(a if op1 is None else a + (op1,)))
+        add("V", OVV + max(64, size(o) * (0.5 if two(o, i) else 1)) * CYC, fn, [i, s1, s2], [o])
+
+    def tt(o, a, b, op):
+        add("V", OVV + max(64, size(o) * (1 if psum(a) or psum(b) else 2)) * CYC,
+            lambda g, T: g.vector.tensor_tensor(get(T, o), get(T, a), get(T, b), op), [a, b], [o])
+
+    def cp(o, i):
+        add("V", OVV + max(64, size(o)) * CYC, lambda g, T: g.vector.tensor_copy(get(T, o), get(T, i)), [i], [o])
+
+    def fill(o, v):
+        add("V", OVV + max(64, size(o)) * CYC, lambda g, T: g.vector.memset(get(T, o), v), [], [o])
+
+    def scan(o, a, b):
+        add("V", OVV + size(o) * (0.5 if two(o, a, b) else 1) * CYC,
+            lambda g, T: g.vector.tensor_tensor_scan(get(T, o), get(T, a), get(T, b), 0.0, A.mult, A.max), [a, b], [o])
+
+    def act(o, i, func, bias=0.0, scale=1.0, acc=None):
+        def fn(g, T):
+            kw = {} if acc is None else {"accum_out": get(T, acc)}
+            return g.scalar.activation(get(T, o), get(T, i), func, bias=val(T, bias), scale=scale, **kw)
+        add("S", OVS + max(64, size(o)) * CYC, fn, [i, bias], [o] + ([] if acc is None else [acc]))
+
+    def gat(e, o, win, off):
+        def fn(g, T):
+            x = get(T, win).indirect(get(T, off))
+            if e == "S":
+                return g.scalar.activation(get(T, o), x, F.Copy)
+            return g.vector.tensor_copy(get(T, o), x) if win[0] == "stw" else g.vector.tensor_scalar(get(T, o), x, -2047.0, None, A.add)
+        add(e, 75 + 1.5 * size(o) * CYC, fn, [win, off], [o])
+
+    def mm(lst):
+        def fn(g, T):
+            x = None
+            for o, l, r, a, b in lst:
+                x = g.tensor.matmul(get(T, o), get(T, l), get(T, r), a, b)
+            return x
+        d = sum(6 + max(64, size(m[0])) * 0.5 * (4 if SCRATCH[m[1][0]][2] == f32 else 1) for m in lst)
+        add("P", 30 + d, fn, [m[1] for m in lst] + [m[2] for m in lst], [m[0] for m in lst])
+
+    def chain(o, *pairs):
+        return [(o, l, r, i == 0, i == len(pairs) - 1) for i, (l, r) in enumerate(pairs)]
+
+    def load(q, name, o, src, dur):
+        add(q, 60, lambda g, T: (g.sync if q == "Y" else g.scalar).dma_start(get(T, o), src(T)), [], [o], tok="l_" + name, lat=dur)
+    load("S", "clk", R("clkw", S_(16, 4112)), lambda T: T.clk[:, :], 5000)
+    load("Y", "tl", R("tli"), lambda T: T.tl[:, :], 2200)
+    load("Y", "dl", R("dli"), lambda T: T.dl[:, :], 2500)
+    load("Y", "za", R("zl", 0), lambda T: T.z0[:, 0:128], 2600)
+    load("Y", "zb", R("zl", 1), lambda T: T.z0[:, 128:256], 2700)
+    load("Y", "th", R("thi"), lambda T: T.th[:, :], 2800)
+    load("Y", "st", R("sti"), lambda T: T.st[:, :], 6500)
+    load("Y", "sc", R("sci"), lambda T: T.sc[:, :], 8000)
+
+    def iota(o, pat, base, cm=0):
+        kw = {} if SCRATCH[o[0]][2] == i32 else {"allow_small_or_imprecise_dtypes": True}
+        add("G", 130 + 2 * size(o), lambda g, T: g.iota(get(T, o), pat, base, cm, **kw), [], [o])
+
+    def aff(o, i, pat, op, base, cm, other=0.0):
+        add("G", 170 + 2 * size(o), lambda g, T: g.affine_select(get(T, o), get(T, i), pat, op, other, base, cm), [i], [o])
+    fill(R("on32"), 1.0)
+    iota(R("pidx"), [[0, 1]], 0, 1)
+    aff(R("boa"), R("on32"), [[-16, 8], [0, 16]], A.is_ge, 0, 1)
+    aff(R("bo32"), R("boa"), [[16, 8], [0, 16]], A.is_ge, 15, -1)
+    aff(R("id32"), R("on32"), [[-1, 128]], A.is_equal, 0, 1)
+    iota(R("iq"), [[0, 24], [1, 16]], 0)
+    iota(R("rowc"), [[0, 8], [-1, 16]], 16)
+    iota(R("q0i"), [[16, 16]], 1024)
+    ts(R("pmi"), R("pidx"), 15, A.bitwise_and)
+    cp(R("pmf"), R("pmi"))
+    pm = R("pmf", S_(0, 1))
+    ts(R("P1"), R("iq", S_(0, 16)), pm, A.is_equal)
+    for j in range(16):
+        ts(R("bc", blk(j)), R("bo32"), R("P1", S_(j, j + 1)), A.mult)
+    fill(R("clkw", S_(0, 16)), -1.0)
+    for n, src, k in (("I16", "id32", 1), ("In16", "id32", -1), ("Im16", "id32", -4112), ("BO16", "bo32", 1), ("BOm16", "bo32", -4112),
+                      ("BOm128", "bo32", -128), ("BO128", "bo32", 128),
+                      ("Ib", "id32", 1), ("Ibn", "id32", -1), ("I4128n", "id32", -4128), ("BOb", "bo32", 1), ("BO64b", "bo32", 64),
+                      ("Ibh", "id32", 0.5), ("Ib512n", "id32", -512), ("Ib256", "id32", 256), ("I8n", "id32", -8), ("k8big", "bo32", 8),
+                      ("Ib256n", "id32", -256), ("Ib4096n", "id32", -4096), ("Ib65536", "id32", 65536)):
+        if ALIAS.get(n, ("kb",))[0] == "kb":
+            act(R(n), R(src), F.Copy, scale=float(k))
+        else:
+            ts(R(n), R(src), float(k), A.mult)
+    for j in range(16):
+        aff(R("selm", blk(j)), R("BOm16"), [[0, 8], [1, 16]], A.is_equal, -j, 0)
+    iota(R("rst"), [[0, 128], [1, 16]], 0)
+    aff(R("rst"), R("rst"), [[0, 128], [1, 16]], A.is_equal, 0, 0, 1.0)
+    for n, x in (("c2048", 2048.0), ("o128b", 1.0 / 128), ("o128h", 1.0 / 128), ("cm2047", -2047.0), ("c2040", 2040.0), ("c16320n", -16320.0),
+                 ("c67584", 67584.0), ("cm4096", -4096.0), ("rs", 1.0)):
+        fill(R(n), x)
+    fill(R("rs", S_(0, 128, 16)), 0.0)
+    for i, x in enumerate((64.5, 0.5, -256.0, -1024.0, 1.0)):
+        fill(R("cst", S_(i, i + 1)), x)
+    ts(R("dM"), R("iq"), pm, A.is_equal)
+    ts(R("tri"), R("iq", S_(0, 256)), pm, A.is_ge, 5000.0, A.mult)
+    ts(R("q0"), R("q0i"), pm, A.add)
+    ts(R("tm0"), R("tli"), 0.0, A.min, 2.0, A.mult)
+    tt(R("ts0"), R("tli"), R("tm0"), A.add)
+    for h in (0, 1):
+        ts(R("tt", h), R("ts0", blk(h)), 16.0, A.add)
+        ts(R("dt", h), R("dli", blk(h)), 16.0, A.add)
+    ts(R("thn"), R("thi"), -1.0, A.mult)
+    cp(R("nlim", S_(0, 1)), R("thn"))
+    for k in range(2):
+        c = blk(k, 512)
+        ts(R("stm", c), R("sti", c), 0.0, A.min, 2.0, A.mult)
+        tt(R("sta", c), R("sti", c), R("stm", c), A.add)
+        act(R("stw", c), R("sta", c), F.Copy, bias=-2047.0)
+    cp(R("scw", S_(0, 1024)), R("sci"))
+
+    WIN = R("clkw")
+    sent = {}
+
+    def arrive(t, h, kind, buf):
+        if t:
+            add("R", 0, None, [], [R(buf, 2 * t + h)], tok="a%d%d%s" % (t, h, kind), inc=nrem, after=sent[(t - 1, h, kind)])
+
+    def send(t, h, kind, src, buf):
+        def fn(g, T):
+            return get(T, R(buf, 2 * t + h + 2)), get(T, R(src, 2 * t + h)), "a%d%d%s" % (t + 1, h, kind)
+        sent[(t, h, kind)] = add("G", 100, fn, [R(src, 2 * t + h)], [], n="send")
+
+    def member(rows, held, eq, h):
+        for q in range(4):
+            rc[0] += 1
+            b = "r%d" % (rc[0] % 2)
+            if q == 0 and eq != "eqA":
+                mm(sum([chain(R(b, blk(i)), (R("bc", blk(i)), R(rows, h, S_(0, 128))), (R("In16"), R(held, h, S_(0, 128)))) for i in range(4)], []))
+                act(R("sd" + eq[2], h), R(b, S_(0, 512)), F.Abs)
+                act(R("se" + eq[2], h), R("sd" + eq[2], h), F.Relu, bias=R("cst", S_(4, 5)), scale=-1.0)
+            else:
+                mm([(R(b, blk(i)), R("bc", blk(4 * q + i)), R(rows, h, S_(0, 128)), True, True) for i in range(4)])
+                tt(R(eq, h, blk(q, 512)), R(held, h, S_(0, 512)), R(b, S_(0, 512)), A.is_equal)
+
+    def counts(eq, cm, h, b):
+        def one(j):
+            return (R("se" + eq[2], h, blk(j)), R("BOb", S_(0, 128, 16))) if j < 4 and eq != "eqA" else (R(eq, h, blk(j)), R("BO16", S_(0, 128, 16)))
+        mm([(R(b, S_(384 + j, 512, 16)),) + one(j) + (True, True) for j in range(16)])
+        act(R(cm, h), R(b, S_(384, 512)), F.Copy)
+        return (R(cm, h), R("I4128n"))
+
+    def stageA(t, h):
+        k = 2 * t + h
+        arrive(t, h, "t", "tt")
+        arrive(t, h, "d", "dt")
+        arrive(t, h, "z", "zl")
+        for hb in (0, 1):
+            gat("S", R("Y", h, blk(hb, 1024)), WIN, R("tt", k, blk(hb, 64)))
+        for dst, src in (("Tq", "tt"), ("Dq", "dt")):
+            for r in range(4):
+                ts(R(dst, h, blk(r)), R(src, k), -2063.0, A.add)
+        D, Tn = R("Dq", h, S_(0, 128)), R("Tq", h, S_(0, 128))
+        member("Tq", "Dq", "eqA", h)
+        pD, pT, c = R(BK["cnt"], S_(0, 128)), R(BK["cnt"], S_(128, 256)), (R("I16"), R("c2048"))
+        mm(chain(pD, c, *[(R("Im16"), R("eqA", h, blk(j))) for j in range(16)]))
+        mm(chain(pT, c, counts("eqA", "cmA", h, BK["ca"])))
+        tt(R("D1", h), D, pD, A.min)
+        tt(R("T1a", h), Tn, pT, A.min)
+        ts(R("D1u", h), R("D1", h), -2048.0, A.max, 2063.0, A.add)
+        ts(R("CT", h), R("T1a", h), -2055.0, A.is_lt)
+        ts(R("KD", h), R("D1", h), -2047.5, A.is_gt)
+        ts(R("CD", h), R("D1", h), -2055.0, A.is_lt)
+        for hb in (0, 1):
+            for q in (0, 1):
+                b = "pg%d" % q
+                mm(sum([chain(R(b, i), (R("Ib"), R("Y", h, S_(1024 * hb + 8 * q + i, 1024 * hb + 1024, 16))), (R("Ibn"), R("zl", k, blk(hb, 64))))
+                        for i in range(8)], []))
+                act(R("GA", h, blk(q, 8), blk(hb, 64)), R(b), F.Abs)
+        d = R(BK["dist"], S_(256, 384))
+        mm([(R(BK["dist"], S_(256 + j, 384, 16)), R("GA", h, j), R("BOb", S_(0, 128, 16)), True, True) for j in range(16)])
+        ts(R("dst", h), d, -2040.0, A.add)
+        mm(chain(d, (R("dst", h), R("I16")), (R("I16"), R("c2040"))))
+        act(R("rl", h), d, F.Relu, bias=R("nlim", S_(t, t + 1)))
+
+    def stageB(t, h):
+        k = 2 * t + h
+        Z, Tn = R("zl", k), R("Tq", h, S_(0, 128))
+        kk, rs = R(BK["key"], S_(0, 128)), R("rs")
+        mm([(kk, Z, R("k8big"), True, False), (kk, R("o128b"), R("rowc"), False, False), (kk, R("o128h"), R("c16320n"), False, False)] +
+           [(R(BK["key"], S_(j, 128, 16)), R("Y", h, S_(j, 2048, 16)), R("k8big", S_(0, 128, 16)), False, False) for j in range(16)] +
+           [(kk, R("I8n"), R("dst", h), False, True)])
+        scan(R("sk", h), rs, kk)
+        cp(R("sk", h, S_(0, 128, 16)), R("sk", h, S_(15, 128, 16)))
+        scan(R("sk2", h), rs, R("sk", h))
+        tt(R("oh", h), R("sk2", h), kk, A.is_equal)
+        o1, o2 = R(BK["oh"], S_(0, 128)), R(BK["oh"], S_(128, 256))
+        mm(chain(o1, (R("oh", h), R("I16"))) + chain(o2, (R("oh", h), R("Im16")), (R("I16"), R("c2048"))))
+        tt(R("KT", h), Tn, o1, A.mult)
+        act(R("OHn", h), o1, F.Copy)
+        tt(R("FC", h), R("rl", h), R("CT", h), A.min)
+        tt(R("T1", h), R("T1a", h), o2, A.min)
+        b = BK["lm"]
+        c = [R(b, blk(i)) for i in range(4)]
+        KD, FC, OHn, KT, BO = R("KD", h), R("FC", h), R("OHn", h), R("KT", h), R("BO16")
+        mm(chain(c[2], (R("o128h"), R("cm2047")), (Z, R("BOb"))) + chain(c[1], (KT, BO)) +
+           chain(c[0], (KD, BO), (FC, R("BO128")), (OHn, R("BO64b"))) + chain(c[3], (BO, KD), (R("BOm128"), FC), (R("BO64b"), OHn)))
+        tt(R("LMs", h), R("dM"), R(b, S_(0, 384)), A.mult)
+        tt(R("ac", h), R("CD", h), c[3], A.min)
+        act(R("SG", h), c[3], F.Sign, bias=R("cst", S_(0, 1)), scale=-1.0)
+        act(R("SA", h), c[3], F.Sign, bias=R("cst", S_(1, 2)))
+        b = BK["ll"]
+        mm([(R(b, blk(i, 8)), R("LMs", h, blk(i)), R("BO16", S_(0, 128, 16)), True, True) for i in range(3)])
+        X, E = R(b, S_(0, 8)), R(b, S_(8, 16))
+        ts(R("nu", h), R(b, S_(8, 24)), 2047.0, A.add)
+        ts(R("a1", h), X, 64.5, A.is_gt)
+        ts(R("nv", h), R("nu", h), 1023, A.bitwise_and)
+        ts(R("nlu", h), E, 2063.0, A.add)
+        v, u = R("nv", h, S_(0, 8)), R("nv", h, S_(8, 16))
+        tt(R("dvu", h), v, u, A.subtract)
+        ts(R("pr", blk(h, 8)), X, 64.0, A.is_equal)
+        tt(R("ms", h), R("dvu", h), R("a1", h), A.mult)
+        tt(R("wf", h), R("ms", h), u, A.add)
+        cp(R("wu", h), R("wf", h))
+        gat("V", R("sw", h), R("stw"), R("wu", h))
+        gat("V", R("cw", h), R("scw", S_(0, 1024)), R("wu", h))
+        gat("S", R("ysb", h), WIN, R("nlu", h))
+        act(R("acr", h), R("ac", h), F.Relu, acc=R("asum", S_(k, k + 1)))
+        if t + 1 < NV and h == 1:
+            a = R(BK["tot"], S_(0, 1))
+            mm(chain(a, *[(R("bo32"), R("asum", S_(i, i + 1))) for i in range(2 * t + 2)]))
+            cp(R("ai"), a)
+            ts(R("a31"), R("ai"), 31, A.bitwise_and)
+            ts(R("nlim", S_(t + 1, t + 2)), R("a31"), -8.0, A.mult, R("thn"), A.add)
+        ts(R("KTf", h), R("T1", h), -2047.5, A.is_gt)
+        ts(R("T1s", blk(h)), R("T1", h), 2047.0, A.add, -1.0, A.max)
+        for hb in (0, 1):
+            gat("S", R("XG", h, blk(hb, 1024)), WIN, R("D1u", h, blk(hb, 64)))
+
+    def out(name, buf, c, lat=2500):
+        add("Y", 60, lambda g, T: g.sync.dma_start(T[name][:, c], get(T, R(buf, c))), [R(buf, c)], [], tok="so", lat=lat)
+
+    def stageC(t, h):
+        k, last = 2 * t + h, t == NV - 1
+        SG, Ib = R("SG", h), R("Ib")
+        p0, p1 = R(BK["h"], S_(0, 128)), R(BK["h"], S_(128, 256))
+        for x, held, cw, eq, c1, m, keep, one, snd, land, low in (("t", "Tq", "sw", "eqC", "C1t", "Tm", "KTf", "T1", "stt", "tt", -2050.0),
+                                                                  ("d", "Dq", "cw", "eqB", "C1", "Dm", "KD", "D1", "sd", "dt", -2048.0)):
+            member(cw, held, eq, h)
+            cnt = counts(eq, "cm" + eq[2], h, BK["cc"])
+            mm(chain(p1, (R("I16"), R(one, h)), (R("Ib4096n"), SG), (Ib, R("cm4096"))) +
+               chain(p0, (Ib, R("c67584")), (R("Ib65536"), SG), (R("Im16"), R(keep, h)), cnt))
+            tt(R(c1, h), R(cw, h), p0, A.min)
+            tt(R(m, h), R(c1, h), p1, A.max)
+            if last:
+                ts(R("o" + x, blk(h)), R(m, h), 2047.0, A.add, -1.0, A.max)
+                out("y" + x, "o" + x, blk(h))
+            else:
+                ts(R(snd, k), R(m, h), low, A.max, 2063.0, A.add)
+                send(t, h, x, snd, land)
+        scan(R("xs", h), R("rst"), R("XG", h))
+        c = [R(BK["z"], blk(i)) for i in range(4)]
+        ys = R("ysb", h)
+        mm(chain(c[0], (R("Ibh"), ys), (R("Ibh"), R("xs", h, S_(15, 2048, 16))), (R("Ib512n"), SG)) +
+           chain(c[1], (Ib, R("zl", k)), (R("Ib256"), SG)) + chain(c[2], (Ib, ys), (R("Ib256n"), R("SA", h))))
+        ts(R("hf", h), c[0], 511.75, A.add, 1024.0, A.max)
+        act(R("zg", h), c[1], F.Relu, bias=R("cst", S_(2, 3)))
+        act(R("yg", h), c[2], F.Relu, bias=R("cst", S_(2, 3)))
+        mm(chain(c[3], (R("I16"), R("hf", h)), (Ib, R("zg", h)), (R("Ibn"), R("yg", h))))
+        act(R("oz", blk(h)) if last else R("sz", k), c[3], F.Abs, bias=R("cst", S_(3, 4)))
+        if last:
+            out("yz", "oz", blk(h))
+        else:
+            send(t, h, "z", "sz", "zl")
+
+    def stageD(t):
+        b, b2 = BK["d"], BK["d2"]
+        for h in (0, 1):
+            tt(R("dvq", blk(h, 8)), R("nv", h, S_(0, 8)), R("q0", blk(h, 8)), A.subtract)
+        tt(R("mvq"), R("dvq"), R("pr"), A.mult)
+        tt(R("PV16"), R("mvq"), R("q0"), A.add)
+        tt(R("PV"), R("mvq"), R("q0"), A.add)
+        mm([(R(b2, S_(r, 256, 16)), R("I16"), R("PV16"), True, True) for r in range(16)])
+        act(R("PVs"), R(b2, S_(0, 256)), F.Copy)
+        mm([(R(b, S_(0, 256)), R("I16"), R("tri"), True, False)] +
+           [(R(b, S_(r, 256, 16)), R("bc", blk(r)), R("PV16"), False, r == 15) for r in range(16)])
+        tt(R("eqP"), R("PVs"), R(b, S_(0, 256)), A.is_equal)
+        mm(chain(R(b, S_(0, 16)), *[(R("selm", blk(r)), R("eqP", S_(r, 256, 16))) for r in range(16)]))
+        tt(R("dq2"), R("q0"), R("PV"), A.subtract)
+        ts(R("lm"), R(b, S_(0, 16)), -1.0, A.is_lt)
+        tt(R("lq"), R("lm"), R("dq2"), A.mult)
+        tt(R("PLf"), R("lq"), R("PV"), A.add)
+        cp(R("PLu", S_(0, 32, 2)), R("PLf"))
+        for c in range(16):
+            o, off, src = R("scw"), R("PLu", S_(2 * c, 2 * c + 1)), R("T1s", blk(c, 16))
+            add("V", 100, lambda g, T, o=o, off=off, src=src: g.vector.tensor_copy(get(T, o).indirect(get(T, off)), get(T, src)), [off, src], [o])
+        if t == NV - 1:
+            out("ys", "scw", S_(0, 1024), 4500)
+
+    for t in range(NV):
+        for s, f, h in (("A0", stageA, 0), ("B0", stageB, 0), ("A1", stageA, 1), ("B1", stageB, 1), ("C0", stageC, 0), ("C1", stageC, 1)):
+            lab[0] = s
+            f(t, h)
+        lab[0] = "D"
+        stageD(t)
+    return ops
+
+
+def depend(ops):
+    hist = {}
+    for i, o in enumerate(ops):
+        pw, acc = set(), {}
+        for x, wr in [(x, False) for x in o["r"]] + [(x, True) for x in o["w"]]:
+            sp = () if psum(x) else tuple(s[:2] for s in span(x))
+            acc[(x[0], sp)] = acc.get((x[0], sp), False) or wr
+        for (name, sp), wr in acc.items():
+            for j, sj, wj in hist.get(name, ()):
+                if j != i and all(a[0] < b[1] and b[0] < a[1] for a, b in zip(sp, sj)):
+                    if wj or wr or ops[j]["e"] != o["e"] and SCRATCH[name][0] == "psum":
+                        pw.add(j)
+        for (name, sp), wr in acc.items():
+            h = hist.setdefault(name, [])
+            if wr:
+                h[:] = [y for y in h if y[0] == i or not all(a[0] <= b[0] and b[1] <= a[1] for a, b in zip(sp, y[1]))]
+            h.append((i, sp, wr))
+        o["pw"] = pw
+
+
+def schedule(ops):
+    n = len(ops)
+    succ, cnt = [[] for _ in range(n)], [0] * n
+    for i, o in enumerate(ops):
+        ps = [(j, WAKE if ops[j]["e"] != o["e"] else SELF) for j in o["pw"]]
+        if "after" in o:
+            ps.append((o["after"], REMOTE))
+        cnt[i] = len(ps)
+        for j, l in ps:
+            succ[j].append((i, l))
+    fin = [o["d"] + o.get("lat", 0.0) for o in ops]
+    pri = [0.0] * n
+    for i in range(n - 1, -1, -1):
+        pri[i] = BIAS.get(ops[i]["g"], 0.0) + fin[i] + max([0.0] + [l + pri[k] for k, l in succ[i]])
+    rdy, free, order = [0.0] * n, {}, []
+    ready = [i for i in range(n) if cnt[i] == 0]
+    while ready:
+        st = {i: max(rdy[i], free.get(ops[i]["e"], 0.0)) for i in ready}
+        tmin = min(st.values()) + LOOK
+        i = max((j for j in ready if st[j] <= tmin), key=lambda j: pri[j])
+        ready.remove(i)
+        o, s = ops[i], st[i]
+        o["s"] = s
+        if o["e"] != "R":
+            free[o["e"]] = s + o["d"]
+        order.append(i)
+        for k, l in succ[i]:
+            cnt[k] -= 1
+            rdy[k] = max(rdy[k], s + fin[i] + l)
+            if cnt[k] == 0:
+                ready.append(k)
+    return order
+
+
+CACHE = {}
+
+
+def rank_program(g, core, T, topo):
+    rank = T.rank_of(core)
+    if rank is None:
+        return
+    dst = T.cores[(rank + 1) % len(T.cores)]
+    rid, pid = topo.addr(dst)[:2]
+    mask, nrem = topo.mask(core, dst), len(topo.engines(core, dst))
+    if nrem not in CACHE:
+        ops = program(nrem)
+        depend(ops)
+        CACHE[nrem] = (ops, schedule(ops))
+    ops, order = CACHE[nrem]
+    queue = {"V": g.vector, "S": g.scalar, "P": g.tensor, "G": g, "Y": g.sync}
+    sem = {"V": "sv", "S": "ss", "P": "sp", "G": "sg"}
+    known, vc, tok, total = {e: {} for e in queue}, {}, {}, {"ls": 0}
+    for i in order:
+        o = ops[i]
+        e = o["e"]
+        if e == "R":
+            tok[i], vc[i] = (o["tok"], o["inc"]), {}
+            total[o["tok"]] = o["inc"]
+            continue
+        kn, need = known[e], {}
+        for j in o["pw"]:
+            need[tok[j][0]] = max(need.get(tok[j][0], 0), tok[j][1])
+        for j in sorted(o["pw"], reverse=True):
+            s = tok[j][0]
+            if kn.get(s, 0) < need[s]:
+                queue[e].wait_ge(T.sem[s], need[s])
+                kn[s] = need[s]
+            for a in vc[j]:
+                kn[a] = max(kn.get(a, 0), vc[j][a])
+        x = o["fn"](g, T)
+        if o.get("n") == "send":
+            g.remote_dma(out_ap=x[0], in_ap=x[1], remote_sem=T.sem[x[2]], local_sem=T.sem["ls"], pid=pid, routing_id=rid, dma_engine_mask=mask)
+            total["ls"] += nrem
+            continue
+        s, n = (o["tok"], 16) if "tok" in o else (sem[e], 1)
+        total[s] = total.get(s, 0) + n
+        x.then_inc(T.sem[s], n)
+        tok[i], vc[i] = (s, total[s]), dict(kn)
+    for s in total:
+        if total[s]:
+            g.wait_ge(T.sem[s], total[s])

@@ -1,3 +1,4 @@
+import math
 from concourse.mybir import AluOpType, ActivationFunctionType
 
 A, F = AluOpType, ActivationFunctionType
@@ -13,35 +14,33 @@ def _decl(text, d, lead):
 
 
 _decl("tli:256 dli:256 thi:1 sci:1024 sti:1024 pidx:1 pmi:1 ai:1 a31:1", i32, [])
-_decl("tm0:256 ts0:256 stm:1024 sta:1024 stw:1024 scw:1280 pmf:1 iq:384 P1:16 on32:128 boa:128 bo32:128 id32:128 "
-      "q0i:16 q0:16 thn:1 nlim:8 asum:16 T1s:256 pr:16 dvq:16 mvq:16 PV:16 PVs:256 lm:16 dq2:16 lq:16 PLf:16 od:256 ot:256 oz:256 cst:5", f32, [])
-_decl("selm:2048 bc:2048 dM:384 tri:256 PV16:16 eqP:256", f16, [])
-_decl("clkw:4112 rst:2048 rs:128 rowc:128 k8big:128", b16, [])
+_decl("tm0:256 ts0:256 stw:1024 scw:1040 pmf:1 iq:256 P1:16 on32:128 boa:128 bo32:128 id32:128 "
+      "q0:1 thn:1 nlim:8 asum:16 T1s:256 od:256 ot:256 oz:256 cst:10", f32, [])
+_decl("PV:16 c385:128", f16, [])
+_decl("clkw:4112 bc:2048 rst:1024 rowc:256 Zs:144 KB:16 BOpm:16 tri:256 eqP:256", b16, [])
 _decl("PLu:32", u16, [])
-_decl("eqA:2048 eqB:2048 eqC:2048 Dq:512 Tq:512 D1:128 KD:128 CD:128 T1a:128 CT:128 FC:128 oh:128 KT:128 T1:128 KTf:128 LMs:384 "
-      "cw:128 sw:128 hf:128 dst:128", f16, [2])
-_decl("Y:2048 GA:16,128 XG:2048 xs:2048 rl:128 OHn:128 SG:128 SA:128 ac:128 acr:128 cmA:128 cmB:128 cmC:128 ysb:128 zg:128 yg:128 "
-      "sdB:512 sdC:512 seB:512 seC:512", b16, [2])
-_decl("sk:128 sk2:128 a1:8 dvu:8 ms:8 wf:8 C1:128 C1t:128 Dm:128 Tm:128", f32, [2])
+_decl("Tq:128 D1:128 Q:256 cw:128 sw:128 hf:128 dst:128 Tm:128", f16, [2])
+_decl("eqA:2048 eqB:2048 fC:2048 Y:2048 MN:2048 XG:2048 xs:2048 nk:128 oh:128 cmA:128 cmB:128 rC:256 cdS:128 FC:128 SG:128 SA:128 "
+      "KTn:128 ysb:128 zy:256 acr:128", b16, [2])
+_decl("sk:128 sk2:128 AS:16 sel:16 npr:8 C1:128 C1t:128", f32, [2])
 _decl("nu:16 nv:16", i32, [2])
 _decl("D1u:128 nlu:8 wu:8", u16, [2])
-_decl("dt:128 tt:128 sd:128 stt:128", u16, [2 * NV])
+_decl("tt:128 stt:128", u16, [2 * NV])
+_decl("Dq:512 sd:128", f16, [2 * NV])
 _decl("zl:128 sz:128", b16, [2 * NV])
-for _b, _l, _d in (("kh", "I16 In16 Im16 BOm16 BO16 BO128 BOm128 c2048 c2040 c16320n I8n o128h cm2047", f16),
-                   ("kb", "Ib Ibn Ibh Ib512n Ib256 Ib256n Ib4096n Ib65536 I4128n BO64b BOb c67584 cm4096 o128b", b16)):
-    _l = _l.split()
-    SCRATCH[_b] = ("sbuf", [128, len(_l), 128], _d)
-    for _i, _n in enumerate(_l):
-        ALIAS[_n] = (_b, _i)
-for _n in ("pc", "po", "pk", "r0", "r1", "r2"):
-    SCRATCH[_n] = ("psum", [128, 512], f32)
-SCRATCH["pg0"] = SCRATCH["pg1"] = ("psum", [128, 8, 64], f32)
-BK = dict(cnt="po", dist="pk", ca="po", key="r2", oh="r2", lm="pc", ll="r2", tot="pc", h="r2", cc="r2", z="pc", d="po", d2="pk")
+_l = "I In I4160n I17 I16 Ih I64 I4096 BO BO128n c2048 one".split()
+SCRATCH["kb"] = ("sbuf", [128, len(_l), 128], b16)
+for _i, _n in enumerate(_l):
+    ALIAS[_n] = ("kb", _i)
+for _i in range(8):
+    SCRATCH["ps%d" % _i] = ("psum", [128, 512], f32)
+BANKS = {"v": (0, 1), "s": (2, 3), "z": (4,), "m": (5, 6, 7)}
 LOADS = ("tl", "dl", "za", "zb", "th", "clk", "st", "sc")
 SEMAPHORES = ["sv", "ss", "sp", "sg", "so", "ls"] + ["l_" + n for n in LOADS]
 SEMAPHORES += ["a%d%d%s" % (t, h, k) for t in range(1, NV) for h in (0, 1) for k in "dtz"]
-CYC, OVV, OVS, WAKE, SELF, REMOTE, LOOK = 1.0, 10.0, 20.0, 70.0, 100.0, 4000.0, 20.0
-BIAS = {"D": -5.0, "B0": 20.0, "B1": 60.0, "A1": -5.0, "C1": -5.0}
+CYC, PEC, OVV, OVS, WAKE, SELF, REMOTE, LOOK = 0.83, 0.43, 30.0, 40.0, 90.0, 90.0, 3500.0, 20.0
+BIAS, LEAD = {}, {"A0": 4000.0, "B0": 4000.0, "C0": 4000.0}
+TEMP, PLACE = {}, {}
 
 
 def R(name, *ix):
@@ -56,31 +55,43 @@ def blk(i, n=128):
     return slice(n * i, n * i + n)
 
 
+def psum(x):
+    return x[0] in TEMP
+
+
 def get(T, x):
+    if psum(x):
+        bank, b0 = PLACE[x[0]]
+        a, b, st = (x[1][0] if x[1] else slice(None)).indices(128 * TEMP[x[0]][1])
+        return T["ps%d" % bank][:, 128 * b0 + a:128 * b0 + b:st]
     return T[x[0]][(slice(None),) + x[1] + (slice(None),) * (len(SCRATCH[x[0]][1]) - 1 - len(x[1]))]
 
 
 def span(x):
     out = []
-    for d, n in enumerate(SCRATCH[x[0]][1][1:]):
+    for d, n in enumerate([128 * TEMP[x[0]][1]] if psum(x) else SCRATCH[x[0]][1][1:]):
         i = x[1][d] if d < len(x[1]) else slice(None)
         if isinstance(i, int):
-            out.append((i, i + 1, 1))
+            out.append((i, i + 1, 1, 1))
         else:
-            a, b, st = i.indices(n)
-            out.append((a, b, len(range(a, b, st))))
+            r = range(*i.indices(n))
+            out.append((min(r[0], r[-1]), max(r[0], r[-1]) + 1, abs(r.step), len(r)))
     return out
 
 
 def size(x):
     n = 1
     for s in span(x):
-        n *= s[2]
+        n *= s[3]
     return n
 
 
-def psum(x):
-    return SCRATCH[x[0]][0] == "psum"
+def meet(p, q):
+    return all(a[0] < b[1] and b[0] < a[1] and (a[0] - b[0]) % math.gcd(a[2], b[2]) == 0 for a, b in zip(p, q))
+
+
+def cover(p, q):
+    return all(a[0] <= b[0] and b[1] <= a[1] and b[2] % a[2] == 0 and (a[0] - b[0]) % a[2] == 0 for a, b in zip(p, q))
 
 
 def two(*xs):
@@ -88,7 +99,12 @@ def two(*xs):
 
 
 def program(nrem):
-    ops, rc, lab = [], [0], [""]
+    ops, lab = [], [""]
+
+    def tmp(role, n):
+        name = "~%d" % len(TEMP)
+        TEMP[name] = (role, n)
+        return name
 
     def add(e, dur, fn, r, w, **kw):
         ops.append(dict(kw, g=lab[0], e=e, d=dur, fn=fn, r=[x for x in r if isinstance(x, tuple)], w=w))
@@ -108,14 +124,14 @@ def program(nrem):
             lambda g, T: g.vector.tensor_tensor(get(T, o), get(T, a), get(T, b), op), [a, b], [o])
 
     def cp(o, i):
-        add("V", OVV + max(64, size(o)) * CYC, lambda g, T: g.vector.tensor_copy(get(T, o), get(T, i)), [i], [o])
+        add("V", OVV + max(64, size(o) * (0.5 if two(o, i) else 1)) * CYC, lambda g, T: g.vector.tensor_copy(get(T, o), get(T, i)), [i], [o])
 
     def fill(o, v):
-        add("V", OVV + max(64, size(o)) * CYC, lambda g, T: g.vector.memset(get(T, o), v), [], [o])
+        add("V", OVV + max(64, size(o) * (0.5 if two(o) else 1)) * CYC, lambda g, T: g.vector.memset(get(T, o), v), [], [o])
 
-    def scan(o, a, b):
-        add("V", OVV + size(o) * (0.5 if two(o, a, b) else 1) * CYC,
-            lambda g, T: g.vector.tensor_tensor_scan(get(T, o), get(T, a), get(T, b), 0.0, A.mult, A.max), [a, b], [o])
+    def scan(o, a, b, op0=A.mult):
+        add("V", OVV + max(64, size(o) * (0.5 if two(o, a, b) else 1)) * CYC,
+            lambda g, T: g.vector.tensor_tensor_scan(get(T, o), get(T, a), get(T, b), 0.0, op0, A.max), [a, b], [o])
 
     def act(o, i, func, bias=0.0, scale=1.0, acc=None):
         def fn(g, T):
@@ -123,13 +139,13 @@ def program(nrem):
             return g.scalar.activation(get(T, o), get(T, i), func, bias=val(T, bias), scale=scale, **kw)
         add("S", OVS + max(64, size(o)) * CYC, fn, [i, bias], [o] + ([] if acc is None else [acc]))
 
-    def gat(e, o, win, off):
+    def gat(e, o, win, off, shift=None):
         def fn(g, T):
             x = get(T, win).indirect(get(T, off))
             if e == "S":
                 return g.scalar.activation(get(T, o), x, F.Copy)
-            return g.vector.tensor_copy(get(T, o), x) if win[0] == "stw" else g.vector.tensor_scalar(get(T, o), x, -2047.0, None, A.add)
-        add(e, 75 + 1.5 * size(o) * CYC, fn, [win, off], [o])
+            return g.vector.tensor_copy(get(T, o), x) if shift is None else g.vector.tensor_scalar(get(T, o), x, shift, None, A.add)
+        add(e, 60 + 1.56 * size(o) * CYC, fn, [win, off], [o])
 
     def mm(lst):
         def fn(g, T):
@@ -137,7 +153,7 @@ def program(nrem):
             for o, l, r, a, b in lst:
                 x = g.tensor.matmul(get(T, o), get(T, l), get(T, r), a, b)
             return x
-        d = sum(6 + max(64, size(m[0])) * 0.5 * (4 if SCRATCH[m[1][0]][2] == f32 else 1) for m in lst)
+        d = sum(4 + max(64, size(m[0])) * PEC * (4 if SCRATCH[m[1][0]][2] == f32 else 1) for m in lst)
         add("P", 30 + d, fn, [m[1] for m in lst] + [m[2] for m in lst], [m[0] for m in lst])
 
     def chain(o, *pairs):
@@ -156,236 +172,234 @@ def program(nrem):
 
     def iota(o, pat, base, cm=0):
         kw = {} if SCRATCH[o[0]][2] == i32 else {"allow_small_or_imprecise_dtypes": True}
-        add("G", 130 + 2 * size(o), lambda g, T: g.iota(get(T, o), pat, base, cm, **kw), [], [o])
+        add("G", 130 + 2 * CYC * size(o), lambda g, T: g.iota(get(T, o), pat, base, cm, **kw), [], [o])
 
     def aff(o, i, pat, op, base, cm, other=0.0):
-        add("G", 170 + 2 * size(o), lambda g, T: g.affine_select(get(T, o), get(T, i), pat, op, other, base, cm), [i], [o])
+        add("G", 170 + 2 * CYC * size(o), lambda g, T: g.affine_select(get(T, o), get(T, i), pat, op, other, base, cm), [i], [o])
+
+    def spread(k):
+        for n in (128, 256):
+            aff(R("Dq", k, S_(n, 2 * n)), R("Dq", k, S_(0, n)), [[0, n]], A.is_ge, 0, 0)
     fill(R("on32"), 1.0)
     iota(R("pidx"), [[0, 1]], 0, 1)
     aff(R("boa"), R("on32"), [[-16, 8], [0, 16]], A.is_ge, 0, 1)
     aff(R("bo32"), R("boa"), [[16, 8], [0, 16]], A.is_ge, 15, -1)
     aff(R("id32"), R("on32"), [[-1, 128]], A.is_equal, 0, 1)
-    iota(R("iq"), [[0, 24], [1, 16]], 0)
-    iota(R("rowc"), [[0, 8], [-1, 16]], 16)
-    iota(R("q0i"), [[16, 16]], 1024)
+    iota(R("iq"), [[0, 16], [1, 16]], 0)
+    fill(R("rowc", blk(1)), 0.0)
+    iota(R("rowc", blk(0)), [[0, 8], [-1, 16]], 16)
     ts(R("pmi"), R("pidx"), 15, A.bitwise_and)
     cp(R("pmf"), R("pmi"))
     pm = R("pmf", S_(0, 1))
     ts(R("P1"), R("iq", S_(0, 16)), pm, A.is_equal)
+    act(R("BO"), R("bo32"), F.Copy)
+    act(R("I"), R("id32"), F.Copy)
     for j in range(16):
-        ts(R("bc", blk(j)), R("bo32"), R("P1", S_(j, j + 1)), A.mult)
+        ts(R("bc", blk(j)), R("BO"), R("P1", S_(j, j + 1)), A.mult)
     fill(R("clkw", S_(0, 16)), -1.0)
-    for n, src, k in (("I16", "id32", 1), ("In16", "id32", -1), ("Im16", "id32", -4112), ("BO16", "bo32", 1), ("BOm16", "bo32", -4112),
-                      ("BOm128", "bo32", -128), ("BO128", "bo32", 128),
-                      ("Ib", "id32", 1), ("Ibn", "id32", -1), ("I4128n", "id32", -4128), ("BOb", "bo32", 1), ("BO64b", "bo32", 64),
-                      ("Ibh", "id32", 0.5), ("Ib512n", "id32", -512), ("Ib256", "id32", 256), ("I8n", "id32", -8), ("k8big", "bo32", 8),
-                      ("Ib256n", "id32", -256), ("Ib4096n", "id32", -4096), ("Ib65536", "id32", 65536)):
-        if ALIAS.get(n, ("kb",))[0] == "kb":
-            act(R(n), R(src), F.Copy, scale=float(k))
-        else:
-            ts(R(n), R(src), float(k), A.mult)
-    for j in range(16):
-        aff(R("selm", blk(j)), R("BOm16"), [[0, 8], [1, 16]], A.is_equal, -j, 0)
-    iota(R("rst"), [[0, 128], [1, 16]], 0)
-    aff(R("rst"), R("rst"), [[0, 128], [1, 16]], A.is_equal, 0, 0, 1.0)
-    for n, x in (("c2048", 2048.0), ("o128b", 1.0 / 128), ("o128h", 1.0 / 128), ("cm2047", -2047.0), ("c2040", 2040.0), ("c16320n", -16320.0),
-                 ("c67584", 67584.0), ("cm4096", -4096.0), ("rs", 1.0)):
+    for n, src, k in (("In", "id32", -1), ("I4160n", "id32", -4160), ("I17", "id32", 131072), ("I16", "id32", 65536), ("Ih", "id32", 0.5),
+                      ("I64", "id32", 64), ("I4096", "id32", 4096), ("BO128n", "bo32", -128)):
+        act(R(n), R(src), F.Copy, scale=float(k))
+    BO8 = R("BO", S_(0, 128, 16))
+    for n, k0, k1 in (("KB", 16.0, -2.0), ("BOpm", 1.0, -1.0)):
+        ts(R(n, S_(0, 8)), BO8, k0, A.mult)
+        ts(R(n, S_(8, 16)), BO8, k1, A.mult)
+    fill(R("Zs"), 0.0)
+    cp(R("Zs", S_(15, 143, 16)), BO8)
+    iota(R("rst"), [[0, 64], [1, 16]], 0)
+    aff(R("rst"), R("rst"), [[0, 64], [1, 16]], A.is_equal, 0, 0, 1.0)
+    for n, x in (("c2048", 2048.0), ("one", 1.0), ("c385", 385.0), ("AS", -1.0e6)):
         fill(R(n), x)
-    fill(R("rs", S_(0, 128, 16)), 0.0)
-    for i, x in enumerate((64.5, 0.5, -256.0, -1024.0, 1.0)):
+    CST = (2048.0, 1064.5, 999.5, -2048.0, -131072.0, -1024.0, -2047.5, 0.0156263)
+    for i, x in enumerate(CST):
         fill(R("cst", S_(i, i + 1)), x)
-    ts(R("dM"), R("iq"), pm, A.is_equal)
-    ts(R("tri"), R("iq", S_(0, 256)), pm, A.is_ge, 5000.0, A.mult)
-    ts(R("q0"), R("q0i"), pm, A.add)
+
+    def cst(x):
+        return R("cst", S_(CST.index(x), CST.index(x) + 1))
+    ts(R("tri"), R("iq"), pm, A.is_le, 4096.0, A.mult)
+    ts(R("q0"), pm, 1024.0, A.add)
     ts(R("tm0"), R("tli"), 0.0, A.min, 2.0, A.mult)
     tt(R("ts0"), R("tli"), R("tm0"), A.add)
     for h in (0, 1):
         ts(R("tt", h), R("ts0", blk(h)), 16.0, A.add)
-        ts(R("dt", h), R("dli", blk(h)), 16.0, A.add)
-    ts(R("thn"), R("thi"), -1.0, A.mult)
+        ts(R("Dq", h, S_(0, 128)), R("dli", blk(h)), -2047.0, A.add)
+    ts(R("thn"), R("thi"), -1.0, A.mult, -2120.5, A.add)
     cp(R("nlim", S_(0, 1)), R("thn"))
     for k in range(2):
-        c = blk(k, 512)
-        ts(R("stm", c), R("sti", c), 0.0, A.min, 2.0, A.mult)
-        tt(R("sta", c), R("sti", c), R("stm", c), A.add)
-        act(R("stw", c), R("sta", c), F.Copy, bias=-2047.0)
+        c, b = blk(k, 512), tmp("s", 4)
+        ts(R(b), R("sti", c), 0.0, A.min, 2.0, A.mult)
+        tt(R("stw", c), R("sti", c), R(b), A.add)
     cp(R("scw", S_(0, 1024)), R("sci"))
 
     WIN = R("clkw")
-    sent = {}
+    I, In, I17, I4160n, BO = R("I"), R("In"), R("I17"), R("I4160n"), R("BO")
+    sent, lists = {}, {}
 
-    def arrive(t, h, kind, buf):
+    def arrive(t, h, kind, x):
         if t:
-            add("R", 0, None, [], [R(buf, 2 * t + h)], tok="a%d%d%s" % (t, h, kind), inc=nrem, after=sent[(t - 1, h, kind)])
+            add("R", 0, None, [], [x], tok="a%d%d%s" % (t, h, kind), inc=nrem, after=sent[(t - 1, h, kind)])
 
-    def send(t, h, kind, src, buf):
+    def send(t, h, kind, src, land):
         def fn(g, T):
-            return get(T, R(buf, 2 * t + h + 2)), get(T, R(src, 2 * t + h)), "a%d%d%s" % (t + 1, h, kind)
+            return get(T, land), get(T, R(src, 2 * t + h)), "a%d%d%s" % (t + 1, h, kind)
         sent[(t, h, kind)] = add("G", 100, fn, [R(src, 2 * t + h)], [], n="send")
 
     def member(rows, held, eq, h):
         for q in range(4):
-            rc[0] += 1
-            b = "r%d" % (rc[0] % 2)
-            if q == 0 and eq != "eqA":
-                mm(sum([chain(R(b, blk(i)), (R("bc", blk(i)), R(rows, h, S_(0, 128))), (R("In16"), R(held, h, S_(0, 128)))) for i in range(4)], []))
-                act(R("sd" + eq[2], h), R(b, S_(0, 512)), F.Abs)
-                act(R("se" + eq[2], h), R("sd" + eq[2], h), F.Relu, bias=R("cst", S_(4, 5)), scale=-1.0)
-            else:
-                mm([(R(b, blk(i)), R("bc", blk(4 * q + i)), R(rows, h, S_(0, 128)), True, True) for i in range(4)])
-                tt(R(eq, h, blk(q, 512)), R(held, h, S_(0, 512)), R(b, S_(0, 512)), A.is_equal)
+            b = tmp("v", 4)
+            mm([(R(b, blk(i)), R("bc", blk(4 * q + i)), rows, True, True) for i in range(4)])
+            tt(R(eq, h, blk(q, 512)), held, R(b), A.is_equal)
 
-    def counts(eq, cm, h, b):
-        def one(j):
-            return (R("se" + eq[2], h, blk(j)), R("BOb", S_(0, 128, 16))) if j < 4 and eq != "eqA" else (R(eq, h, blk(j)), R("BO16", S_(0, 128, 16)))
-        mm([(R(b, S_(384 + j, 512, 16)),) + one(j) + (True, True) for j in range(16)])
-        act(R(cm, h), R(b, S_(384, 512)), F.Copy)
-        return (R(cm, h), R("I4128n"))
+    def to_list(o, x, n):
+        return [(o, R("Zs", S_(15 - r, 143 - r)), (x[0], x[1] + (S_(r, n, 16),))) for r in range(16)]
 
     def stageA(t, h):
         k = 2 * t + h
-        arrive(t, h, "t", "tt")
-        arrive(t, h, "d", "dt")
-        arrive(t, h, "z", "zl")
+        D, Z, Tn = R("Dq", k, S_(0, 128)), R("zl", k), R("Tq", h)
+        arrive(t, h, "t", R("tt", k))
+        arrive(t, h, "d", D)
+        arrive(t, h, "z", Z)
         for hb in (0, 1):
             gat("S", R("Y", h, blk(hb, 1024)), WIN, R("tt", k, blk(hb, 64)))
-        for dst, src in (("Tq", "tt"), ("Dq", "dt")):
-            for r in range(4):
-                ts(R(dst, h, blk(r)), R(src, k), -2063.0, A.add)
-        D, Tn = R("Dq", h, S_(0, 128)), R("Tq", h, S_(0, 128))
-        member("Tq", "Dq", "eqA", h)
-        pD, pT, c = R(BK["cnt"], S_(0, 128)), R(BK["cnt"], S_(128, 256)), (R("I16"), R("c2048"))
-        mm(chain(pD, c, *[(R("Im16"), R("eqA", h, blk(j))) for j in range(16)]))
-        mm(chain(pT, c, counts("eqA", "cmA", h, BK["ca"])))
-        tt(R("D1", h), D, pD, A.min)
-        tt(R("T1a", h), Tn, pT, A.min)
-        ts(R("D1u", h), R("D1", h), -2048.0, A.max, 2063.0, A.add)
-        ts(R("CT", h), R("T1a", h), -2055.0, A.is_lt)
-        ts(R("KD", h), R("D1", h), -2047.5, A.is_gt)
-        ts(R("CD", h), R("D1", h), -2055.0, A.is_lt)
+        ts(Tn, R("tt", k), -2063.0, A.add)
+        spread(k)
+        b = tmp("z", 4)
+        mm([(R(b, S_(i, 512, 4)), I, Z, True, True) for i in range(4)])
         for hb in (0, 1):
-            for q in (0, 1):
-                b = "pg%d" % q
-                mm(sum([chain(R(b, i), (R("Ib"), R("Y", h, S_(1024 * hb + 8 * q + i, 1024 * hb + 1024, 16))), (R("Ibn"), R("zl", k, blk(hb, 64))))
-                        for i in range(8)], []))
-                act(R("GA", h, blk(q, 8), blk(hb, 64)), R(b), F.Abs)
-        d = R(BK["dist"], S_(256, 384))
-        mm([(R(BK["dist"], S_(256 + j, 384, 16)), R("GA", h, j), R("BOb", S_(0, 128, 16)), True, True) for j in range(16)])
-        ts(R("dst", h), d, -2040.0, A.add)
-        mm(chain(d, (R("dst", h), R("I16")), (R("I16"), R("c2040"))))
-        act(R("rl", h), d, F.Relu, bias=R("nlim", S_(t, t + 1)))
+            for q in range(4):
+                c = S_(1024 * hb + q, 1024 * hb + 1024, 4)
+                tt(R("MN", h, c), R("Y", h, c), R(b, blk(hb, 256)), A.min)
+        lists[h] = L = tmp("m", 1)
+        u = [(x[1], x[2]) for x in to_list(None, R("zl", k), 128)]
+        mm(chain(R(L, S_(17, 32, 2)), (I, R("c2048", S_(0, 8))), (I, R("one", S_(0, 8))), *u))
+        member(Tn, R("Dq", k), "eqA", h)
+        pD = R(tmp("m", 1))
+        mm(chain(pD, (I, R("c2048")), *[(I4160n, R("eqA", h, blk(j))) for j in range(16)]))
+        tt(R("D1", h), D, pD, A.min)
+        act(R("cdS", h), pD, F.Sign, bias=cst(2048.0), scale=-1.0)
+        ts(R("D1u", h), R("D1", h), -2048.0, A.max, 2063.0, A.add)
+        ts(R("nk", h), R("D1", h), -2047.5, A.is_le, 0.5, A.add)
+        b = tmp("m", 1)
+        mm([(R(b, S_(j, 128, 16)), R("eqA", h, blk(j)), BO8, True, True) for j in range(16)])
+        act(R("cmA", h), R(b), F.Sign)
+        for hb in (0, 1):
+            gat("S", R("XG", h, blk(hb, 1024)), WIN, R("D1u", h, blk(hb, 64)))
+            scan(R("xs", h, blk(hb, 1024)), R("rst"), R("XG", h, blk(hb, 1024)))
 
     def stageB(t, h):
         k = 2 * t + h
-        Z, Tn = R("zl", k), R("Tq", h, S_(0, 128))
-        kk, rs = R(BK["key"], S_(0, 128)), R("rs")
-        mm([(kk, Z, R("k8big"), True, False), (kk, R("o128b"), R("rowc"), False, False), (kk, R("o128h"), R("c16320n"), False, False)] +
-           [(R(BK["key"], S_(j, 128, 16)), R("Y", h, S_(j, 2048, 16)), R("k8big", S_(0, 128, 16)), False, False) for j in range(16)] +
-           [(kk, R("I8n"), R("dst", h), False, True)])
+        Z, Tn, rs, oh = R("zl", k), R("Tq", h), R("rst", S_(0, 128)), R("oh", h)
+        b = tmp("m", 2)
+        kk, d = R(b, blk(0)), R(b, blk(1))
+        mm([(R(b), I, R("rowc"), True, False), (d, Z, BO, False, False)] +
+           [(R(b, S_(128 + j, 256, 16)), R("Y", h, S_(j, 2048, 16)), BO8, False, False) for j in range(16)] +
+           [(R(b, S_(j, 256, 16)), R("MN", h, S_(j, 2048, 16)), R("KB"), False, j == 15) for j in range(16)])
         scan(R("sk", h), rs, kk)
-        cp(R("sk", h, S_(0, 128, 16)), R("sk", h, S_(15, 128, 16)))
-        scan(R("sk2", h), rs, R("sk", h))
-        tt(R("oh", h), R("sk2", h), kk, A.is_equal)
-        o1, o2 = R(BK["oh"], S_(0, 128)), R(BK["oh"], S_(128, 256))
-        mm(chain(o1, (R("oh", h), R("I16"))) + chain(o2, (R("oh", h), R("Im16")), (R("I16"), R("c2048"))))
-        tt(R("KT", h), Tn, o1, A.mult)
-        act(R("OHn", h), o1, F.Copy)
-        tt(R("FC", h), R("rl", h), R("CT", h), A.min)
-        tt(R("T1", h), R("T1a", h), o2, A.min)
-        b = BK["lm"]
-        c = [R(b, blk(i)) for i in range(4)]
-        KD, FC, OHn, KT, BO = R("KD", h), R("FC", h), R("OHn", h), R("KT", h), R("BO16")
-        mm(chain(c[2], (R("o128h"), R("cm2047")), (Z, R("BOb"))) + chain(c[1], (KT, BO)) +
-           chain(c[0], (KD, BO), (FC, R("BO128")), (OHn, R("BO64b"))) + chain(c[3], (BO, KD), (R("BOm128"), FC), (R("BO64b"), OHn)))
-        tt(R("LMs", h), R("dM"), R(b, S_(0, 384)), A.mult)
-        tt(R("ac", h), R("CD", h), c[3], A.min)
-        act(R("SG", h), c[3], F.Sign, bias=R("cst", S_(0, 1)), scale=-1.0)
-        act(R("SA", h), c[3], F.Sign, bias=R("cst", S_(1, 2)))
-        b = BK["ll"]
-        mm([(R(b, blk(i, 8)), R("LMs", h, blk(i)), R("BO16", S_(0, 128, 16)), True, True) for i in range(3)])
-        X, E = R(b, S_(0, 8)), R(b, S_(8, 16))
-        ts(R("nu", h), R(b, S_(8, 24)), 2047.0, A.add)
-        ts(R("a1", h), X, 64.5, A.is_gt)
+        scan(R("sk2", h, S_(None, None, -1)), rs, R("sk", h, S_(None, None, -1)))
+        tt(oh, R("sk2", h), kk, A.is_equal)
+        ts(R("dst", h), d, -2040.0, A.add)
+        d = R(tmp("m", 1))
+        mm(chain(d, (R("dst", h), In), (R("cmA", h), I4160n)))
+        act(R("FC", h), d, F.Sign, bias=R("nlim", S_(t, t + 1)), scale=-1.0)
+        FC, XS, KT = R("FC", h), R("Q", h, blk(0)), R("Q", h, blk(1))
+        o1, x, p = R(tmp("m", 1)), R(tmp("m", 1)), R(tmp("m", 1))
+        mm(chain(o1, (oh, I)))
+        tt(KT, Tn, o1, A.mult)
+        mm(chain(x, (In, R("nk", h)), (R("I64"), FC), (oh, R("I64"))))
+        cp(XS, x)
+        L = lists[h]
+        mm(chain(R(L, S_(0, 32, 2)), *[(y[1], y[2]) for y in to_list(None, R("Q", h), 256)]))
+        X = R(L, S_(0, 16, 2))
+        ts(R("AS", h, S_(1, 16, 2)), X, -983.5, A.is_gt, 16384.0, A.mult)
+        scan(R("sel", h), R("AS", h), R(L, S_(16, 32)), A.add)
+        ts(R("npr", h), X, -984.0, A.not_equal, 1056.0, A.mult)
+        ts(R("nu", h), R("sel", h), 2047.0, A.add)
         ts(R("nv", h), R("nu", h), 1023, A.bitwise_and)
-        ts(R("nlu", h), E, 2063.0, A.add)
-        v, u = R("nv", h, S_(0, 8)), R("nv", h, S_(8, 16))
-        tt(R("dvu", h), v, u, A.subtract)
-        ts(R("pr", blk(h, 8)), X, 64.0, A.is_equal)
-        tt(R("ms", h), R("dvu", h), R("a1", h), A.mult)
-        tt(R("wf", h), R("ms", h), u, A.add)
-        cp(R("wu", h), R("wf", h))
-        gat("V", R("sw", h), R("stw"), R("wu", h))
-        gat("V", R("cw", h), R("scw", S_(0, 1024)), R("wu", h))
+        cp(R("wu", h), R("nv", h, S_(1, 16, 2)))
+        gat("V", R("sw", h), R("stw"), R("wu", h), -2047.0)
+        gat("V", R("cw", h), R("scw", S_(0, 1024)), R("wu", h), -2047.0)
+        ts(R("nlu", h), R("sel", h, S_(0, 16, 2)), 2063.0, A.add)
         gat("S", R("ysb", h), WIN, R("nlu", h))
-        act(R("acr", h), R("ac", h), F.Relu, acc=R("asum", S_(k, k + 1)))
+        tt(R("PV", blk(h, 8)), R("nv", h, S_(0, 16, 2)), R("npr", h), A.add)
+        c = R(tmp("m", 1))
+        mm(chain(c, (BO, XS), (R("BO128n"), FC)))
+        act(R("SG", h), c, F.Sign, bias=cst(1064.5), scale=-1.0)
+        act(R("SA", h), c, F.Sign, bias=cst(999.5), scale=-1.0)
+        mm(chain(p, (I, Tn), (R("cmA", h), I4160n), (oh, I4160n)))
+        act(R("KTn", h), p, F.Sign, bias=cst(-2047.5), scale=-1.0)
+        ts(R("T1s", blk(h)), p, 2047.0, A.add, -1.0, A.max)
+        if t + 1 < NV:
+            c = R(tmp("m", 1))
+            mm(chain(c, (I, R("cdS", h)), (R("BO128n"), FC)))
+            act(R("acr", h), c, F.Relu, bias=cst(-2048.0), acc=R("asum", S_(k, k + 1)))
         if t + 1 < NV and h == 1:
-            a = R(BK["tot"], S_(0, 1))
+            a = R(tmp("m", 1), S_(0, 1))
             mm(chain(a, *[(R("bo32"), R("asum", S_(i, i + 1))) for i in range(2 * t + 2)]))
             cp(R("ai"), a)
             ts(R("a31"), R("ai"), 31, A.bitwise_and)
             ts(R("nlim", S_(t + 1, t + 2)), R("a31"), -8.0, A.mult, R("thn"), A.add)
-        ts(R("KTf", h), R("T1", h), -2047.5, A.is_gt)
-        ts(R("T1s", blk(h)), R("T1", h), 2047.0, A.add, -1.0, A.max)
-        for hb in (0, 1):
-            gat("S", R("XG", h, blk(hb, 1024)), WIN, R("D1u", h, blk(hb, 64)))
 
     def out(name, buf, c, lat=2500):
         add("Y", 60, lambda g, T: g.sync.dma_start(T[name][:, c], get(T, R(buf, c))), [R(buf, c)], [], tok="so", lat=lat)
 
     def stageC(t, h):
         k, last = 2 * t + h, t == NV - 1
-        SG, Ib = R("SG", h), R("Ib")
-        p0, p1 = R(BK["h"], S_(0, 128)), R(BK["h"], S_(128, 256))
-        for x, held, cw, eq, c1, m, keep, one, snd, land, low in (("t", "Tq", "sw", "eqC", "C1t", "Tm", "KTf", "T1", "stt", "tt", -2050.0),
-                                                                  ("d", "Dq", "cw", "eqB", "C1", "Dm", "KD", "D1", "sd", "dt", -2048.0)):
-            member(cw, held, eq, h)
-            cnt = counts(eq, "cm" + eq[2], h, BK["cc"])
-            mm(chain(p1, (R("I16"), R(one, h)), (R("Ib4096n"), SG), (Ib, R("cm4096"))) +
-               chain(p0, (Ib, R("c67584")), (R("Ib65536"), SG), (R("Im16"), R(keep, h)), cnt))
-            tt(R(c1, h), R(cw, h), p0, A.min)
-            tt(R(m, h), R(c1, h), p1, A.max)
-            if last:
-                ts(R("o" + x, blk(h)), R(m, h), 2047.0, A.add, -1.0, A.max)
-                out("y" + x, "o" + x, blk(h))
-            else:
-                ts(R(snd, k), R(m, h), low, A.max, 2063.0, A.add)
-                send(t, h, x, snd, land)
-        scan(R("xs", h), R("rst"), R("XG", h))
-        c = [R(BK["z"], blk(i)) for i in range(4)]
-        ys = R("ysb", h)
-        mm(chain(c[0], (R("Ibh"), ys), (R("Ibh"), R("xs", h, S_(15, 2048, 16))), (R("Ib512n"), SG)) +
-           chain(c[1], (Ib, R("zl", k)), (R("Ib256"), SG)) + chain(c[2], (Ib, ys), (R("Ib256n"), R("SA", h))))
-        ts(R("hf", h), c[0], 511.75, A.add, 1024.0, A.max)
-        act(R("zg", h), c[1], F.Relu, bias=R("cst", S_(2, 3)))
-        act(R("yg", h), c[2], F.Relu, bias=R("cst", S_(2, 3)))
-        mm(chain(c[3], (R("I16"), R("hf", h)), (Ib, R("zg", h)), (R("Ibn"), R("yg", h))))
-        act(R("oz", blk(h)) if last else R("sz", k), c[3], F.Abs, bias=R("cst", S_(3, 4)))
+        SG, Tn, one = R("SG", h), R("Tq", h), R("one")
+        for q in range(4):
+            b = tmp("s", 4)
+            mm(sum([chain(R(b, blk(i)), (R("bc", blk(4 * q + i)), R("sw", h)), (In, Tn)) for i in range(4)], []))
+            act(R("fC", h, blk(q, 512)), R(b), F.Tanh, bias=cst(0.0156263), scale=16.0)
+        b = tmp("m", 2)
+        mm([(R(b, S_(j, 256, 16)), R("fC", h, blk(j)), R("BOpm"), True, True) for j in range(16)])
+        act(R("rC", h), R(b), F.Copy, bias=-192.49, scale=-1.0)
+        p0, p1 = R(tmp("m", 1)), R(tmp("m", 1))
+        mm(chain(p1, (I, Tn), (R("cmA", h), I4160n), (R("oh", h), I4160n), (I4160n, SG), (I4160n, one)))
+        mm(chain(p0, (I17, SG), (R("I16"), R("KTn", h)), (I17, R("c385")), (R("rC", h, blk(0)), I17), (R("rC", h, blk(1)), I17)))
+        tt(R("C1t", h), R("sw", h), p0, A.min)
+        tt(R("Tm", h), R("C1t", h), p1, A.max)
+        if last:
+            ts(R("ot", blk(h)), R("Tm", h), 2047.0, A.add, -1.0, A.max)
+            out("yt", "ot", blk(h))
+        else:
+            ts(R("stt", k), R("Tm", h), -2063.0, A.max, 2063.0, A.add)
+            send(t, h, "t", "stt", R("tt", k + 2))
+        member(R("cw", h), R("Dq", k), "eqB", h)
+        b = tmp("m", 1)
+        mm([(R(b, S_(j, 128, 16)), R("eqB", h, blk(j)), BO8, True, True) for j in range(16)])
+        act(R("cmB", h), R(b), F.Sign, scale=-1.0)
+        p0, p1 = R(tmp("m", 1)), R(tmp("m", 1))
+        mm(chain(p1, (I, R("D1", h)), (I4160n, SG), (I4160n, one)))
+        mm(chain(p0, (I17, SG), (I17, R("nk", h)), (R("cmB", h), I17)))
+        tt(R("C1", h), R("cw", h), p0, A.min)
+        tt(R("sd", k), R("C1", h), p1, A.max)
+        if last:
+            ts(R("od", blk(h)), R("sd", k), 2047.0, A.add, -1.0, A.max)
+            out("yd", "od", blk(h))
+        else:
+            send(t, h, "d", "sd", R("Dq", k + 2, S_(0, 128)))
+        ys, c0, b, c3 = R("ysb", h), R(tmp("m", 1)), tmp("m", 2), R(tmp("m", 1))
+        mm(chain(c0, (R("Ih"), ys), (R("Ih"), R("xs", h, S_(15, 2048, 16))), (I4160n, SG)))
+        ts(R("hf", h), c0, 1023.75 - 4160.0, A.add, 1024.0, A.max)
+        mm(chain(R(b, blk(0)), (I, R("zl", k)), (I17, SG)) + chain(R(b, blk(1)), (I, ys), (I17, R("SA", h))))
+        act(R("zy", h), R(b), F.Relu, bias=cst(-131072.0))
+        mm(chain(c3, (I, R("hf", h)), (I, R("zy", h, blk(0))), (In, R("zy", h, blk(1)))))
+        act(R("oz", blk(h)) if last else R("sz", k), c3, F.Abs, bias=cst(-1024.0))
         if last:
             out("yz", "oz", blk(h))
         else:
-            send(t, h, "z", "sz", "zl")
+            send(t, h, "z", "sz", R("zl", k + 2))
 
     def stageD(t):
-        b, b2 = BK["d"], BK["d2"]
-        for h in (0, 1):
-            tt(R("dvq", blk(h, 8)), R("nv", h, S_(0, 8)), R("q0", blk(h, 8)), A.subtract)
-        tt(R("mvq"), R("dvq"), R("pr"), A.mult)
-        tt(R("PV16"), R("mvq"), R("q0"), A.add)
-        tt(R("PV"), R("mvq"), R("q0"), A.add)
-        mm([(R(b2, S_(r, 256, 16)), R("I16"), R("PV16"), True, True) for r in range(16)])
-        act(R("PVs"), R(b2, S_(0, 256)), F.Copy)
-        mm([(R(b, S_(0, 256)), R("I16"), R("tri"), True, False)] +
-           [(R(b, S_(r, 256, 16)), R("bc", blk(r)), R("PV16"), False, r == 15) for r in range(16)])
-        tt(R("eqP"), R("PVs"), R(b, S_(0, 256)), A.is_equal)
-        mm(chain(R(b, S_(0, 16)), *[(R("selm", blk(r)), R("eqP", S_(r, 256, 16))) for r in range(16)]))
-        tt(R("dq2"), R("q0"), R("PV"), A.subtract)
-        ts(R("lm"), R(b, S_(0, 16)), -1.0, A.is_lt)
-        tt(R("lq"), R("lm"), R("dq2"), A.mult)
-        tt(R("PLf"), R("lq"), R("PV"), A.add)
-        cp(R("PLu", S_(0, 32, 2)), R("PLf"))
+        b, PV = tmp("m", 2), R("PV")
+        mm([(R(b), I, R("tri"), True, False)] +
+           [(R(b, S_(r, 256, 16)), x, PV, False, r == 15 and x == In) for r in range(16) for x in (R("bc", blk(r)), In)])
+        ts(R("eqP"), R(b), 0.0, A.is_equal)
+        c = R(tmp("m", 1), S_(0, 16))
+        mm(chain(c, (I, PV), *[(R("I4096"), R("eqP", S_(r, 256, 16))) for r in range(16)]))
+        ts(R("PLu", S_(0, 32, 2)), c, R("q0"), A.min)
         for c in range(16):
             o, off, src = R("scw"), R("PLu", S_(2 * c, 2 * c + 1)), R("T1s", blk(c, 16))
-            add("V", 100, lambda g, T, o=o, off=off, src=src: g.vector.tensor_copy(get(T, o).indirect(get(T, off)), get(T, src)), [off, src], [o])
+            add("V", 60 + 16 * 3.8 * CYC, lambda g, T, o=o, off=off, src=src: g.vector.tensor_copy(get(T, o).indirect(get(T, off)), get(T, src)), [off, src], [o])
         if t == NV - 1:
             out("ys", "scw", S_(0, 1024), 4500)
 
@@ -403,24 +417,25 @@ def depend(ops):
     for i, o in enumerate(ops):
         pw, acc = set(), {}
         for x, wr in [(x, False) for x in o["r"]] + [(x, True) for x in o["w"]]:
-            sp = () if psum(x) else tuple(s[:2] for s in span(x))
+            sp = tuple(s[:3] for s in span(x))
             acc[(x[0], sp)] = acc.get((x[0], sp), False) or wr
         for (name, sp), wr in acc.items():
             for j, sj, wj in hist.get(name, ()):
-                if j != i and all(a[0] < b[1] and b[0] < a[1] for a, b in zip(sp, sj)):
-                    if wj or wr or ops[j]["e"] != o["e"] and SCRATCH[name][0] == "psum":
-                        pw.add(j)
+                if j != i and (wj or wr) and meet(sp, sj):
+                    pw.add(j)
         for (name, sp), wr in acc.items():
             h = hist.setdefault(name, [])
             if wr:
-                h[:] = [y for y in h if y[0] == i or not all(a[0] <= b[0] and b[1] <= a[1] for a, b in zip(sp, y[1]))]
+                h[:] = [y for y in h if y[0] == i or not cover(sp, y[1])]
             h.append((i, sp, wr))
         o["pw"] = pw
+        o["t"] = sorted({x[0] for x in o["r"] + o["w"] if psum(x)})
 
 
 def schedule(ops):
     n = len(ops)
     succ, cnt = [[] for _ in range(n)], [0] * n
+    users = {}
     for i, o in enumerate(ops):
         ps = [(j, WAKE if ops[j]["e"] != o["e"] else SELF) for j in o["pw"]]
         if "after" in o:
@@ -428,25 +443,64 @@ def schedule(ops):
         cnt[i] = len(ps)
         for j, l in ps:
             succ[j].append((i, l))
+        for x in o["t"]:
+            users[x] = users.get(x, 0) + 1
     fin = [o["d"] + o.get("lat", 0.0) for o in ops]
     pri = [0.0] * n
     for i in range(n - 1, -1, -1):
         pri[i] = BIAS.get(ops[i]["g"], 0.0) + fin[i] + max([0.0] + [l + pri[k] for k, l in succ[i]])
-    rdy, free, order = [0.0] * n, {}, []
+    pri = [p + LEAD.get(o["g"], 0.0) for p, o in zip(pri, ops)]
+    rdy, free, order, end = [0.0] * n, {}, [], {}
+    last = [{} for _ in range(8)]
+    held = [[None] * 4 for _ in range(8)]
+    past = [[{} for _ in range(4)] for _ in range(8)]
+
+    def start(i):
+        o = ops[i]
+        s, new, pw = max(rdy[i], free.get(o["e"], 0.0)), {}, set()
+        for x in o["t"]:
+            if x in PLACE:
+                opts = [PLACE[x]]
+            else:
+                role, m = TEMP[x]
+                opts = [(b, a) for b in BANKS[role] for a in range(0, 5 - m) if all(held[b][c] is None for c in range(a, a + m))]
+            best = None
+            for b, a in opts:
+                w = {j for e, j in last[b].items() if e != o["e"]}
+                if x not in PLACE:
+                    w |= {j for c in range(a, a + TEMP[x][1]) for j in past[b][c].values()}
+                s1 = max([s] + [end[j] + WAKE for j in w])
+                if best is None or s1 < best[0]:
+                    best = (s1, (b, a), w)
+            if best is None:
+                return None
+            s, new[x] = best[0], best[1]
+            pw |= best[2]
+        return s, new, pw
     ready = [i for i in range(n) if cnt[i] == 0]
     while ready:
-        st = {i: max(rdy[i], free.get(ops[i]["e"], 0.0)) for i in ready}
-        tmin = min(st.values()) + LOOK
-        i = max((j for j in ready if st[j] <= tmin), key=lambda j: pri[j])
+        st = {i: start(i) for i in ready}
+        can = [i for i in ready if st[i]]
+        tmin = min(st[i][0] for i in can) + LOOK
+        i = max((j for j in can if st[j][0] <= tmin), key=lambda j: pri[j])
         ready.remove(i)
-        o, s = ops[i], st[i]
-        o["s"] = s
+        o = ops[i]
+        s, new, pw = st[i]
+        o["s"], end[i] = s, s + fin[i]
+        o["pw"] = o["pw"] | pw
+        for x, (b, a) in new.items():
+            PLACE[x] = (b, a)
+            users[x] -= 1
+            last[b][o["e"]] = i
+            for c in range(a, a + TEMP[x][1]):
+                held[b][c] = x if users[x] else None
+                past[b][c][o["e"]] = i
         if o["e"] != "R":
             free[o["e"]] = s + o["d"]
         order.append(i)
         for k, l in succ[i]:
             cnt[k] -= 1
-            rdy[k] = max(rdy[k], s + fin[i] + l)
+            rdy[k] = max(rdy[k], end[i] + l)
             if cnt[k] == 0:
                 ready.append(k)
     return order

@@ -14,32 +14,33 @@ def _decl(text, d, lead):
 
 
 _decl("tli:256 dli:256 thi:1 sci:1024 sti:1024 pidx:1 pmi:1 ai:1 a31:1", i32, [])
-_decl("tm0:256 ts0:256 stw:1024 scw:1040 pmf:1 iq:256 P1:16 on32:128 boa:128 bo32:128 id32:128 "
+_decl("tm0:256 ts0:256 stw:1024 scw:1040 pmf:1 iq:16 P1:16 Pd:8 on32:128 boa:128 bo32:128 id32:128 "
       "q0:1 thn:1 nlim:8 asum:16 T1s:256 od:256 ot:256 oz:256 cst:10", f32, [])
-_decl("PV:16 c385:128", f16, [])
-_decl("clkw:4112 bc:2048 rst:1024 rowc:256 Zs:144 KB:16 BOpm:16 tri:256 eqP:256", b16, [])
+_decl("PV:16", f16, [])
+_decl("clkw:4112 bc:2048 bd:1024 dd:2048 rst:1024 rowc:256 Zs:144 KB:16 eqP:256 zl:256", b16, [])
 _decl("PLu:32", u16, [])
-_decl("Tq:128 D1:128 Q:256 cw:128 sw:128 hf:128 dst:128 Tm:128", f16, [2])
-_decl("eqA:2048 eqB:2048 fC:2048 Y:2048 MN:2048 XG:2048 xs:2048 nk:128 oh:128 cmA:128 cmB:128 rC:256 cdS:128 FC:128 SG:128 SA:128 "
-      "KTn:128 ysb:128 zy:256 acr:128", b16, [2])
-_decl("sk:128 sk2:128 AS:16 sel:16 npr:8 C1:128 C1t:128", f32, [2])
+_decl("Tq:512 D1:128 cw:128 sw:128 hf:128 dst:128 Tm:128 zy:256", f16, [2])
+_decl("eqA:2048 eqB:2048 fC:2048 Y:2048 MN:2048 XG:2048 xs:2048 nk:128 oh:128 cmA:128 cmB:128 rC:256 FC:128 NG:128 NA:128 "
+      "KTn:128 ysb:128 acr:128", b16, [2])
+_decl("sk:128 sk2:128 AS:8 sel:8 npr:8 C1:128 C1t:128", f32, [2])
 _decl("nu:16 nv:16", i32, [2])
 _decl("D1u:128 nlu:8 wu:8", u16, [2])
 _decl("tt:128 stt:128", u16, [2 * NV])
-_decl("Dq:512 sd:128", f16, [2 * NV])
-_decl("zl:128 sz:128", b16, [2 * NV])
-_l = "I In I4160n I17 I16 Ih I64 I4096 BO BO128n c2048 one".split()
+_decl("Dq:512 Q:384 sd:128 sz:128", f16, [2 * NV])
+_l = "I In I4160n I17 I16 Ih I64 I4096 BO BO128n".split()
 SCRATCH["kb"] = ("sbuf", [128, len(_l), 128], b16)
 for _i, _n in enumerate(_l):
     ALIAS[_n] = ("kb", _i)
 for _i in range(8):
     SCRATCH["ps%d" % _i] = ("psum", [128, 512], f32)
 BANKS = {"v": (0, 1), "s": (2, 3), "z": (4,), "m": (5, 6, 7)}
-LOADS = ("tl", "dl", "za", "zb", "th", "clk", "st", "sc")
+LOADS = ("tl", "dl", "z", "th", "clk", "st", "sc")
+OPT = dict(xs="S", dst="S", sw="S", cw="V", hf="V", delta=0)
 SEMAPHORES = ["sv", "ss", "sp", "sg", "so", "ls"] + ["l_" + n for n in LOADS]
 SEMAPHORES += ["a%d%d%s" % (t, h, k) for t in range(1, NV) for h in (0, 1) for k in "dtz"]
-CYC, PEC, OVV, OVS, WAKE, SELF, REMOTE, LOOK = 0.83, 0.43, 30.0, 40.0, 90.0, 90.0, 3500.0, 20.0
-BIAS, LEAD = {}, {"A0": 4000.0, "B0": 4000.0, "C0": 4000.0}
+CYC, PEC, OVV, OVS, WAKE, SELF, REMOTE, LOOK = 0.83, 0.43, 30.0, 40.0, 90.0, 90.0, 3500.0, 0.5
+ROUNDS, LOOKB = 6, 0.1
+LEAD = {"A0": 4000.0, "B0": 4000.0, "C0": 4000.0}
 TEMP, PLACE = {}, {}
 
 
@@ -143,7 +144,7 @@ def program(nrem):
         def fn(g, T):
             x = get(T, win).indirect(get(T, off))
             if e == "S":
-                return g.scalar.activation(get(T, o), x, F.Copy)
+                return g.scalar.activation(get(T, o), x, F.Copy, bias=shift or 0.0)
             return g.vector.tensor_copy(get(T, o), x) if shift is None else g.vector.tensor_scalar(get(T, o), x, shift, None, A.add)
         add(e, 60 + 1.56 * size(o) * CYC, fn, [win, off], [o])
 
@@ -164,8 +165,7 @@ def program(nrem):
     load("S", "clk", R("clkw", S_(16, 4112)), lambda T: T.clk[:, :], 5000)
     load("Y", "tl", R("tli"), lambda T: T.tl[:, :], 2200)
     load("Y", "dl", R("dli"), lambda T: T.dl[:, :], 2500)
-    load("Y", "za", R("zl", 0), lambda T: T.z0[:, 0:128], 2600)
-    load("Y", "zb", R("zl", 1), lambda T: T.z0[:, 128:256], 2700)
+    load("Y", "z", R("zl"), lambda T: T.z0[:, :], 2700)
     load("Y", "th", R("thi"), lambda T: T.th[:, :], 2800)
     load("Y", "st", R("sti"), lambda T: T.st[:, :], 6500)
     load("Y", "sc", R("sci"), lambda T: T.sc[:, :], 8000)
@@ -177,15 +177,18 @@ def program(nrem):
     def aff(o, i, pat, op, base, cm, other=0.0):
         add("G", 170 + 2 * CYC * size(o), lambda g, T: g.affine_select(get(T, o), get(T, i), pat, op, other, base, cm), [i], [o])
 
-    def spread(k):
+    def spread(x, k):
         for n in (128, 256):
-            aff(R("Dq", k, S_(n, 2 * n)), R("Dq", k, S_(0, n)), [[0, n]], A.is_ge, 0, 0)
+            aff(R(x, k, S_(n, 2 * n)), R(x, k, S_(0, n)), [[0, n]], A.is_ge, 0, 0)
+
+    def shift(e, o, i, x):
+        return act(o, i, F.Copy, bias=x) if e == "S" else ts(o, i, x, A.add)
     fill(R("on32"), 1.0)
     iota(R("pidx"), [[0, 1]], 0, 1)
     aff(R("boa"), R("on32"), [[-16, 8], [0, 16]], A.is_ge, 0, 1)
     aff(R("bo32"), R("boa"), [[16, 8], [0, 16]], A.is_ge, 15, -1)
     aff(R("id32"), R("on32"), [[-1, 128]], A.is_equal, 0, 1)
-    iota(R("iq"), [[0, 16], [1, 16]], 0)
+    iota(R("iq"), [[1, 16]], 0)
     fill(R("rowc", blk(1)), 0.0)
     iota(R("rowc", blk(0)), [[0, 8], [-1, 16]], 16)
     ts(R("pmi"), R("pidx"), 15, A.bitwise_and)
@@ -201,23 +204,28 @@ def program(nrem):
                       ("I64", "id32", 64), ("I4096", "id32", 4096), ("BO128n", "bo32", -128)):
         act(R(n), R(src), F.Copy, scale=float(k))
     BO8 = R("BO", S_(0, 128, 16))
-    for n, k0, k1 in (("KB", 16.0, -2.0), ("BOpm", 1.0, -1.0)):
-        ts(R(n, S_(0, 8)), BO8, k0, A.mult)
-        ts(R(n, S_(8, 16)), BO8, k1, A.mult)
+    ts(R("KB", S_(0, 8)), BO8, 16.0, A.mult)
+    ts(R("KB", S_(8, 16)), BO8, -2.0, A.mult)
     fill(R("Zs"), 0.0)
     cp(R("Zs", S_(15, 143, 16)), BO8)
     iota(R("rst"), [[0, 64], [1, 16]], 0)
     aff(R("rst"), R("rst"), [[0, 64], [1, 16]], A.is_equal, 0, 0, 1.0)
-    for n, x in (("c2048", 2048.0), ("one", 1.0), ("c385", 385.0), ("AS", -1.0e6)):
-        fill(R(n), x)
-    CST = (2048.0, 1064.5, 999.5, -2048.0, -131072.0, -1024.0, -2047.5, 0.0156263)
+    aff(R("dd"), R("bc"), [[1, 16], [0, 8], [-1, 16]], A.is_gt, 0, 0)
+    aff(R("dd"), R("dd"), [[0, 16], [-1, 128]], A.not_equal, 0, 1, -1.0)
+    if OPT["delta"]:
+        tt(R("Pd"), R("P1", S_(8, 16)), R("P1", S_(0, 8)), A.subtract)
+        for j in range(8):
+            ts(R("bd", blk(j)), R("BO"), R("Pd", S_(j, j + 1)), A.mult)
+    CST = (2048.0, 4322.0, -1015.5, -64.0, -1024.0, -2047.5, 0.0156263, 1023.75, 1024.0)
     for i, x in enumerate(CST):
-        fill(R("cst", S_(i, i + 1)), x)
+        if OPT["hf"] == "S" or i < 7:
+            fill(R("cst", S_(i, i + 1)), x)
 
     def cst(x):
         return R("cst", S_(CST.index(x), CST.index(x) + 1))
-    ts(R("tri"), R("iq"), pm, A.is_le, 4096.0, A.mult)
     ts(R("q0"), pm, 1024.0, A.add)
+    for h in (0, 1):
+        act(R("Q", h, blk(2)), R("zl", blk(h)), F.Copy)
     ts(R("tm0"), R("tli"), 0.0, A.min, 2.0, A.mult)
     tt(R("ts0"), R("tli"), R("tm0"), A.add)
     for h in (0, 1):
@@ -250,35 +258,30 @@ def program(nrem):
             mm([(R(b, blk(i)), R("bc", blk(4 * q + i)), rows, True, True) for i in range(4)])
             tt(R(eq, h, blk(q, 512)), held, R(b), A.is_equal)
 
-    def to_list(o, x, n):
-        return [(o, R("Zs", S_(15 - r, 143 - r)), (x[0], x[1] + (S_(r, n, 16),))) for r in range(16)]
-
     def stageA(t, h):
         k = 2 * t + h
-        D, Z, Tn = R("Dq", k, S_(0, 128)), R("zl", k), R("Tq", h)
+        D, Z, Tn = R("Dq", k, blk(0)), R("Q", k, blk(2)), R("Tq", h, blk(0))
         arrive(t, h, "t", R("tt", k))
         arrive(t, h, "d", D)
         arrive(t, h, "z", Z)
         for hb in (0, 1):
             gat("S", R("Y", h, blk(hb, 1024)), WIN, R("tt", k, blk(hb, 64)))
         ts(Tn, R("tt", k), -2063.0, A.add)
-        spread(k)
+        spread("Dq", k)
+        if OPT["delta"]:
+            spread("Tq", h)
         b = tmp("z", 4)
         mm([(R(b, S_(i, 512, 4)), I, Z, True, True) for i in range(4)])
         for hb in (0, 1):
             for q in range(4):
                 c = S_(1024 * hb + q, 1024 * hb + 1024, 4)
                 tt(R("MN", h, c), R("Y", h, c), R(b, blk(hb, 256)), A.min)
-        lists[h] = L = tmp("m", 1)
-        u = [(x[1], x[2]) for x in to_list(None, R("zl", k), 128)]
-        mm(chain(R(L, S_(17, 32, 2)), (I, R("c2048", S_(0, 8))), (I, R("one", S_(0, 8))), *u))
         member(Tn, R("Dq", k), "eqA", h)
         pD = R(tmp("m", 1))
-        mm(chain(pD, (I, R("c2048")), *[(I4160n, R("eqA", h, blk(j))) for j in range(16)]))
-        tt(R("D1", h), D, pD, A.min)
-        act(R("cdS", h), pD, F.Sign, bias=cst(2048.0), scale=-1.0)
+        mm(chain(pD, (I, D), *[(I4160n, R("eqA", h, blk(j))) for j in range(16)]))
+        ts(R("D1", h), pD, -2112.0, A.max)
         ts(R("D1u", h), R("D1", h), -2048.0, A.max, 2063.0, A.add)
-        ts(R("nk", h), R("D1", h), -2047.5, A.is_le, 0.5, A.add)
+        ts(R("nk", h), R("D1", h), -2047.5, A.is_le, -0.5, A.add)
         b = tmp("m", 1)
         mm([(R(b, S_(j, 128, 16)), R("eqA", h, blk(j)), BO8, True, True) for j in range(16)])
         act(R("cmA", h), R(b), F.Sign)
@@ -288,7 +291,7 @@ def program(nrem):
 
     def stageB(t, h):
         k = 2 * t + h
-        Z, Tn, rs, oh = R("zl", k), R("Tq", h), R("rst", S_(0, 128)), R("oh", h)
+        Z, Tn, rs, oh = R("Q", k, blk(2)), R("Tq", h, blk(0)), R("rst", S_(0, 128)), R("oh", h)
         b = tmp("m", 2)
         kk, d = R(b, blk(0)), R(b, blk(1))
         mm([(R(b), I, R("rowc"), True, False), (d, Z, BO, False, False)] +
@@ -297,41 +300,42 @@ def program(nrem):
         scan(R("sk", h), rs, kk)
         scan(R("sk2", h, S_(None, None, -1)), rs, R("sk", h, S_(None, None, -1)))
         tt(oh, R("sk2", h), kk, A.is_equal)
-        ts(R("dst", h), d, -2040.0, A.add)
+        shift(OPT["dst"], R("dst", h), d, -2040.0)
         d = R(tmp("m", 1))
         mm(chain(d, (R("dst", h), In), (R("cmA", h), I4160n)))
         act(R("FC", h), d, F.Sign, bias=R("nlim", S_(t, t + 1)), scale=-1.0)
-        FC, XS, KT = R("FC", h), R("Q", h, blk(0)), R("Q", h, blk(1))
+        FC, XS, KT = R("FC", h), R("Q", k, blk(0)), R("Q", k, blk(1))
         o1, x, p = R(tmp("m", 1)), R(tmp("m", 1)), R(tmp("m", 1))
         mm(chain(o1, (oh, I)))
         tt(KT, Tn, o1, A.mult)
         mm(chain(x, (In, R("nk", h)), (R("I64"), FC), (oh, R("I64"))))
-        cp(XS, x)
-        L = lists[h]
-        mm(chain(R(L, S_(0, 32, 2)), *[(y[1], y[2]) for y in to_list(None, R("Q", h), 256)]))
-        X = R(L, S_(0, 16, 2))
-        ts(R("AS", h, S_(1, 16, 2)), X, -983.5, A.is_gt, 16384.0, A.mult)
-        scan(R("sel", h), R("AS", h), R(L, S_(16, 32)), A.add)
-        ts(R("npr", h), X, -984.0, A.not_equal, 1056.0, A.mult)
-        ts(R("nu", h), R("sel", h), 2047.0, A.add)
+        shift(OPT["xs"], XS, x, 0.0)
+        L = tmp("m", 1)
+        mm(chain(R(L, S_(0, 24)), *[(R("Zs", S_(15 - r, 143 - r)), R("Q", k, S_(r, 384, 16))) for r in range(16)]))
+        X, E, U = R(L, S_(0, 8)), R(L, S_(8, 16)), R(L, S_(16, 24))
+        ts(R("AS", h), X, -967.5, A.is_gt, 16384.0, A.mult)
+        ts(R("nu", h, S_(0, 8)), E, 2047.0 - 8192.0, A.add)
+        tt(R("sel", h), R("nu", h, S_(0, 8)), R("AS", h), A.add)
+        tt(R("nu", h, S_(8, 16)), R("sel", h), U, A.max)
+        ts(R("npr", h), X, -968.0, A.is_equal, -1056.0, A.mult)
+        ts(R("nlu", h), E, 2063.0, A.add)
         ts(R("nv", h), R("nu", h), 1023, A.bitwise_and)
-        cp(R("wu", h), R("nv", h, S_(1, 16, 2)))
-        gat("V", R("sw", h), R("stw"), R("wu", h), -2047.0)
-        gat("V", R("cw", h), R("scw", S_(0, 1024)), R("wu", h), -2047.0)
-        ts(R("nlu", h), R("sel", h, S_(0, 16, 2)), 2063.0, A.add)
+        cp(R("wu", h), R("nv", h, S_(8, 16)))
+        gat(OPT["sw"], R("sw", h), R("stw"), R("wu", h), -2047.0)
+        gat(OPT["cw"], R("cw", h), R("scw", S_(0, 1024)), R("wu", h), -2047.0)
         gat("S", R("ysb", h), WIN, R("nlu", h))
-        tt(R("PV", blk(h, 8)), R("nv", h, S_(0, 16, 2)), R("npr", h), A.add)
+        tt(R("PV", blk(h, 8)), R("nv", h, S_(0, 8)), R("npr", h), A.add)
         c = R(tmp("m", 1))
         mm(chain(c, (BO, XS), (R("BO128n"), FC)))
-        act(R("SG", h), c, F.Sign, bias=cst(1064.5), scale=-1.0)
-        act(R("SA", h), c, F.Sign, bias=cst(999.5), scale=-1.0)
+        act(R("NG", h), c, F.Relu, bias=cst(4322.0), scale=-4.0)
+        act(R("NA", h), c, F.Relu, bias=cst(-1015.5))
         mm(chain(p, (I, Tn), (R("cmA", h), I4160n), (oh, I4160n)))
         act(R("KTn", h), p, F.Sign, bias=cst(-2047.5), scale=-1.0)
-        ts(R("T1s", blk(h)), p, 2047.0, A.add, -1.0, A.max)
+        act(R("T1s", blk(h)), p, F.Relu, bias=cst(2048.0))
         if t + 1 < NV:
             c = R(tmp("m", 1))
-            mm(chain(c, (I, R("cdS", h)), (R("BO128n"), FC)))
-            act(R("acr", h), c, F.Relu, bias=cst(-2048.0), acc=R("asum", S_(k, k + 1)))
+            mm(chain(c, (In, R("D1", h)), (R("BO128n"), FC)))
+            act(R("acr", h), c, F.Relu, bias=cst(-64.0), scale=1.0 / 64, acc=R("asum", S_(k, k + 1)))
         if t + 1 < NV and h == 1:
             a = R(tmp("m", 1), S_(0, 1))
             mm(chain(a, *[(R("bo32"), R("asum", S_(i, i + 1))) for i in range(2 * t + 2)]))
@@ -344,17 +348,24 @@ def program(nrem):
 
     def stageC(t, h):
         k, last = 2 * t + h, t == NV - 1
-        SG, Tn, one = R("SG", h), R("Tq", h), R("one")
+        NG, Tn, Z = R("NG", h), R("Tq", h, blk(0)), R("Q", k, blk(2))
+        bs = [tmp("s", 4) for _ in range(2 if OPT["delta"] else 4)]
         for q in range(4):
-            b = tmp("s", 4)
-            mm(sum([chain(R(b, blk(i)), (R("bc", blk(4 * q + i)), R("sw", h)), (In, Tn)) for i in range(4)], []))
+            b = bs[q % len(bs)]
+            if not OPT["delta"]:
+                mm(sum([chain(R(b, blk(i)), (R("bc", blk(4 * q + i)), R("sw", h)), (In, Tn)) for i in range(4)], []))
+            elif q < 2:
+                mm([(R(b), In, R("Tq", h), True, False)] + [(R(b, blk(i)), R("bc", blk(4 * q + i)), R("sw", h), False, False) for i in range(4)])
+            else:
+                mm([(R(b, blk(i)), R("bd", blk(4 * q + i - 8)), R("sw", h), False, i == 3) for i in range(4)])
             act(R("fC", h, blk(q, 512)), R(b), F.Tanh, bias=cst(0.0156263), scale=16.0)
-        b = tmp("m", 2)
-        mm([(R(b, S_(j, 256, 16)), R("fC", h, blk(j)), R("BOpm"), True, True) for j in range(16)])
-        act(R("rC", h), R(b), F.Copy, bias=-192.49, scale=-1.0)
+        b = tmp("m", 1)
+        mm([(R(b, S_(j, 128, 16)), R("fC", h, blk(j)), BO8, True, True) for j in range(16)])
+        act(R("rC", h, blk(0)), R(b), F.Copy, bias=-192.49, scale=-1.0)
+        act(R("rC", h, blk(1)), R(b), F.Copy, bias=192.0)
         p0, p1 = R(tmp("m", 1)), R(tmp("m", 1))
-        mm(chain(p1, (I, Tn), (R("cmA", h), I4160n), (R("oh", h), I4160n), (I4160n, SG), (I4160n, one)))
-        mm(chain(p0, (I17, SG), (R("I16"), R("KTn", h)), (I17, R("c385")), (R("rC", h, blk(0)), I17), (R("rC", h, blk(1)), I17)))
+        mm(chain(p1, (I, Tn), (R("cmA", h), I4160n), (R("oh", h), I4160n), (I4160n, NG)))
+        mm(chain(p0, (I17, NG), (R("I16"), R("KTn", h)), (R("rC", h, blk(0)), I17), (R("rC", h, blk(1)), I17)))
         tt(R("C1t", h), R("sw", h), p0, A.min)
         tt(R("Tm", h), R("C1t", h), p1, A.max)
         if last:
@@ -368,8 +379,8 @@ def program(nrem):
         mm([(R(b, S_(j, 128, 16)), R("eqB", h, blk(j)), BO8, True, True) for j in range(16)])
         act(R("cmB", h), R(b), F.Sign, scale=-1.0)
         p0, p1 = R(tmp("m", 1)), R(tmp("m", 1))
-        mm(chain(p1, (I, R("D1", h)), (I4160n, SG), (I4160n, one)))
-        mm(chain(p0, (I17, SG), (I17, R("nk", h)), (R("cmB", h), I17)))
+        mm(chain(p1, (I, R("D1", h)), (I4160n, NG)))
+        mm(chain(p0, (R("I4096"), NG), (R("I4096"), R("nk", h)), (R("cmB", h), R("I4096"))))
         tt(R("C1", h), R("cw", h), p0, A.min)
         tt(R("sd", k), R("C1", h), p1, A.max)
         if last:
@@ -378,28 +389,33 @@ def program(nrem):
         else:
             send(t, h, "d", "sd", R("Dq", k + 2, S_(0, 128)))
         ys, c0, b, c3 = R("ysb", h), R(tmp("m", 1)), tmp("m", 2), R(tmp("m", 1))
-        mm(chain(c0, (R("Ih"), ys), (R("Ih"), R("xs", h, S_(15, 2048, 16))), (I4160n, SG)))
-        ts(R("hf", h), c0, 1023.75 - 4160.0, A.add, 1024.0, A.max)
-        mm(chain(R(b, blk(0)), (I, R("zl", k)), (I17, SG)) + chain(R(b, blk(1)), (I, ys), (I17, R("SA", h))))
-        act(R("zy", h), R(b), F.Relu, bias=cst(-131072.0))
-        mm(chain(c3, (I, R("hf", h)), (I, R("zy", h, blk(0))), (In, R("zy", h, blk(1)))))
-        act(R("oz", blk(h)) if last else R("sz", k), c3, F.Abs, bias=cst(-1024.0))
+        mm(chain(c0, (R("Ih"), ys), (R("Ih"), R("xs", h, S_(15, 2048, 16))), (I4160n, NG)))
+        mm(chain(R(b, blk(0)), (I, Z), (I4160n, NG)) + chain(R(b, blk(1)), (I, ys), (I4160n, R("NA", h))))
+        if OPT["hf"] == "V":
+            ts(R("hf", h), c0, 1023.75, A.add, 1024.0, A.max)
+            act(R("zy", h), R(b), F.Relu)
+        else:
+            act(R("hf", h), c0, F.Relu, bias=cst(1023.75))
+            act(R("zy", h, blk(0)), R(b, blk(0)), F.Relu, bias=cst(1024.0))
+            act(R("zy", h, blk(1)), R(b, blk(1)), F.Relu)
+        mm(chain(c3, (I, Z), (I, R("hf", h)), (In, R("zy", h, blk(0))), (In, R("zy", h, blk(1)))))
+        act(R("oz", blk(h)) if last else R("sz", k), c3, F.Abs, bias=cst(-1024.0) if OPT["hf"] == "V" else 0.0)
         if last:
             out("yz", "oz", blk(h))
         else:
-            send(t, h, "z", "sz", R("zl", k + 2))
+            send(t, h, "z", "sz", R("Q", k + 2, blk(2)))
 
     def stageD(t):
         b, PV = tmp("m", 2), R("PV")
-        mm([(R(b), I, R("tri"), True, False)] +
-           [(R(b, S_(r, 256, 16)), x, PV, False, r == 15 and x == In) for r in range(16) for x in (R("bc", blk(r)), In)])
+        mm([(R(b, S_(r, 256, 16)), R("dd", blk(r)), PV, True, True) for r in range(16)])
         ts(R("eqP"), R(b), 0.0, A.is_equal)
         c = R(tmp("m", 1), S_(0, 16))
         mm(chain(c, (I, PV), *[(R("I4096"), R("eqP", S_(r, 256, 16))) for r in range(16)]))
-        ts(R("PLu", S_(0, 32, 2)), c, R("q0"), A.min)
+        ts(R("PLu", S_(0, 32, 2)), c, 1056.0, A.add, R("q0"), A.min)
         for c in range(16):
             o, off, src = R("scw"), R("PLu", S_(2 * c, 2 * c + 1)), R("T1s", blk(c, 16))
-            add("V", 60 + 16 * 3.8 * CYC, lambda g, T, o=o, off=off, src=src: g.vector.tensor_copy(get(T, o).indirect(get(T, off)), get(T, src)), [off, src], [o])
+            add("V", 60 + 16 * 3.8 * CYC, lambda g, T, o=o, off=off, src=src: g.vector.tensor_scalar(
+                get(T, o).indirect(get(T, off)), get(T, src), 1.0, -1.0, A.mult, A.add), [off, src], [o])
         if t == NV - 1:
             out("ys", "scw", S_(0, 1024), 4500)
 
@@ -434,22 +450,59 @@ def depend(ops):
 
 def schedule(ops):
     n = len(ops)
-    succ, cnt = [[] for _ in range(n)], [0] * n
-    users = {}
+    pred, succ = [], [[] for _ in range(n)]
     for i, o in enumerate(ops):
-        ps = [(j, WAKE if ops[j]["e"] != o["e"] else SELF) for j in o["pw"]]
-        if "after" in o:
-            ps.append((o["after"], REMOTE))
-        cnt[i] = len(ps)
-        for j, l in ps:
+        pred.append([(j, WAKE if ops[j]["e"] != o["e"] else SELF) for j in o["pw"]] + ([(o["after"], REMOTE)] if "after" in o else []))
+        for j, l in pred[i]:
             succ[j].append((i, l))
-        for x in o["t"]:
-            users[x] = users.get(x, 0) + 1
     fin = [o["d"] + o.get("lat", 0.0) for o in ops]
     pri = [0.0] * n
     for i in range(n - 1, -1, -1):
-        pri[i] = BIAS.get(ops[i]["g"], 0.0) + fin[i] + max([0.0] + [l + pri[k] for k, l in succ[i]])
+        pri[i] = fin[i] + max([0.0] + [l + pri[k] for k, l in succ[i]])
     pri = [p + LEAD.get(o["g"], 0.0) for p, o in zip(pri, ops)]
+    best = None
+    for _ in range(ROUNDS):
+        x = forward(ops, pred, succ, fin, pri)
+        if best is None or x[0] < best[0]:
+            best = x
+        pri = backward(ops, pred, succ, fin, x[2])
+    PLACE.update(best[4])
+    for i, o in enumerate(ops):
+        o["s"], o["pw"] = best[2][i] - fin[i], o["pw"] | best[3][i]
+    return best[1]
+
+
+def pick(ops, st, pri, look):
+    a = min(st, key=lambda j: st[j] + ops[j]["d"])
+    same = [j for j in st if ops[j]["e"] == ops[a]["e"]]
+    lo = min(st[j] for j in same)
+    return max((j for j in same if st[j] <= lo + look * (st[a] + ops[a]["d"] - lo)), key=lambda j: pri[j])
+
+
+def backward(ops, pred, succ, fin, pri):
+    cnt, rdy, free, out = [len(x) for x in succ], [0.0] * len(ops), {}, [0.0] * len(ops)
+    ready = [i for i in range(len(ops)) if cnt[i] == 0]
+    while ready:
+        st = {i: max(rdy[i] + fin[i] - ops[i]["d"], free.get(ops[i]["e"], 0.0)) for i in ready}
+        i = pick(ops, st, pri, LOOKB)
+        ready.remove(i)
+        out[i] = st[i] + ops[i]["d"]
+        if ops[i]["e"] != "R":
+            free[ops[i]["e"]] = out[i]
+        for k, l in pred[i]:
+            cnt[k] -= 1
+            rdy[k] = max(rdy[k], out[i] + l)
+            if cnt[k] == 0:
+                ready.append(k)
+    return out
+
+
+def forward(ops, pred, succ, fin, pri):
+    n = len(ops)
+    cnt, users, PLACE, more = [len(x) for x in pred], {}, {}, {}
+    for o in ops:
+        for x in o["t"]:
+            users[x] = users.get(x, 0) + 1
     rdy, free, order, end = [0.0] * n, {}, [], {}
     last = [{} for _ in range(8)]
     held = [[None] * 4 for _ in range(8)]
@@ -481,13 +534,13 @@ def schedule(ops):
     while ready:
         st = {i: start(i) for i in ready}
         can = [i for i in ready if st[i]]
-        tmin = min(st[i][0] for i in can) + LOOK
-        i = max((j for j in can if st[j][0] <= tmin), key=lambda j: pri[j])
+        if not can:
+            return 1e30, order, [end.get(i, 1e9) for i in range(n)]
+        i = pick(ops, {j: st[j][0] for j in can}, pri, LOOK)
         ready.remove(i)
         o = ops[i]
-        s, new, pw = st[i]
-        o["s"], end[i] = s, s + fin[i]
-        o["pw"] = o["pw"] | pw
+        s, new, more[i] = st[i]
+        end[i] = s + fin[i]
         for x, (b, a) in new.items():
             PLACE[x] = (b, a)
             users[x] -= 1
@@ -503,7 +556,7 @@ def schedule(ops):
             rdy[k] = max(rdy[k], end[i] + l)
             if cnt[k] == 0:
                 ready.append(k)
-    return order
+    return max(end.values()), order, end, more, PLACE
 
 
 CACHE = {}

@@ -14,12 +14,12 @@ def _decl(text, d, lead):
 
 
 _decl("tli:256 dli:256 thi:1 sci:1024 sti:1024 pidx:1 pmi:1 ai:1 a31:1", i32, [])
-_decl("tm0:256 ts0:256 stw:1024 scw:1040 pmf:1 iq:16 P1:16 Pd:8 on32:128 boa:128 bo32:128 id32:128 "
+_decl("tm0:256 ts0:256 stw:1024 scw:1040 pmf:1 iq:16 P1:16 PLf:16 on32:128 boa:128 bo32:128 id32:128 "
       "q0:1 thn:1 nlim:8 asum:16 T1s:256 od:256 ot:256 oz:256 cst:10", f32, [])
 _decl("PV:16", f16, [])
-_decl("clkw:4112 bc:2048 bd:1024 dd:2048 rst:1024 rowc:256 Zs:144 KB:16 eqP:256 zl:256", b16, [])
+_decl("clkw:4112 bc:2048 sk8:2,1024 dd:2048 rst:1024 rowc:256 Zs:144 KB:16 eqP:256 eqS:256 zl:256", b16, [])
 _decl("PLu:32", u16, [])
-_decl("Tq:512 D1:128 cw:128 sw:128 hf:128 dst:128 Tm:128 zy:256", f16, [2])
+_decl("Tq:128 PS:256 T1:128 D1:128 cw:128 sw:128 hf:128 dst:128 Tm:128 zy:256", f16, [2])
 _decl("eqA:2048 eqB:2048 fC:2048 Y:2048 MN:2048 XG:2048 xs:2048 nk:128 oh:128 cmA:128 cmB:128 rC:256 FC:128 NG:128 NA:128 "
       "KTn:128 ysb:128 acr:128", b16, [2])
 _decl("sk:128 sk2:128 AS:8 sel:8 npr:8 C1:128 C1t:128", f32, [2])
@@ -35,12 +35,12 @@ for _i in range(8):
     SCRATCH["ps%d" % _i] = ("psum", [128, 512], f32)
 BANKS = {"v": (0, 1), "s": (2, 3), "z": (4,), "m": (5, 6, 7)}
 LOADS = ("tl", "dl", "z", "th", "clk", "st", "sc")
-OPT = dict(xs="S", dst="S", sw="S", cw="V", hf="V", delta=0)
-SEMAPHORES = ["sv", "ss", "sp", "sg", "so", "ls"] + ["l_" + n for n in LOADS]
+OPT = dict(xs="S", dst="S", sw="S", cw="V", hf="V", ps="VV", t1="", dscan=0, ny=2, nx=4, cd=(5, 9, 13), cc=(8, 12), ck=(18, 30))
+SEMAPHORES = ["sv", "ss", "sp", "sg", "so", "ls", "tp0", "tp1"] + ["l_" + n for n in LOADS]
 SEMAPHORES += ["a%d%d%s" % (t, h, k) for t in range(1, NV) for h in (0, 1) for k in "dtz"]
 CYC, PEC, OVV, OVS, WAKE, SELF, REMOTE, LOOK = 0.83, 0.43, 30.0, 40.0, 90.0, 90.0, 3500.0, 0.5
 ROUNDS, LOOKB = 6, 0.1
-LEAD = {"A0": 4000.0, "B0": 4000.0, "C0": 4000.0}
+LEAD = {"A0": 3000.0, "B0": 3000.0, "C0": 3000.0}
 TEMP, PLACE = {}, {}
 
 
@@ -65,7 +65,11 @@ def get(T, x):
         bank, b0 = PLACE[x[0]]
         a, b, st = (x[1][0] if x[1] else slice(None)).indices(128 * TEMP[x[0]][1])
         return T["ps%d" % bank][:, 128 * b0 + a:128 * b0 + b:st]
-    return T[x[0]][(slice(None),) + x[1] + (slice(None),) * (len(SCRATCH[x[0]][1]) - 1 - len(x[1]))]
+    return T[x[0]][(x[2:] or (slice(None),)) + x[1] + (slice(None),) * (len(SCRATCH[x[0]][1]) - 1 - len(x[1]))]
+
+
+def half(x, i):
+    return x + (blk(i, 64),)
 
 
 def span(x):
@@ -148,14 +152,18 @@ def program(nrem):
             return g.vector.tensor_copy(get(T, o), x) if shift is None else g.vector.tensor_scalar(get(T, o), x, shift, None, A.add)
         add(e, 60 + 1.56 * size(o) * CYC, fn, [win, off], [o])
 
-    def mm(lst):
+    def mm(lst, *cuts):
+        if cuts:
+            mm(lst[:cuts[0]])
+            return mm(lst[cuts[0]:], *[c - cuts[0] for c in cuts[1:]])
+
         def fn(g, T):
             x = None
             for o, l, r, a, b in lst:
                 x = g.tensor.matmul(get(T, o), get(T, l), get(T, r), a, b)
             return x
         d = sum(4 + max(64, size(m[0])) * PEC * (4 if SCRATCH[m[1][0]][2] == f32 else 1) for m in lst)
-        add("P", 30 + d, fn, [m[1] for m in lst] + [m[2] for m in lst], [m[0] for m in lst])
+        add("P", 30 + d, fn, [m[1] for m in lst] + [m[2] for m in lst], [m[0] for m in lst], open=not lst[-1][4])
 
     def chain(o, *pairs):
         return [(o, l, r, i == 0, i == len(pairs) - 1) for i, (l, r) in enumerate(pairs)]
@@ -212,10 +220,11 @@ def program(nrem):
     aff(R("rst"), R("rst"), [[0, 64], [1, 16]], A.is_equal, 0, 0, 1.0)
     aff(R("dd"), R("bc"), [[1, 16], [0, 8], [-1, 16]], A.is_gt, 0, 0)
     aff(R("dd"), R("dd"), [[0, 16], [-1, 128]], A.not_equal, 0, 1, -1.0)
-    if OPT["delta"]:
-        tt(R("Pd"), R("P1", S_(8, 16)), R("P1", S_(0, 8)), A.subtract)
-        for j in range(8):
-            ts(R("bd", blk(j)), R("BO"), R("Pd", S_(j, j + 1)), A.mult)
+    for i in (0, 1):
+        aff(R("sk8", i, blk(0)), R("rowc", blk(1)), [[-16, 4], [0, 2], [-1, 16]], A.not_equal, 64 * i - 64, 1, -1.0)
+        for n in (128, 256, 512):
+            aff(R("sk8", i, S_(n, 2 * n)), R("sk8", i, S_(0, n)), [[0, n]], A.is_ge, 0, 0)
+        aff(R("sk8", i), R("sk8", i), [[-1, 8], [-8, 8], [0, 16]], A.not_equal, -64 * i, 1, 1.0)
     CST = (2048.0, 4322.0, -1015.5, -64.0, -1024.0, -2047.5, 0.0156263, 1023.75, 1024.0)
     for i, x in enumerate(CST):
         if OPT["hf"] == "S" or i < 7:
@@ -264,12 +273,13 @@ def program(nrem):
         arrive(t, h, "t", R("tt", k))
         arrive(t, h, "d", D)
         arrive(t, h, "z", Z)
-        for hb in (0, 1):
-            gat("S", R("Y", h, blk(hb, 1024)), WIN, R("tt", k, blk(hb, 64)))
+        n = OPT["ny"]
+        for hb in range(n):
+            gat("S", R("Y", h, blk(hb, 2048 // n)), WIN, R("tt", k, blk(hb, 128 // n)))
         ts(Tn, R("tt", k), -2063.0, A.add)
         spread("Dq", k)
-        if OPT["delta"]:
-            spread("Tq", h)
+        add("Y", 120, lambda g, T: [g.sync.dma_start(get(T, half(R("PS", h, blk(i)), 1 - i)), get(T, half(Tn, i))) for i in (0, 1)],
+            [Tn], [R("PS", h)], tok="tp%d" % h, lat=2200)
         b = tmp("z", 4)
         mm([(R(b, S_(i, 512, 4)), I, Z, True, True) for i in range(4)])
         for hb in (0, 1):
@@ -278,15 +288,17 @@ def program(nrem):
                 tt(R("MN", h, c), R("Y", h, c), R(b, blk(hb, 256)), A.min)
         member(Tn, R("Dq", k), "eqA", h)
         pD = R(tmp("m", 1))
-        mm(chain(pD, (I, D), *[(I4160n, R("eqA", h, blk(j))) for j in range(16)]))
+        mm(chain(pD, (I, D), *[(I4160n, R("eqA", h, blk(j))) for j in range(16)]), *OPT["cd"])
         ts(R("D1", h), pD, -2112.0, A.max)
         ts(R("D1u", h), R("D1", h), -2048.0, A.max, 2063.0, A.add)
         ts(R("nk", h), R("D1", h), -2047.5, A.is_le, -0.5, A.add)
         b = tmp("m", 1)
-        mm([(R(b, S_(j, 128, 16)), R("eqA", h, blk(j)), BO8, True, True) for j in range(16)])
+        mm([(R(b, S_(j, 128, 16)), R("eqA", h, blk(j)), BO8, True, True) for j in range(16)], *OPT["cc"])
         act(R("cmA", h), R(b), F.Sign)
+        n = OPT["nx"]
+        for hb in range(n):
+            gat("S", R("XG", h, blk(hb, 2048 // n)), WIN, R("D1u", h, blk(hb, 128 // n)))
         for hb in (0, 1):
-            gat("S", R("XG", h, blk(hb, 1024)), WIN, R("D1u", h, blk(hb, 64)))
             scan(R("xs", h, blk(hb, 1024)), R("rst"), R("XG", h, blk(hb, 1024)))
 
     def stageB(t, h):
@@ -296,7 +308,7 @@ def program(nrem):
         kk, d = R(b, blk(0)), R(b, blk(1))
         mm([(R(b), I, R("rowc"), True, False), (d, Z, BO, False, False)] +
            [(R(b, S_(128 + j, 256, 16)), R("Y", h, S_(j, 2048, 16)), BO8, False, False) for j in range(16)] +
-           [(R(b, S_(j, 256, 16)), R("MN", h, S_(j, 2048, 16)), R("KB"), False, j == 15) for j in range(16)])
+           [(R(b, S_(j, 256, 16)), R("MN", h, S_(j, 2048, 16)), R("KB"), False, j == 15) for q in range(4) for j in range(q, 16, 4)], *OPT["ck"])
         scan(R("sk", h), rs, kk)
         scan(R("sk2", h, S_(None, None, -1)), rs, R("sk", h, S_(None, None, -1)))
         tt(oh, R("sk2", h), kk, A.is_equal)
@@ -332,6 +344,8 @@ def program(nrem):
         mm(chain(p, (I, Tn), (R("cmA", h), I4160n), (oh, I4160n)))
         act(R("KTn", h), p, F.Sign, bias=cst(-2047.5), scale=-1.0)
         act(R("T1s", blk(h)), p, F.Relu, bias=cst(2048.0))
+        if OPT["t1"]:
+            shift(OPT["t1"], R("T1", h), p, 0.0)
         if t + 1 < NV:
             c = R(tmp("m", 1))
             mm(chain(c, (In, R("D1", h)), (R("BO128n"), FC)))
@@ -349,22 +363,21 @@ def program(nrem):
     def stageC(t, h):
         k, last = 2 * t + h, t == NV - 1
         NG, Tn, Z = R("NG", h), R("Tq", h, blk(0)), R("Q", k, blk(2))
-        bs = [tmp("s", 4) for _ in range(2 if OPT["delta"] else 4)]
+        for i in (0, 1):
+            shift(OPT["ps"][i], half(R("PS", h, blk(i)), i), half(R("sw", h), i), 0.0)
         for q in range(4):
-            b = bs[q % len(bs)]
-            if not OPT["delta"]:
-                mm(sum([chain(R(b, blk(i)), (R("bc", blk(4 * q + i)), R("sw", h)), (In, Tn)) for i in range(4)], []))
-            elif q < 2:
-                mm([(R(b), In, R("Tq", h), True, False)] + [(R(b, blk(i)), R("bc", blk(4 * q + i)), R("sw", h), False, False) for i in range(4)])
-            else:
-                mm([(R(b, blk(i)), R("bd", blk(4 * q + i - 8)), R("sw", h), False, i == 3) for i in range(4)])
+            b = tmp("s", 4)
+            mm([(R(b, blk(i)), R("sk8", q // 2, blk(4 * (q % 2) + i)), R("PS", h, blk(q // 2)), True, True) for i in range(4)])
             act(R("fC", h, blk(q, 512)), R(b), F.Tanh, bias=cst(0.0156263), scale=16.0)
         b = tmp("m", 1)
-        mm([(R(b, S_(j, 128, 16)), R("fC", h, blk(j)), BO8, True, True) for j in range(16)])
+        mm([(R(b, S_(64 * (j // 8) + j % 8, 64 * (j // 8) + 64, 8)), R("fC", h, blk(j)), BO8, True, True) for j in range(16)], *OPT["cc"])
         act(R("rC", h, blk(0)), R(b), F.Copy, bias=-192.49, scale=-1.0)
         act(R("rC", h, blk(1)), R(b), F.Copy, bias=192.0)
         p0, p1 = R(tmp("m", 1)), R(tmp("m", 1))
-        mm(chain(p1, (I, Tn), (R("cmA", h), I4160n), (R("oh", h), I4160n), (I4160n, NG)))
+        if OPT["t1"]:
+            mm(chain(p1, (I, R("T1", h)), (I4160n, NG)))
+        else:
+            mm(chain(p1, (I, Tn), (R("cmA", h), I4160n), (R("oh", h), I4160n), (I4160n, NG)))
         mm(chain(p0, (I17, NG), (R("I16"), R("KTn", h)), (R("rC", h, blk(0)), I17), (R("rC", h, blk(1)), I17)))
         tt(R("C1t", h), R("sw", h), p0, A.min)
         tt(R("Tm", h), R("C1t", h), p1, A.max)
@@ -376,7 +389,7 @@ def program(nrem):
             send(t, h, "t", "stt", R("tt", k + 2))
         member(R("cw", h), R("Dq", k), "eqB", h)
         b = tmp("m", 1)
-        mm([(R(b, S_(j, 128, 16)), R("eqB", h, blk(j)), BO8, True, True) for j in range(16)])
+        mm([(R(b, S_(j, 128, 16)), R("eqB", h, blk(j)), BO8, True, True) for j in range(16)], *OPT["cc"])
         act(R("cmB", h), R(b), F.Sign, scale=-1.0)
         p0, p1 = R(tmp("m", 1)), R(tmp("m", 1))
         mm(chain(p1, (I, R("D1", h)), (I4160n, NG)))
@@ -408,9 +421,15 @@ def program(nrem):
     def stageD(t):
         b, PV = tmp("m", 2), R("PV")
         mm([(R(b, S_(r, 256, 16)), R("dd", blk(r)), PV, True, True) for r in range(16)])
-        ts(R("eqP"), R(b), 0.0, A.is_equal)
-        c = R(tmp("m", 1), S_(0, 16))
-        mm(chain(c, (I, PV), *[(R("I4096"), R("eqP", S_(r, 256, 16))) for r in range(16)]))
+        if OPT["dscan"]:
+            ts(R("eqP"), R(b), 0.0, A.is_equal, 4096.0, A.mult)
+            scan(R("eqS"), R("rst", S_(0, 256)), R("eqP"))
+            c = R("PLf")
+            tt(c, R("eqS", S_(15, 256, 16)), PV, A.add)
+        else:
+            ts(R("eqP"), R(b), 0.0, A.is_equal)
+            c = R(tmp("m", 1), S_(0, 16))
+            mm(chain(c, (I, PV), *[(R("I4096"), R("eqP", S_(r, 256, 16))) for r in range(16)]))
         ts(R("PLu", S_(0, 32, 2)), c, 1056.0, A.add, R("q0"), A.min)
         for c in range(16):
             o, off, src = R("scw"), R("PLu", S_(2 * c, 2 * c + 1)), R("T1s", blk(c, 16))
@@ -431,20 +450,20 @@ def program(nrem):
 def depend(ops):
     hist = {}
     for i, o in enumerate(ops):
-        pw, acc = set(), {}
+        pw, seq, acc = set(), set(), {}
         for x, wr in [(x, False) for x in o["r"]] + [(x, True) for x in o["w"]]:
             sp = tuple(s[:3] for s in span(x))
             acc[(x[0], sp)] = acc.get((x[0], sp), False) or wr
         for (name, sp), wr in acc.items():
             for j, sj, wj in hist.get(name, ()):
                 if j != i and (wj or wr) and meet(sp, sj):
-                    pw.add(j)
+                    (seq if name in TEMP and o["e"] == ops[j]["e"] == "P" else pw).add(j)
         for (name, sp), wr in acc.items():
             h = hist.setdefault(name, [])
             if wr:
                 h[:] = [y for y in h if y[0] == i or not cover(sp, y[1])]
             h.append((i, sp, wr))
-        o["pw"] = pw
+        o["pw"], o["seq"] = pw, seq
         o["t"] = sorted({x[0] for x in o["r"] + o["w"] if psum(x)})
 
 
@@ -452,7 +471,8 @@ def schedule(ops):
     n = len(ops)
     pred, succ = [], [[] for _ in range(n)]
     for i, o in enumerate(ops):
-        pred.append([(j, WAKE if ops[j]["e"] != o["e"] else SELF) for j in o["pw"]] + ([(o["after"], REMOTE)] if "after" in o else []))
+        pred.append([(j, WAKE if ops[j]["e"] != o["e"] else SELF) for j in o["pw"]] + [(j, 0.0) for j in o["seq"]] +
+                    ([(o["after"], REMOTE)] if "after" in o else []))
         for j, l in pred[i]:
             succ[j].append((i, l))
     fin = [o["d"] + o.get("lat", 0.0) for o in ops]
@@ -505,6 +525,7 @@ def forward(ops, pred, succ, fin, pri):
             users[x] = users.get(x, 0) + 1
     rdy, free, order, end = [0.0] * n, {}, [], {}
     last = [{} for _ in range(8)]
+    lock = [None] * 8
     held = [[None] * 4 for _ in range(8)]
     past = [[{} for _ in range(4)] for _ in range(8)]
 
@@ -519,6 +540,8 @@ def forward(ops, pred, succ, fin, pri):
                 opts = [(b, a) for b in BANKS[role] for a in range(0, 5 - m) if all(held[b][c] is None for c in range(a, a + m))]
             best = None
             for b, a in opts:
+                if o["e"] == "P" and lock[b] not in (None, x):
+                    continue
                 w = {j for e, j in last[b].items() if e != o["e"]}
                 if x not in PLACE:
                     w |= {j for c in range(a, a + TEMP[x][1]) for j in past[b][c].values()}
@@ -545,6 +568,8 @@ def forward(ops, pred, succ, fin, pri):
             PLACE[x] = (b, a)
             users[x] -= 1
             last[b][o["e"]] = i
+            if o["e"] == "P":
+                lock[b] = x if o["open"] else None
             for c in range(a, a + TEMP[x][1]):
                 held[b][c] = x if users[x] else None
                 past[b][c][o["e"]] = i
@@ -600,8 +625,9 @@ def rank_program(g, core, T, topo):
             total["ls"] += nrem
             continue
         s, n = (o["tok"], 16) if "tok" in o else (sem[e], 1)
-        total[s] = total.get(s, 0) + n
-        x.then_inc(T.sem[s], n)
+        for y in x if isinstance(x, list) else [x]:
+            total[s] = total.get(s, 0) + n
+            y.then_inc(T.sem[s], n)
         tok[i], vc[i] = (s, total[s]), dict(kn)
     for s in total:
         if total[s]:

@@ -13,34 +13,32 @@ def _decl(text, d, lead):
         SCRATCH[n] = ("sbuf", [128] + lead + [int(x) for x in s.split(",")], d)
 
 
-_decl("tli:256 dli:256 thi:1 sci:1024 sti:1024 pidx:1 pmi:1 ai:1 a31:1", i32, [])
-_decl("tm0:256 ts0:256 stw:1024 scw:1040 pmf:1 iq:16 P1:16 PLf:16 on32:128 boa:128 bo32:128 id32:128 "
-      "q0:1 thn:1 nlim:8 asum:16 T1s:256 od:256 ot:256 oz:256 cst:10", f32, [])
-_decl("PV:16", f16, [])
-_decl("clkw:4112 bc:2048 sk8:2,1024 dd:2048 rst:1024 rowc:256 Zs:144 KB:16 eqP:256 eqS:256 zl:256", b16, [])
-_decl("PLu:32", u16, [])
-_decl("Tq:128 PS:256 T1:128 D1:128 cw:128 sw:128 hf:128 dst:128 Tm:128 zy:256", f16, [2])
-_decl("eqA:2048 eqB:2048 fC:2048 Y:2048 MN:2048 XG:2048 xs:2048 nk:128 oh:128 cmA:128 cmB:128 rC:256 FC:128 NG:128 NA:128 "
-      "KTn:128 ysb:128 acr:128", b16, [2])
-_decl("sk:128 sk2:128 AS:8 sel:8 npr:8 C1:128 C1t:128", f32, [2])
-_decl("nu:16 nv:16", i32, [2])
-_decl("D1u:128 nlu:8 wu:8", u16, [2])
-_decl("tt:128 stt:128", u16, [2 * NV])
-_decl("Dq:512 Q:384 sd:128 sz:128", f16, [2 * NV])
-_l = "I In I4160n I17 I16 Ih I64 I4096 BO BO128n".split()
+_decl("tli:256 dli:256 thi:1 sci:1024 sti:1024 pidx:1 pmi:1 ai:1 a31:1 nu:32 nv:32", i32, [])
+_decl("tm0:256 ts0:256 stw:1024 scw:1040 pmf:1 iq:16 P1:16 on32:128 boa:128 bo32:128 id32:128 io:256 turn:1 pf:8 "
+      "q0:1 thn:1 nlim:8 asum:16 T1s:256 od:256 ot:256 oz:256 cst:12 sk:256 sk2:256 AS:16 sel:16 npr:16 C1:256 C1t:256", f32, [])
+_decl("LC:48 PV:16 PS:512 D1:256 cw:256 sw:256 hf:256 dst:256 zy:512 Ds:2,1024", f16, [])
+_decl("clkw:4112 bc:2048 sk8:2,1024 dd:2048 rst:1024 rowc:1024 Zs:144 KB:3,32 eqP:256 zl:256 "
+      "eqA:4096 eqB:4096 fC:4096 Y:4096 MN:4096 XG:4096 xs:4096 nk:256 oh:256 cmA:256 cmB:256 rC:512 FC:256 NG:256 NA:256 "
+      "KTn:256 ysb:256 acr:256 cmD:256 eqn:256 one:256 sp:8,128 Wd:32 Wt:32", b16, [])
+_decl("PLu:32 D1u:256 nlu:16 wu:16", u16, [])
+_decl("tt:256 stt:256", u16, [NV])
+_decl("Df:256 Tf:256 Can:512 Q:768 sd:256 sT:256 sC:512 sz:256", f16, [NV])
+_l = "I In I4160n I17 I16 Ih I64 I64n I4096 I4096n I8192 I2080n I69n BO BO128n".split()
 SCRATCH["kb"] = ("sbuf", [128, len(_l), 128], b16)
 for _i, _n in enumerate(_l):
     ALIAS[_n] = ("kb", _i)
 for _i in range(8):
     SCRATCH["ps%d" % _i] = ("psum", [128, 512], f32)
-BANKS = {"v": (0, 1), "s": (2, 3), "z": (4,), "m": (5, 6, 7)}
+BANKS = {"v": tuple(range(8)), "s": tuple(range(8)), "z": tuple(range(8)), "m": tuple(range(7, -1, -1))}
 LOADS = ("tl", "dl", "z", "th", "clk", "st", "sc")
-OPT = dict(xs="S", dst="S", sw="S", cw="V", hf="V", ps="VV", t1="", dscan=0, ny=2, nx=4, cd=(5, 9, 13), cc=(8, 12), ck=(18, 30))
-SEMAPHORES = ["sv", "ss", "sp", "sg", "so", "ls", "tp0", "tp1"] + ["l_" + n for n in LOADS]
-SEMAPHORES += ["a%d%d%s" % (t, h, k) for t in range(1, NV) for h in (0, 1) for k in "dtz"]
-CYC, PEC, OVV, OVS, WAKE, SELF, REMOTE, LOOK = 0.83, 0.43, 30.0, 40.0, 90.0, 90.0, 3500.0, 0.5
-ROUNDS, LOOKB = 6, 0.1
-LEAD = {"A0": 3000.0, "B0": 3000.0, "C0": 3000.0}
+OPT = dict(xs="S", dst="S", sw="S", cw="V", ys="S", hf="S", ps="GG", ny=8, nm=4, nx=8, cc=8, ck=8, mk=1, ww=0, join=0, d0="S", xv=(0,), yv=(),
+           spec=1, ds="Y", dup=1, ce=8, pA=1, pD=1, pT=1, pK=1, pB=1, pC=1, pZ=1)
+SEMAPHORES = ["sv", "ss", "sp", "sg", "so", "ls", "tp0", "tp1", "d00", "d01", "d10", "d11", "tq00", "tq01", "tq10", "tq11"] + ["l_" + n for n in LOADS]
+SEMAPHORES += ["a%d%d%s" % (t, h, k) for t in range(1, NV) for h in (0, 1) for k in "dtfzce"]
+CYC, PEC, OVV, OVS, WAKE, SELF, REMOTE, LOOK = 0.83, 0.43, 30.0, 40.0, 90.0, 90.0, 3500.0, 0.3
+GAT, SCA, PEM = 1.56, 3.8, 4.0
+ROUNDS, LOOKB = 2, 0.1
+PLAN = {'P': 21.7, 'mu': 1.5, 'SYA': (6.6, 6.2), 'SXGA': (12.6, 6.0), 'SfCC': (23.0, 3.9), 'VeqAA': (8.6, 3.3), 'VMNA': (10.2, 5.0), 'VeqBC': (24.8, 3.3), 'VscwD': (29.2, -0.3), 'VwuB': (22.4, -1), 'VsttC': (24.2, -0.5), 'VsdC': (29.7, 0), 'VsTC': (29.5, -2), 'SszC': (27.0, 0), 'VxsA': (19.0, 5), 'VD1uA': (15.7, -2.5), 'P~kbD': (25.8, 1.0), 'VohB': (16.3, 2.0), 'P~eqBC': (28.7, 3.3), 'VQB': (20.4, 1.0), 'VeqnC': (21.0, 1.0), 'P~kbA': (9.7, 2.0), 'P~dstB': (15.3, 0.5), 'P~fCC': (25.3, 1.2)}
 TEMP, PLACE = {}, {}
 
 
@@ -62,7 +60,7 @@ def psum(x):
 
 def get(T, x):
     if psum(x):
-        bank, b0 = PLACE[x[0]]
+        bank, b0 = PLACE[x[0]][:2]
         a, b, st = (x[1][0] if x[1] else slice(None)).indices(128 * TEMP[x[0]][1])
         return T["ps%d" % bank][:, 128 * b0 + a:128 * b0 + b:st]
     return T[x[0]][(x[2:] or (slice(None),)) + x[1] + (slice(None),) * (len(SCRATCH[x[0]][1]) - 1 - len(x[1]))]
@@ -103,7 +101,16 @@ def two(*xs):
     return all(not psum(x) and SCRATCH[x[0]][2] in (f16, b16, u16) for x in xs)
 
 
-def program(nrem):
+def parts(name):
+    n = OPT[name]
+    return [(h, 3 - n, blk(h, 256 // n), blk(h, 16 // n)) for h in range(n)]
+
+
+def off(c, x):
+    return slice(c.start + x, c.stop + x)
+
+
+def program():
     ops, lab = [], [""]
 
     def tmp(role, n):
@@ -111,8 +118,12 @@ def program(nrem):
         TEMP[name] = (role, n)
         return name
 
-    def add(e, dur, fn, r, w, **kw):
-        ops.append(dict(kw, g=lab[0], e=e, d=dur, fn=fn, r=[x for x in r if isinstance(x, tuple)], w=w))
+    def add(e, c, fn, r, w, **kw):
+        c = c + (0,) * (6 - len(c))
+        d = c[0] + CYC * (c[1] + GAT * c[2] + SCA * c[3]) + PEM * c[4] + PEC * c[5]
+        r = [x for x in r if isinstance(x, tuple)]
+        name = "" if not w else "~" + r[0][0] if psum(w[0]) else w[0][0]
+        ops.append(dict(kw, g=lab[0], n=e + name + lab[0][:1], e=e, c=c, d=d, fn=fn, r=r, w=w))
         return len(ops) - 1
 
     def val(T, x):
@@ -122,37 +133,38 @@ def program(nrem):
         def fn(g, T):
             a = (get(T, o), get(T, i), val(T, s1), val(T, s2), op0)
             return g.vector.tensor_scalar(*(a if op1 is None else a + (op1,)))
-        add("V", OVV + max(64, size(o) * (0.5 if two(o, i) else 1)) * CYC, fn, [i, s1, s2], [o])
+        add("V", (OVV, max(64, size(o) * (0.5 if two(o, i) else 1))), fn, [i, s1, s2], [o])
 
     def tt(o, a, b, op):
-        add("V", OVV + max(64, size(o) * (1 if psum(a) or psum(b) else 2)) * CYC,
+        add("V", (OVV, max(64, size(o) * (1 if psum(a) or psum(b) else 2))),
             lambda g, T: g.vector.tensor_tensor(get(T, o), get(T, a), get(T, b), op), [a, b], [o])
 
     def cp(o, i):
-        add("V", OVV + max(64, size(o) * (0.5 if two(o, i) else 1)) * CYC, lambda g, T: g.vector.tensor_copy(get(T, o), get(T, i)), [i], [o])
+        add("V", (OVV, max(64, size(o) * (0.5 if two(o, i) else 1))), lambda g, T: g.vector.tensor_copy(get(T, o), get(T, i)), [i], [o])
 
     def fill(o, v):
-        add("V", OVV + max(64, size(o) * (0.5 if two(o) else 1)) * CYC, lambda g, T: g.vector.memset(get(T, o), v), [], [o])
+        add("V", (OVV, max(64, size(o) * (0.5 if two(o) else 1))), lambda g, T: g.vector.memset(get(T, o), v), [], [o])
 
     def scan(o, a, b, op0=A.mult):
-        add("V", OVV + max(64, size(o) * (0.5 if two(o, a, b) else 1)) * CYC,
+        add("V", (OVV, max(64, size(o) * (0.5 if two(o, a, b) else 1))),
             lambda g, T: g.vector.tensor_tensor_scan(get(T, o), get(T, a), get(T, b), 0.0, op0, A.max), [a, b], [o])
 
     def act(o, i, func, bias=0.0, scale=1.0, acc=None):
         def fn(g, T):
             kw = {} if acc is None else {"accum_out": get(T, acc)}
             return g.scalar.activation(get(T, o), get(T, i), func, bias=val(T, bias), scale=scale, **kw)
-        add("S", OVS + max(64, size(o)) * CYC, fn, [i, bias], [o] + ([] if acc is None else [acc]))
+        add("S", (OVS, max(64, size(o))), fn, [i, bias], [o] + ([] if acc is None else [acc]))
 
-    def gat(e, o, win, off, shift=None):
+    def gat(e, o, win, offs, shift=None):
         def fn(g, T):
-            x = get(T, win).indirect(get(T, off))
+            x = get(T, win).indirect(get(T, offs))
             if e == "S":
                 return g.scalar.activation(get(T, o), x, F.Copy, bias=shift or 0.0)
             return g.vector.tensor_copy(get(T, o), x) if shift is None else g.vector.tensor_scalar(get(T, o), x, shift, None, A.add)
-        add(e, 60 + 1.56 * size(o) * CYC, fn, [win, off], [o])
+        add(e, (60, 0, size(o)), fn, [win, offs], [o])
 
     def mm(lst, *cuts):
+        cuts = [c for c in cuts if 0 < c < len(lst)]
         if cuts:
             mm(lst[:cuts[0]])
             return mm(lst[cuts[0]:], *[c - cuts[0] for c in cuts[1:]])
@@ -162,14 +174,20 @@ def program(nrem):
             for o, l, r, a, b in lst:
                 x = g.tensor.matmul(get(T, o), get(T, l), get(T, r), a, b)
             return x
-        d = sum(4 + max(64, size(m[0])) * PEC * (4 if SCRATCH[m[1][0]][2] == f32 else 1) for m in lst)
-        add("P", 30 + d, fn, [m[1] for m in lst] + [m[2] for m in lst], [m[0] for m in lst], open=not lst[-1][4])
+        d = sum(max(64, size(m[0])) * (4 if SCRATCH[m[1][0]][2] == f32 else 1) for m in lst)
+        add("P", (30, 0, 0, 0, len(lst), d), fn, [m[1] for m in lst] + [m[2] for m in lst], [m[0] for m in lst], open=not lst[-1][4])
 
-    def chain(o, *pairs):
-        return [(o, l, r, i == 0, i == len(pairs) - 1) for i, (l, r) in enumerate(pairs)]
+    def group(lst, *cuts):
+        mm([m + (i == 0, i == len(lst) - 1) for i, m in enumerate(lst)], *cuts)
+
+    def chain(b, *terms):
+        return [(R(b, *m[2:]), m[0], m[1], i == 0, i == len(terms) - 1) for i, m in enumerate(terms)]
+
+    def turned(buf, k, h0, n, x=0):
+        return [(R(buf, blk(x + h0 + i)), k, blk(i)) for i in range(n)]
 
     def load(q, name, o, src, dur):
-        add(q, 60, lambda g, T: (g.sync if q == "Y" else g.scalar).dma_start(get(T, o), src(T)), [], [o], tok="l_" + name, lat=dur)
+        add(q, (60,), lambda g, T: (g.sync if q == "Y" else g.scalar).dma_start(get(T, o), src(T)), [], [o], tok="l_" + name, lat=dur)
     load("S", "clk", R("clkw", S_(16, 4112)), lambda T: T.clk[:, :], 5000)
     load("Y", "tl", R("tli"), lambda T: T.tl[:, :], 2200)
     load("Y", "dl", R("dli"), lambda T: T.dl[:, :], 2500)
@@ -180,14 +198,11 @@ def program(nrem):
 
     def iota(o, pat, base, cm=0):
         kw = {} if SCRATCH[o[0]][2] == i32 else {"allow_small_or_imprecise_dtypes": True}
-        add("G", 130 + 2 * CYC * size(o), lambda g, T: g.iota(get(T, o), pat, base, cm, **kw), [], [o])
+        add("G", (130, 2 * size(o)), lambda g, T: g.iota(get(T, o), pat, base, cm, **kw), [R("turn")], [o])
 
     def aff(o, i, pat, op, base, cm, other=0.0):
-        add("G", 170 + 2 * CYC * size(o), lambda g, T: g.affine_select(get(T, o), get(T, i), pat, op, other, base, cm), [i], [o])
-
-    def spread(x, k):
-        for n in (128, 256):
-            aff(R(x, k, S_(n, 2 * n)), R(x, k, S_(0, n)), [[0, n]], A.is_ge, 0, 0)
+        alone = [R("turn")] * (len(o) > 2 and o[2].start > 0)
+        add("G", (170, 2 * size(o)), lambda g, T: g.affine_select(get(T, o), get(T, i), pat, op, other, base, cm), [i, R("turn")], [o] + alone)
 
     def shift(e, o, i, x):
         return act(o, i, F.Copy, bias=x) if e == "S" else ts(o, i, x, A.add)
@@ -197,8 +212,9 @@ def program(nrem):
     aff(R("bo32"), R("boa"), [[16, 8], [0, 16]], A.is_ge, 15, -1)
     aff(R("id32"), R("on32"), [[-1, 128]], A.is_equal, 0, 1)
     iota(R("iq"), [[1, 16]], 0)
-    fill(R("rowc", blk(1)), 0.0)
-    iota(R("rowc", blk(0)), [[0, 8], [-1, 16]], 16)
+    kn = 3 - OPT["pK"]
+    fill(R("rowc", S_(128 * kn, 1024)), 0.0)
+    iota(R("rowc", S_(0, 128 * kn)), [[0, 8 * kn], [-1, 16]], 16)
     ts(R("pmi"), R("pidx"), 15, A.bitwise_and)
     cp(R("pmf"), R("pmi"))
     pm = R("pmf", S_(0, 1))
@@ -209,11 +225,17 @@ def program(nrem):
         ts(R("bc", blk(j)), R("BO"), R("P1", S_(j, j + 1)), A.mult)
     fill(R("clkw", S_(0, 16)), -1.0)
     for n, src, k in (("In", "id32", -1), ("I4160n", "id32", -4160), ("I17", "id32", 131072), ("I16", "id32", 65536), ("Ih", "id32", 0.5),
-                      ("I64", "id32", 64), ("I4096", "id32", 4096), ("BO128n", "bo32", -128)):
+                      ("I64", "id32", 64), ("I64n", "id32", -64), ("I4096", "id32", 4096), ("I4096n", "id32", -4096), ("I8192", "id32", 8192),
+                      ("I2080n", "id32", -2080), ("I69n", "id32", -69632), ("BO128n", "bo32", -128)):
         act(R(n), R(src), F.Copy, scale=float(k))
     BO8 = R("BO", S_(0, 128, 16))
-    ts(R("KB", S_(0, 8)), BO8, 16.0, A.mult)
-    ts(R("KB", S_(8, 16)), BO8, -2.0, A.mult)
+    if kn == 2:
+        fill(R("KB"), 0.0)
+    for i in range(kn):
+        ts(R("KB", i, blk(i, 8)), BO8, 16.0, A.mult)
+        ts(R("KB", i, blk(kn + i, 8)), BO8, -2.0, A.mult)
+    for i, x in enumerate((0.0, 2047.0, 4096.0)):
+        fill(R("LC", blk(i, 16)), x)
     fill(R("Zs"), 0.0)
     cp(R("Zs", S_(15, 143, 16)), BO8)
     iota(R("rst"), [[0, 64], [1, 16]], 0)
@@ -221,26 +243,37 @@ def program(nrem):
     aff(R("dd"), R("bc"), [[1, 16], [0, 8], [-1, 16]], A.is_gt, 0, 0)
     aff(R("dd"), R("dd"), [[0, 16], [-1, 128]], A.not_equal, 0, 1, -1.0)
     for i in (0, 1):
-        aff(R("sk8", i, blk(0)), R("rowc", blk(1)), [[-16, 4], [0, 2], [-1, 16]], A.not_equal, 64 * i - 64, 1, -1.0)
+        aff(R("sk8", i, blk(0)), R("rowc", blk(3)), [[-16, 4], [0, 2], [-1, 16]], A.not_equal, 64 * i - 64, 1, -1.0)
         for n in (128, 256, 512):
             aff(R("sk8", i, S_(n, 2 * n)), R("sk8", i, S_(0, n)), [[0, n]], A.is_ge, 0, 0)
         aff(R("sk8", i), R("sk8", i), [[-1, 8], [-8, 8], [0, 16]], A.not_equal, -64 * i, 1, 1.0)
-    CST = (2048.0, 4322.0, -1015.5, -64.0, -1024.0, -2047.5, 0.0156263, 1023.75, 1024.0)
+    CST = (-32.0, 4322.0, -1015.5, -64.0, -1024.0, 32.5, 0.0156263, -0.5, 1.0, 1023.75, 1024.0)
     for i, x in enumerate(CST):
-        if OPT["hf"] == "S" or i < 7:
+        if OPT["hf"] == "S" or i < 9:
             fill(R("cst", S_(i, i + 1)), x)
 
     def cst(x):
         return R("cst", S_(CST.index(x), CST.index(x) + 1))
     ts(R("q0"), pm, 1024.0, A.add)
-    for h in (0, 1):
-        act(R("Q", h, blk(2)), R("zl", blk(h)), F.Copy)
+    act(R("Q", 0, blk(2, 256)), R("zl"), F.Copy)
+    spec = OPT["spec"]
+    fill(R("one"), 1.0)
+    cp(R("pf", S_(0, 1)), R("pidx"))
+    for x, pat in enumerate(([[4, 4], [16, 8], [0, 4]], [[0, 4], [16, 8], [4, 4]])):
+        iota(R("io", blk(x)), pat, 0)
+        for b in range(4):
+            ts(R("sp", 4 * x + b), R("io", blk(x)), float(b), A.add, R("pf", S_(0, 1)), A.is_equal)
+    aff(R("Wd"), R("one", S_(0, 32)), [[-1, 32]], A.is_equal, 0, 1)
+    for jj in range(1, 4):
+        aff(R("Wd"), R("Wd"), [[-1, 32]], A.not_equal, -32 * jj, 1, 1.0)
+    aff(R("Wt"), R("one", S_(0, 32)), [[-4, 8], [-32, 4]], A.is_ge, 0, 1)
+    aff(R("Wt"), R("Wt"), [[4, 8], [32, 4]], A.is_ge, 3, -1)
     ts(R("tm0"), R("tli"), 0.0, A.min, 2.0, A.mult)
     tt(R("ts0"), R("tli"), R("tm0"), A.add)
-    for h in (0, 1):
-        ts(R("tt", h), R("ts0", blk(h)), 16.0, A.add)
-        ts(R("Dq", h, S_(0, 128)), R("dli", blk(h)), -2047.0, A.add)
-    ts(R("thn"), R("thi"), -1.0, A.mult, -2120.5, A.add)
+    ts(R("tt", 0), R("ts0"), 16.0, A.add)
+    ts(R("Tf", 0), R("tt", 0), -2063.0, A.add)
+    ts(R("Df", 0), R("dli"), -2047.0, A.add)
+    ts(R("thn"), R("thi"), -1.0, A.mult, -40.5, A.add)
     cp(R("nlim", S_(0, 1)), R("thn"))
     for k in range(2):
         c, b = blk(k, 512), tmp("s", 4)
@@ -249,201 +282,295 @@ def program(nrem):
     cp(R("scw", S_(0, 1024)), R("sci"))
 
     WIN = R("clkw")
-    I, In, I17, I4160n, BO = R("I"), R("In"), R("I17"), R("I4160n"), R("BO")
-    sent, lists = {}, {}
+    I, In, I17, I4160n, BO, I2080n = R("I"), R("In"), R("I17"), R("I4160n"), R("BO"), R("I2080n")
+    sent = {}
+
+    def can(buf, t, c, x):
+        return R(buf, t, off(c, 256 * x))
 
     def arrive(t, h, kind, x):
-        if t:
-            add("R", 0, None, [], [x], tok="a%d%d%s" % (t, h, kind), inc=nrem, after=sent[(t - 1, h, kind)])
+        j = sent[(t - 1, h, kind)]
+        add("R", (0,), None, [], [x], tok="a%d%d%s" % (t, h, kind), after=j, xl=ops[j]["xl"])
 
     def send(t, h, kind, src, land):
-        def fn(g, T):
-            return get(T, land), get(T, R(src, 2 * t + h)), "a%d%d%s" % (t + 1, h, kind)
-        sent[(t, h, kind)] = add("G", 100, fn, [R(src, 2 * t + h)], [], n="send")
+        sent[(t, h, kind)] = add("G", (100,), None, [src], [], src=src, land=land, tok="a%d%d%s" % (t + 1, h, kind), xl=2.0 * (size(src) - 128))
 
-    def member(rows, held, eq, h):
-        for q in range(4):
-            b = tmp("v", 4)
-            mm([(R(b, blk(i)), R("bc", blk(4 * q + i)), rows, True, True) for i in range(4)])
-            tt(R(eq, h, blk(q, 512)), held, R(b), A.is_equal)
+    def rows(w, h, j, i=0):
+        return S_(2048 * h * (w == 128) + w * j + 128 * i, 2048 * h * (w == 128) + w * j + 128 * i + 128)
 
-    def stageA(t, h):
-        k = 2 * t + h
-        D, Z, Tn = R("Dq", k, blk(0)), R("Q", k, blk(2)), R("Tq", h, blk(0))
-        arrive(t, h, "t", R("tt", k))
-        arrive(t, h, "d", D)
-        arrive(t, h, "z", Z)
+    def spread(x, src, h, e):
+        w = size(src)
+        o = R("Ds", x, blk(h, 4 * w))
+        if e == "Y":
+            add("Y", (240,), lambda g, T: [g.sync.dma_start(get(T, o + (blk(jj, 32),)), get(T, src)) for jj in range(4)], [src], [o], tok="d%d%d" % (x, h), lat=2400)
+            return
+        for q in range(w // 128):
+            b, r = tmp("v", 4), 512 // w
+            mm([(R(b, blk(i, w)), R("sp", 4 + r * q + i), src, True, True) for i in range(r)])
+            shift(e, R("Ds", x, blk(h * w // 128 + q, 512)), R(b), 0.0)
+
+    def member(src, x, eq, h):
+        w, r = size(src), OPT["dup"]
+        for q in range(w * r // 128):
+            b, nb = tmp("v", 4), 512 // (w * r)
+            mm([(R(b, blk(i, w)), R("sp", nb * q + i // r), src, True, True) for i in range(nb * r)])
+            for i in range(nb):
+                for a in range(0, 4, r):
+                    y = 16 * w * h + w * (4 * (nb * q + i) + a)
+                    tt(R(eq, S_(y, y + r * w)), R("Ds", x, S_(w * (4 * h + a), w * (4 * h + a + r))), R(b, blk(i, r * w)), A.is_equal)
+
+    def stageA(t):
+        if t:
+            for h, n, c, _ in parts("pC"):
+                arrive(t, h, "t", R("tt", t, c))
+                arrive(t, h, "c", R("Can", t) if OPT["join"] else can("Can", t, c, 0))
+                if spec and not OPT["join"]:
+                    arrive(t, h, "e", can("Can", t, c, 1))
+            for h, n, c, _ in parts("pT"):
+                arrive(t, h, "f", R("Tf", t, c))
+            for h, n, c, _ in parts("pD"):
+                arrive(t, h, "d", R("Df", t, c))
+            for h, n, c, _ in parts("pZ"):
+                arrive(t, h, "z", R("Q", t, off(c, 512)))
         n = OPT["ny"]
         for hb in range(n):
-            gat("S", R("Y", h, blk(hb, 2048 // n)), WIN, R("tt", k, blk(hb, 128 // n)))
-        ts(Tn, R("tt", k), -2063.0, A.add)
-        spread("Dq", k)
-        add("Y", 120, lambda g, T: [g.sync.dma_start(get(T, half(R("PS", h, blk(i)), 1 - i)), get(T, half(Tn, i))) for i in (0, 1)],
-            [Tn], [R("PS", h)], tok="tp%d" % h, lat=2200)
-        b = tmp("z", 4)
-        mm([(R(b, S_(i, 512, 4)), I, Z, True, True) for i in range(4)])
-        for hb in (0, 1):
-            for q in range(4):
-                c = S_(1024 * hb + q, 1024 * hb + 1024, 4)
-                tt(R("MN", h, c), R("Y", h, c), R(b, blk(hb, 256)), A.min)
-        member(Tn, R("Dq", k), "eqA", h)
-        pD = R(tmp("m", 1))
-        mm(chain(pD, (I, D), *[(I4160n, R("eqA", h, blk(j))) for j in range(16)]), *OPT["cd"])
-        ts(R("D1", h), pD, -2112.0, A.max)
-        ts(R("D1u", h), R("D1", h), -2048.0, A.max, 2063.0, A.add)
-        ts(R("nk", h), R("D1", h), -2047.5, A.is_le, -0.5, A.add)
-        b = tmp("m", 1)
-        mm([(R(b, S_(j, 128, 16)), R("eqA", h, blk(j)), BO8, True, True) for j in range(16)], *OPT["cc"])
-        act(R("cmA", h), R(b), F.Sign)
+            gat("V" if hb in OPT["yv"] else "S", R("Y", blk(hb, 4096 // n)), WIN, R("tt", t, blk(hb, 256 // n)))
+        for h, n, c, _ in parts("pT"):
+            add("Y", (120,), lambda g, T, c=c: [g.sync.dma_start(get(T, half(R("PS", off(c, 256 * i)), 1 - i)), get(T, half(R("Tf", t, c), i))) for i in (0, 1)],
+                [R("Tf", t, c)], [R("PS", c), R("PS", off(c, 256))], tok="tp%d" % h, lat=2200)
+        for h in (0, 1):
+            b, n = tmp("z", 4), OPT["nm"] // 2
+            mm([(R(b, S_(i, 512, 4)), I, R("Q", t, blk(4 + h)), True, True) for i in range(4)])
+            for hb in range(n):
+                for q in range(4):
+                    c = S_(2048 * h + 2048 // n * hb + q, 2048 * h + 2048 // n * (hb + 1), 4)
+                    tt(R("MN", c), R("Y", c), R(b, blk(hb, 512 // n)), A.min)
+        early = spec and t
+        for h, n, c, _ in parts("pD"):
+            spread(1, R("Df", t, c), h, "Y" if t else OPT["d0"])
+        for h, n, c, _ in parts("pA"):
+            w = 128 * n
+            if early:
+                spread(0, can("Can", t, c, 1), h, OPT["ds"])
+            member(can("Can", t, c, 0) if early else R("Tf", t, c), 0 if early else 1, "eqA", h)
+            b = tmp("m", 2 * n)
+            lst = [(R(b), I, R("rowc", S_(512, 512 + 2 * w)))]
+            for y in range(4):
+                for a in range(4):
+                    for i in range(n):
+                        e = R("eqA", rows(w, h, 4 * y + a, i))
+                        lst += [(R(b, S_(128 * i + a, 128 * i + 128, 4)), e, R("Wd")), (R(b, S_(w + 128 * i + y, w + 128 * i + 128, 4)), e, R("Wt"))]
+            cuts = list(range(1 + OPT["ce"], len(lst) + 1, OPT["ce"]))
+            for x, fin in enumerate(("Df", "Tf") if early else ()):
+                for i in range(n):
+                    o = R(b, blk(n * x + i))
+                    lst += [(o, R(fin, t, blk(h + i)), R("I64")), (o, can("Can", t, blk(h + i), 1 - x), R("I64n"))]
+            group(lst, *cuts)
+            act(R("cmD", c), R(b, blk(0, w)), F.Sign, bias=cst(-0.5))
+            act(R("cmA", c), R(b, blk(1, w)), F.Sign, bias=cst(-0.5))
+            pD = tmp("m", n)
+            mm(chain(pD, (I, R("Df", t, c)), *turned("cmD", I2080n, h, n)))
+            ts(R("D1", c), R(pD), -2080.0, A.add, -2112.0, A.max)
+            ts(R("D1u", c), R("D1", c), -2048.0, A.max, 2063.0, A.add)
+            ts(R("nk", c), R("D1", c), -2047.5, A.is_le, -0.5, A.add)
         n = OPT["nx"]
         for hb in range(n):
-            gat("S", R("XG", h, blk(hb, 2048 // n)), WIN, R("D1u", h, blk(hb, 128 // n)))
-        for hb in (0, 1):
-            scan(R("xs", h, blk(hb, 1024)), R("rst"), R("XG", h, blk(hb, 1024)))
+            gat("V" if hb in OPT["xv"] else "S", R("XG", blk(hb, 4096 // n)), WIN, R("D1u", blk(hb, 256 // n)))
+        for hb in range(4):
+            scan(R("xs", blk(hb, 1024)), R("rst"), R("XG", blk(hb, 1024)))
 
-    def stageB(t, h):
-        k = 2 * t + h
-        Z, Tn, rs, oh = R("Q", k, blk(2)), R("Tq", h, blk(0)), R("rst", S_(0, 128)), R("oh", h)
-        b = tmp("m", 2)
-        kk, d = R(b, blk(0)), R(b, blk(1))
-        mm([(R(b), I, R("rowc"), True, False), (d, Z, BO, False, False)] +
-           [(R(b, S_(128 + j, 256, 16)), R("Y", h, S_(j, 2048, 16)), BO8, False, False) for j in range(16)] +
-           [(R(b, S_(j, 256, 16)), R("MN", h, S_(j, 2048, 16)), R("KB"), False, j == 15) for q in range(4) for j in range(q, 16, 4)], *OPT["ck"])
-        scan(R("sk", h), rs, kk)
-        scan(R("sk2", h, S_(None, None, -1)), rs, R("sk", h, S_(None, None, -1)))
-        tt(oh, R("sk2", h), kk, A.is_equal)
-        shift(OPT["dst"], R("dst", h), d, -2040.0)
-        d = R(tmp("m", 1))
-        mm(chain(d, (R("dst", h), In), (R("cmA", h), I4160n)))
-        act(R("FC", h), d, F.Sign, bias=R("nlim", S_(t, t + 1)), scale=-1.0)
-        FC, XS, KT = R("FC", h), R("Q", k, blk(0)), R("Q", k, blk(1))
-        o1, x, p = R(tmp("m", 1)), R(tmp("m", 1)), R(tmp("m", 1))
-        mm(chain(o1, (oh, I)))
-        tt(KT, Tn, o1, A.mult)
-        mm(chain(x, (In, R("nk", h)), (R("I64"), FC), (oh, R("I64"))))
-        shift(OPT["xs"], XS, x, 0.0)
-        L = tmp("m", 1)
-        mm(chain(R(L, S_(0, 24)), *[(R("Zs", S_(15 - r, 143 - r)), R("Q", k, S_(r, 384, 16))) for r in range(16)]))
-        X, E, U = R(L, S_(0, 8)), R(L, S_(8, 16)), R(L, S_(16, 24))
-        ts(R("AS", h), X, -967.5, A.is_gt, 16384.0, A.mult)
-        ts(R("nu", h, S_(0, 8)), E, 2047.0 - 8192.0, A.add)
-        tt(R("sel", h), R("nu", h, S_(0, 8)), R("AS", h), A.add)
-        tt(R("nu", h, S_(8, 16)), R("sel", h), U, A.max)
-        ts(R("npr", h), X, -968.0, A.is_equal, -1056.0, A.mult)
-        ts(R("nlu", h), E, 2063.0, A.add)
-        ts(R("nv", h), R("nu", h), 1023, A.bitwise_and)
-        cp(R("wu", h), R("nv", h, S_(8, 16)))
-        gat(OPT["sw"], R("sw", h), R("stw"), R("wu", h), -2047.0)
-        gat(OPT["cw"], R("cw", h), R("scw", S_(0, 1024)), R("wu", h), -2047.0)
-        gat("S", R("ysb", h), WIN, R("nlu", h))
-        tt(R("PV", blk(h, 8)), R("nv", h, S_(0, 8)), R("npr", h), A.add)
-        c = R(tmp("m", 1))
-        mm(chain(c, (BO, XS), (R("BO128n"), FC)))
-        act(R("NG", h), c, F.Relu, bias=cst(4322.0), scale=-4.0)
-        act(R("NA", h), c, F.Relu, bias=cst(-1015.5))
-        mm(chain(p, (I, Tn), (R("cmA", h), I4160n), (oh, I4160n)))
-        act(R("KTn", h), p, F.Sign, bias=cst(-2047.5), scale=-1.0)
-        act(R("T1s", blk(h)), p, F.Relu, bias=cst(2048.0))
-        if OPT["t1"]:
-            shift(OPT["t1"], R("T1", h), p, 0.0)
+    def stageB(t):
+        for h0, n, c, _ in parts("pK"):
+            b, w = tmp("m", 2 * n), 128 * n
+            kk, d = R(b, S_(0, w)), R(b, S_(w, 2 * w))
+            lst = [(R(b), I, R("rowc", S_(0, 2 * w)))] + [(R(b, blk(n + i)), R("Q", t, blk(4 + h0 + i)), BO) for i in range(n)]
+            for i in range(n):
+                x = 2048 * (h0 + i)
+                lst += [(R(b, S_(w + 128 * i + j, w + 128 * i + 128, 16)), R("Y", S_(x + j, x + 2048, 16)), BO8) for j in range(16)]
+                lst += [(R(b, S_(j, 2 * w, 16)), R("MN", S_(x + j, x + 2048, 16)), R("KB", i, S_(0, 16 * n))) for q in range(4) for j in range(q, 16, 4)]
+            cuts = list(range(1 + n, len(lst), OPT["ck"]))
+            if t:
+                y = cuts[-OPT["mk"]]
+                cuts = [x + 2 * n * (x > y) for x in cuts] + [y + 2 * n]
+                for i in range(n):
+                    lst[y:y] = [(R(b, blk(i)), R("Tf", t, blk(h0 + i)), R("I64")), (R(b, blk(i)), can("Can", t, blk(h0 + i), 0), R("I64n"))]
+            group(lst, *sorted(cuts))
+            rs, back = R("rst", S_(0, w)), S_(c.stop - 1, c.start - 1 if c.start else None, -1)
+            scan(R("sk", c), rs, kk)
+            scan(R("sk2", back), rs, R("sk", back))
+            tt(R("oh", c), R("sk2", c), kk, A.is_equal)
+            shift(OPT["dst"], R("dst", c), d, -2040.0)
+        for h, n, c, l in parts("pB"):
+            Tf, D1 = R("Tf", t, c), R("D1", c)
+            d = tmp("m", n)
+            mm([m for i in range(n) for m in chain(d, (R("dst", blk(h + i)), In, blk(i)), (R("cmA", blk(h + i)), I2080n, blk(i)))])
+            act(R("FC", c), R(d), F.Sign, bias=R("nlim", S_(t, t + 1)), scale=-1.0)
+            FC, XS = R("FC", c), R("Q", t, c)
+            o1, x, p = tmp("m", n), tmp("m", n), tmp("m", n)
+            mm([(R(o1, blk(i)), R("oh", blk(h + i)), I, True, True) for i in range(n)])
+            tt(R("Q", t, off(c, 256)), Tf, R(o1), A.mult)
+            mm(chain(x, (In, R("nk", c)), (R("I64"), FC), *turned("oh", R("I64"), h, n)))
+            shift(OPT["xs"], XS, R(x), 0.0)
+            L, w = tmp("m", 1), 8 * n
+            y = 32 + w
+            mm(chain(L, *([(R("Zs", S_(15 - r, 143 - r)), R("Q", t, S_(128 * h + r, 128 * h + 16 * y, 16)), S_(0, y)) for r in range(16)] +
+                          [(I, R("LC", S_(0, y)), S_(0, y))])))
+            X, E, U = R(L, S_(0, w)), R(L, S_(16, 16 + w)), R(L, S_(32, 32 + w))
+            both = blk(h, 2 * w)
+            lo, hi = S_(both.start, both.start + w), S_(both.start + w, both.stop)
+            ts(R("AS", l), X, -967.5, A.is_gt, 16384.0, A.mult)
+            tt(R("nu", lo), R("AS", l), E, A.add)
+            tt(R("nu", hi), R("nu", lo), U, A.max)
+            ts(R("npr", l), X, -968.0, A.is_equal, -1056.0, A.mult)
+            ts(R("nlu", l), E, 16.0, A.add)
+            ts(R("nv", both), R("nu", both), 1023, A.bitwise_and)
+            cp(R("wu", l), R("nv", hi))
+            gat(OPT["sw"], R("sw", c), R("stw"), R("wu", l), -2047.0)
+            gat(OPT["cw"], R("cw", c), R("scw", S_(0, 1024)), R("wu", l), -2047.0)
+            gat(OPT["ys"], R("ysb", c), WIN, R("nlu", l))
+            tt(R("PV", l), R("nv", lo), R("npr", l), A.add)
+            b = tmp("m", n)
+            mm(chain(b, (BO, XS), (R("BO128n"), FC)))
+            act(R("NG", c), R(b), F.Relu, bias=cst(4322.0), scale=-4.0)
+            act(R("NA", c), R(b), F.Relu, bias=cst(-1015.5))
+            mm(chain(p, (I, Tf), *(turned("cmA", I2080n, h, n) + turned("oh", I4160n, h, n))))
+            act(R("KTn", c), R(p), F.Sign, bias=cst(32.5), scale=-1.0)
+            act(R("T1s", c), R(p), F.Relu, bias=cst(-32.0))
+            if t + 1 < NV:
+                b, k = tmp("m", n), OPT["pB"] * t + h
+                mm(chain(b, (In, D1), (R("BO128n"), FC)))
+                act(R("acr", c), R(b), F.Relu, bias=cst(-64.0), scale=1.0 / 64, acc=R("asum", S_(k, k + 1)))
         if t + 1 < NV:
-            c = R(tmp("m", 1))
-            mm(chain(c, (In, R("D1", h)), (R("BO128n"), FC)))
-            act(R("acr", h), c, F.Relu, bias=cst(-64.0), scale=1.0 / 64, acc=R("asum", S_(k, k + 1)))
-        if t + 1 < NV and h == 1:
-            a = R(tmp("m", 1), S_(0, 1))
-            mm(chain(a, *[(R("bo32"), R("asum", S_(i, i + 1))) for i in range(2 * t + 2)]))
-            cp(R("ai"), a)
+            a = tmp("m", 1)
+            mm(chain(a, *[(R("bo32"), R("asum", S_(i, i + 1)), S_(0, 1)) for i in range(OPT["pB"] * (t + 1))]))
+            cp(R("ai"), R(a, S_(0, 1)))
             ts(R("a31"), R("ai"), 31, A.bitwise_and)
             ts(R("nlim", S_(t + 1, t + 2)), R("a31"), -8.0, A.mult, R("thn"), A.add)
 
     def out(name, buf, c, lat=2500):
-        add("Y", 60, lambda g, T: g.sync.dma_start(T[name][:, c], get(T, R(buf, c))), [R(buf, c)], [], tok="so", lat=lat)
+        add("Y", (60,), lambda g, T: g.sync.dma_start(T[name][:, c], get(T, R(buf, c))), [R(buf, c)], [], tok="so", lat=lat)
 
-    def stageC(t, h):
-        k, last = 2 * t + h, t == NV - 1
-        NG, Tn, Z = R("NG", h), R("Tq", h, blk(0)), R("Q", k, blk(2))
-        for i in (0, 1):
-            shift(OPT["ps"][i], half(R("PS", h, blk(i)), i), half(R("sw", h), i), 0.0)
-        for q in range(4):
-            b = tmp("s", 4)
-            mm([(R(b, blk(i)), R("sk8", q // 2, blk(4 * (q % 2) + i)), R("PS", h, blk(q // 2)), True, True) for i in range(4)])
-            act(R("fC", h, blk(q, 512)), R(b), F.Tanh, bias=cst(0.0156263), scale=16.0)
-        b = tmp("m", 1)
-        mm([(R(b, S_(64 * (j // 8) + j % 8, 64 * (j // 8) + 64, 8)), R("fC", h, blk(j)), BO8, True, True) for j in range(16)], *OPT["cc"])
-        act(R("rC", h, blk(0)), R(b), F.Copy, bias=-192.49, scale=-1.0)
-        act(R("rC", h, blk(1)), R(b), F.Copy, bias=192.0)
-        p0, p1 = R(tmp("m", 1)), R(tmp("m", 1))
-        if OPT["t1"]:
-            mm(chain(p1, (I, R("T1", h)), (I4160n, NG)))
-        else:
-            mm(chain(p1, (I, Tn), (R("cmA", h), I4160n), (R("oh", h), I4160n), (I4160n, NG)))
-        mm(chain(p0, (I17, NG), (R("I16"), R("KTn", h)), (R("rC", h, blk(0)), I17), (R("rC", h, blk(1)), I17)))
-        tt(R("C1t", h), R("sw", h), p0, A.min)
-        tt(R("Tm", h), R("C1t", h), p1, A.max)
-        if last:
-            ts(R("ot", blk(h)), R("Tm", h), 2047.0, A.add, -1.0, A.max)
-            out("yt", "ot", blk(h))
-        else:
-            ts(R("stt", k), R("Tm", h), -2063.0, A.max, 2063.0, A.add)
-            send(t, h, "t", "stt", R("tt", k + 2))
-        member(R("cw", h), R("Dq", k), "eqB", h)
-        b = tmp("m", 1)
-        mm([(R(b, S_(j, 128, 16)), R("eqB", h, blk(j)), BO8, True, True) for j in range(16)], *OPT["cc"])
-        act(R("cmB", h), R(b), F.Sign, scale=-1.0)
-        p0, p1 = R(tmp("m", 1)), R(tmp("m", 1))
-        mm(chain(p1, (I, R("D1", h)), (I4160n, NG)))
-        mm(chain(p0, (R("I4096"), NG), (R("I4096"), R("nk", h)), (R("cmB", h), R("I4096"))))
-        tt(R("C1", h), R("cw", h), p0, A.min)
-        tt(R("sd", k), R("C1", h), p1, A.max)
-        if last:
-            ts(R("od", blk(h)), R("sd", k), 2047.0, A.add, -1.0, A.max)
-            out("yd", "od", blk(h))
-        else:
-            send(t, h, "d", "sd", R("Dq", k + 2, S_(0, 128)))
-        ys, c0, b, c3 = R("ysb", h), R(tmp("m", 1)), tmp("m", 2), R(tmp("m", 1))
-        mm(chain(c0, (R("Ih"), ys), (R("Ih"), R("xs", h, S_(15, 2048, 16))), (I4160n, NG)))
-        mm(chain(R(b, blk(0)), (I, Z), (I4160n, NG)) + chain(R(b, blk(1)), (I, ys), (I4160n, R("NA", h))))
-        if OPT["hf"] == "V":
-            ts(R("hf", h), c0, 1023.75, A.add, 1024.0, A.max)
-            act(R("zy", h), R(b), F.Relu)
-        else:
-            act(R("hf", h), c0, F.Relu, bias=cst(1023.75))
-            act(R("zy", h, blk(0)), R(b, blk(0)), F.Relu, bias=cst(1024.0))
-            act(R("zy", h, blk(1)), R(b, blk(1)), F.Relu)
-        mm(chain(c3, (I, Z), (I, R("hf", h)), (In, R("zy", h, blk(0))), (In, R("zy", h, blk(1)))))
-        act(R("oz", blk(h)) if last else R("sz", k), c3, F.Abs, bias=cst(-1024.0) if OPT["hf"] == "V" else 0.0)
-        if last:
-            out("yz", "oz", blk(h))
-        else:
-            send(t, h, "z", "sz", R("Q", k + 2, blk(2)))
+    def stageC(t):
+        last = t == NV - 1
+        for h, n, c, _ in parts("pC"):
+            NG = R("NG", c)
+            p0, p1, tc, dc = tmp("m", n), tmp("m", n), can("sC", t, c, 0), can("sC", t, c, 1)
+            mm(chain(p1, (I2080n, R("one", S_(0, 128 * n))), (I, R("Tf", t, c)), (I2080n, R("KTn", c)), (I4160n, NG)))
+            if spec and not last:
+                b = tmp("m", n)
+                mm(chain(b, (BO, R("Q", t, off(c, 256)))))
+                tt(R("eqn", c), R("sw", c), R(b), A.is_equal)
+            mm(chain(p0, (I17, NG), (R("I16"), R("KTn", c)), *[(R("I69n"), R("eqn", c))] * (spec and not last)))
+            tt(R("C1t", c), R("sw", c), R(p0), A.min)
+            tt(tc, R("C1t", c), R(p1), A.max)
+            if not last:
+                ts(R("stt", t, c), tc, -2063.0, A.max, 2063.0, A.add)
+                send(t, h, "t", R("stt", t, c), R("tt", t + 1, c))
+            if spec and not last:
+                p0, p1 = tmp("m", n), tmp("m", n)
+                mm(chain(p1, (I, R("D1", c)), (I4160n, NG)))
+                mm(chain(p0, (R("I4096"), NG), (R("I4096"), R("nk", c))))
+                tt(R("C1", c), R("cw", c), R(p0), A.min)
+                tt(dc, R("C1", c), R(p1), A.max)
+                if not OPT["join"]:
+                    send(t, h, "e", dc, can("Can", t + 1, c, 1))
+            if not last:
+                y = S_(0, 512) if OPT["join"] else c
+                send(t, h, "c", R("sC", t, y), R("Can", t + 1, y))
+        for h, n, c, _ in parts("pT"):
+            w = 128 * n
+            for i in (0, 1):
+                o, x = half(R("PS", off(c, 256 * i)), i), half(R("sw", c), i)
+                if OPT["ps"][i] == "G":
+                    aff(o, x, [[0, w]], A.is_ge, 0, 0)
+                elif OPT["ps"][i] == "Y":
+                    add("Y", (60,), lambda g, T, o=o, x=x: g.sync.dma_start(get(T, o), get(T, x)), [x], [o], tok="tq%d%d" % (h, i), lat=2200)
+                else:
+                    shift(OPT["ps"][i], o, x, 0.0)
+            r = 512 // w
+            for q in range(16 // r):
+                b = tmp("s", 4)
+                mm([(R(b, blk(i, w)), R("sk8", (r * q + i) // 8, blk((r * q + i) % 8)), R("PS", off(c, 256 * ((r * q + i) // 8))), True, True) for i in range(r)])
+                act(R("fC", S_(2048 * h + 512 * q, 2048 * h + 512 * q + 512)), R(b), F.Tanh, bias=cst(0.0156263), scale=16.0)
+            b = tmp("m", n)
+            mm([(R(b, S_(128 * i + 64 * (j // 8) + j % 8, 128 * i + 64 * (j // 8) + 64, 8)), R("fC", rows(w, h, j, i)), BO8, True, True)
+                for j in range(16) for i in range(n)], *range(OPT["cc"] * n, 16 * n, 4 * n))
+            act(R("rC", c), R(b), F.Copy, bias=-192.49, scale=-1.0)
+            act(R("rC", off(c, 256)), R(b), F.Copy, bias=193.0)
+            p = tmp("m", n)
+            mm(chain(p, (R("I8192"), R("NG", c)), (R("I4096n"), R("KTn", c)), *(turned("rC", R("I8192"), h, n) + turned("rC", R("I8192"), h, n, 2))))
+            fin = R("sT", t, c)
+            for x in ([c] if OPT["pT"] >= OPT["pC"] else [blk(0), blk(1)]):
+                tt(R("sT", t, x), can("sC", t, x, 0), R(p, off(x, -c.start)), A.min)
+            if last:
+                ts(R("ot", c), fin, 2047.0, A.add, -1.0, A.max)
+                out("yt", "ot", c)
+            else:
+                send(t, h, "f", fin, R("Tf", t + 1, c))
+        for h, n, c, _ in parts("pD"):
+            NG = R("NG", c)
+            member(R("cw", c), 1, "eqB", h)
+            b, w = tmp("m", n), 128 * n
+            lst = [m for y in range(4) for i in range(n) for m in
+                   chain(b, *[(R("eqB", rows(w, h, 4 * y + a, i)), R("Wt"), S_(128 * i + y, 128 * i + 128, 4)) for a in range(4)])]
+            mm(lst, *range(4 * n, 16 * n, 4 * n))
+            if spec and not last:
+                act(R("cmB", c), R(b), F.Relu, bias=cst(1.0), scale=-1.0)
+                p = tmp("m", n)
+                mm(chain(p, (R("I4096"), NG), (R("I4096n"), R("nk", c)), *turned("cmB", R("I4096"), h, n)))
+                for x in ([c] if OPT["pD"] >= OPT["pC"] else [blk(0), blk(1)]):
+                    tt(R("sd", t, x), can("sC", t, x, 1), R(p, off(x, -c.start)), A.min)
+            else:
+                act(R("cmB", c), R(b), F.Sign, scale=-1.0)
+                p0, p1 = tmp("m", n), tmp("m", n)
+                mm(chain(p1, (I, R("D1", c)), (I4160n, NG)))
+                mm(chain(p0, (R("I4096"), NG), (R("I4096"), R("nk", c)), *turned("cmB", R("I4096"), h, n)))
+                tt(R("C1", c), R("cw", c), R(p0), A.min)
+                tt(R("sd", t, c), R("C1", c), R(p1), A.max)
+            if last:
+                ts(R("od", c), R("sd", t, c), 2047.0, A.add, -1.0, A.max)
+                out("yd", "od", c)
+            else:
+                send(t, h, "d", R("sd", t, c), R("Df", t + 1, c))
+        for h, n, c, _ in parts("pZ"):
+            NG, Z, w = R("NG", c), R("Q", t, off(c, 512)), 128 * n
+            ys, c0, b, c3 = R("ysb", c), tmp("m", n), tmp("m", 2 * n), tmp("m", n)
+            zy = blk(h, 2 * w)
+            z0, z1 = R("zy", S_(zy.start, zy.start + w)), R("zy", S_(zy.start + w, zy.stop))
+            mm(chain(c0, (R("Ih"), ys), (I4160n, NG), (R("Ih"), R("xs", S_(16 * c.start + 15, 16 * c.stop, 16)))))
+            mm(chain(b, (I, Z, blk(0, w)), (I4160n, NG, blk(0, w))) + chain(b, (I, ys, blk(1, w)), (I4160n, R("NA", c), blk(1, w))))
+            if OPT["hf"] == "V":
+                ts(R("hf", c), R(c0), 1023.75, A.add, 1024.0, A.max)
+                act(R("zy", zy), R(b), F.Relu)
+            else:
+                act(R("hf", c), R(c0), F.Relu, bias=cst(1023.75))
+                act(z0, R(b, blk(0, w)), F.Relu, bias=cst(1024.0))
+                act(z1, R(b, blk(1, w)), F.Relu)
+            mm(chain(c3, (I, Z), (In, z0), (In, z1), (I, R("hf", c))))
+            act(R("oz", c) if last else R("sz", t, c), R(c3), F.Abs, bias=cst(-1024.0) if OPT["hf"] == "V" else 0.0)
+            if last:
+                out("yz", "oz", c)
+            else:
+                send(t, h, "z", R("sz", t, c), R("Q", t + 1, off(c, 512)))
 
     def stageD(t):
         b, PV = tmp("m", 2), R("PV")
         mm([(R(b, S_(r, 256, 16)), R("dd", blk(r)), PV, True, True) for r in range(16)])
-        if OPT["dscan"]:
-            ts(R("eqP"), R(b), 0.0, A.is_equal, 4096.0, A.mult)
-            scan(R("eqS"), R("rst", S_(0, 256)), R("eqP"))
-            c = R("PLf")
-            tt(c, R("eqS", S_(15, 256, 16)), PV, A.add)
-        else:
-            ts(R("eqP"), R(b), 0.0, A.is_equal)
-            c = R(tmp("m", 1), S_(0, 16))
-            mm(chain(c, (I, PV), *[(R("I4096"), R("eqP", S_(r, 256, 16))) for r in range(16)]))
-        ts(R("PLu", S_(0, 32, 2)), c, 1056.0, A.add, R("q0"), A.min)
+        ts(R("eqP"), R(b), 0.0, A.is_equal)
+        c = tmp("m", 1)
+        mm(chain(c, (I, PV, S_(0, 16)), *[(R("I4096"), R("eqP", S_(r, 256, 16)), S_(0, 16)) for r in range(16)]))
+        ts(R("PLu", S_(0, 32, 2)), R(c, S_(0, 16)), 1056.0, A.add, R("q0"), A.min)
         for c in range(16):
-            o, off, src = R("scw"), R("PLu", S_(2 * c, 2 * c + 1)), R("T1s", blk(c, 16))
-            add("V", 60 + 16 * 3.8 * CYC, lambda g, T, o=o, off=off, src=src: g.vector.tensor_scalar(
-                get(T, o).indirect(get(T, off)), get(T, src), 1.0, -1.0, A.mult, A.add), [off, src], [o])
+            o, offs, src = R("scw"), R("PLu", S_(2 * c, 2 * c + 1)), R("T1s", blk(c, 16))
+            add("V", (60, 0, 0, 16), lambda g, T, o=o, offs=offs, src=src: g.vector.tensor_scalar(
+                get(T, o).indirect(get(T, offs)), get(T, src), 1.0, -1.0, A.mult, A.add), [offs, src], [o])
         if t == NV - 1:
             out("ys", "scw", S_(0, 1024), 4500)
 
     for t in range(NV):
-        for s, f, h in (("A0", stageA, 0), ("B0", stageB, 0), ("A1", stageA, 1), ("B1", stageB, 1), ("C0", stageC, 0), ("C1", stageC, 1)):
-            lab[0] = s
-            f(t, h)
-        lab[0] = "D"
-        stageD(t)
+        for s, f in (("A", stageA), ("B", stageB), ("C", stageC), ("D", stageD)):
+            lab[0] = s + str(t)
+            f(t)
     return ops
 
 
@@ -454,10 +581,13 @@ def depend(ops):
         for x, wr in [(x, False) for x in o["r"]] + [(x, True) for x in o["w"]]:
             sp = tuple(s[:3] for s in span(x))
             acc[(x[0], sp)] = acc.get((x[0], sp), False) or wr
+        rd = {(x[0], tuple(s[:3] for s in span(x))) for x in o["r"]}
         for (name, sp), wr in acc.items():
             for j, sj, wj in hist.get(name, ()):
-                if j != i and (wj or wr) and meet(sp, sj):
-                    (seq if name in TEMP and o["e"] == ops[j]["e"] == "P" else pw).add(j)
+                if j != i and name in TEMP and o["e"] == ops[j]["e"] == "P":
+                    seq.add(j)
+                elif j != i and (wj or wr) and meet(sp, sj):
+                    (seq if OPT["ww"] and (name, sp) not in rd and o["e"] == ops[j]["e"] in "VS" and "tok" not in ops[j] else pw).add(j)
         for (name, sp), wr in acc.items():
             h = hist.setdefault(name, [])
             if wr:
@@ -472,20 +602,23 @@ def schedule(ops):
     pred, succ = [], [[] for _ in range(n)]
     for i, o in enumerate(ops):
         pred.append([(j, WAKE if ops[j]["e"] != o["e"] else SELF) for j in o["pw"]] + [(j, 0.0) for j in o["seq"]] +
-                    ([(o["after"], REMOTE)] if "after" in o else []))
+                    ([(o["after"], REMOTE + o["xl"])] if "after" in o else []))
         for j, l in pred[i]:
             succ[j].append((i, l))
     fin = [o["d"] + o.get("lat", 0.0) for o in ops]
-    pri = [0.0] * n
+    steps, key = {}, [None] * n
+    for i, o in enumerate(ops):
+        if o["n"] in PLAN:
+            steps.setdefault((o["n"], int(o["g"][1])), []).append(i)
+    for (name, t), l in steps.items():
+        for k, i in enumerate(l):
+            key[i] = 1000 * (t * PLAN["P"] + PLAN[name][0] + PLAN[name][1] * k / max(1, len(l) - 1))
     for i in range(n - 1, -1, -1):
-        pri[i] = fin[i] + max([0.0] + [l + pri[k] for k, l in succ[i]])
-    pri = [p + LEAD.get(o["g"], 0.0) for p, o in zip(pri, ops)]
-    best = None
-    for _ in range(ROUNDS):
-        x = forward(ops, pred, succ, fin, pri)
-        if best is None or x[0] < best[0]:
-            best = x
-        pri = backward(ops, pred, succ, fin, x[2])
+        if key[i] is None:
+            key[i] = min([key[k] - PLAN["mu"] * (fin[i] + l) for k, l in succ[i]] or [1000 * PLAN["P"] * (int(ops[i]["g"][1:] or 0) + 1.3)])
+    best = forward(ops, pred, succ, fin, [-a for a in key])
+    for _ in range(ROUNDS - 1):
+        best = forward(ops, pred, succ, fin, backward(ops, pred, succ, fin, best[2]))
     PLACE.update(best[4])
     for i, o in enumerate(ops):
         o["s"], o["pw"] = best[2][i] - fin[i], o["pw"] | best[3][i]
@@ -537,7 +670,7 @@ def forward(ops, pred, succ, fin, pri):
                 opts = [PLACE[x]]
             else:
                 role, m = TEMP[x]
-                opts = [(b, a) for b in BANKS[role] for a in range(0, 5 - m) if all(held[b][c] is None for c in range(a, a + m))]
+                opts = [(b, a) for b in BANKS[role] for a in range(0, 5 - m, m) if all(held[b][c] is None for c in range(a, a + m))]
             best = None
             for b, a in opts:
                 if o["e"] == "P" and lock[b] not in (None, x):
@@ -584,7 +717,7 @@ def forward(ops, pred, succ, fin, pri):
     return max(end.values()), order, end, more, PLACE
 
 
-CACHE = {}
+CACHE = []
 
 
 def rank_program(g, core, T, topo):
@@ -593,12 +726,13 @@ def rank_program(g, core, T, topo):
         return
     dst = T.cores[(rank + 1) % len(T.cores)]
     rid, pid = topo.addr(dst)[:2]
-    mask, nrem = topo.mask(core, dst), len(topo.engines(core, dst))
-    if nrem not in CACHE:
-        ops = program(nrem)
+    mask, nout = topo.mask(core, dst), len(topo.engines(core, dst))
+    nin = len(topo.engines(T.cores[rank - 1], core))
+    if not CACHE:
+        ops = program()
         depend(ops)
-        CACHE[nrem] = (ops, schedule(ops))
-    ops, order = CACHE[nrem]
+        CACHE.extend((ops, schedule(ops)))
+    ops, order = CACHE
     queue = {"V": g.vector, "S": g.scalar, "P": g.tensor, "G": g, "Y": g.sync}
     sem = {"V": "sv", "S": "ss", "P": "sp", "G": "sg"}
     known, vc, tok, total = {e: {} for e in queue}, {}, {}, {"ls": 0}
@@ -606,8 +740,8 @@ def rank_program(g, core, T, topo):
         o = ops[i]
         e = o["e"]
         if e == "R":
-            tok[i], vc[i] = (o["tok"], o["inc"]), {}
-            total[o["tok"]] = o["inc"]
+            tok[i], vc[i] = (o["tok"], nin), {}
+            total[o["tok"]] = nin
             continue
         kn, need = known[e], {}
         for j in o["pw"]:
@@ -619,11 +753,12 @@ def rank_program(g, core, T, topo):
                 kn[s] = need[s]
             for a in vc[j]:
                 kn[a] = max(kn.get(a, 0), vc[j][a])
-        x = o["fn"](g, T)
-        if o.get("n") == "send":
-            g.remote_dma(out_ap=x[0], in_ap=x[1], remote_sem=T.sem[x[2]], local_sem=T.sem["ls"], pid=pid, routing_id=rid, dma_engine_mask=mask)
-            total["ls"] += nrem
+        if "land" in o:
+            g.remote_dma(out_ap=get(T, o["land"]), in_ap=get(T, o["src"]), remote_sem=T.sem[o["tok"]], local_sem=T.sem["ls"],
+                         pid=pid, routing_id=rid, dma_engine_mask=mask)
+            total["ls"] += nout
             continue
+        x = o["fn"](g, T)
         s, n = (o["tok"], 16) if "tok" in o else (sem[e], 1)
         for y in x if isinstance(x, list) else [x]:
             total[s] = total.get(s, 0) + n

@@ -13,32 +13,37 @@ def _decl(text, d, lead):
         SCRATCH[n] = ("sbuf", [128] + lead + [int(x) for x in s.split(",")], d)
 
 
-_decl("tli:256 dli:256 thi:1 sci:1024 sti:1024 pidx:1 pmi:1 ai:1 a31:1 nu:32 nv:32", i32, [])
-_decl("tm0:256 ts0:256 stw:1024 scw:1040 pmf:1 iq:16 P1:16 on32:128 boa:128 bo32:128 id32:128 io:256 turn:1 pf:8 "
-      "q0:1 thn:1 nlim:8 asum:16 T1s:256 od:256 ot:256 oz:256 cst:12 sk:256 sk2:256 AS:16 sel:16 npr:16 C1:256 C1t:256", f32, [])
-_decl("LC:48 PV:16 PS:512 D1:256 cw:256 sw:256 hf:256 dst:256 zy:512 Ds:2,1024", f16, [])
-_decl("clkw:4112 bc:2048 sk8:2,1024 dd:2048 rst:1024 rowc:1024 Zs:144 KB:3,32 eqP:256 zl:256 "
-      "eqA:4096 eqB:4096 fC:4096 Y:4096 MN:4096 XG:4096 xs:4096 nk:256 oh:256 cmA:256 cmB:256 rC:512 FC:256 NG:256 NA:256 "
-      "KTn:256 ysb:256 acr:256 cmD:256 eqn:256 one:256 sp:8,128 Wd:32 Wt:32", b16, [])
-_decl("PLu:32 D1u:256 nlu:16 wu:16", u16, [])
+_decl("tli:256 dli:256 thi:1 sci:1024 sti:1024 pidx:1 pmi:1 ai:1 a31:1 nu:32 nv:32 idi:64", i32, [])
+_decl("scw:1040 pmf:1 on32:128 boa:128 bo32:128 id32:128 io:256 pf:8 q0:1 thn:1 nlim:8 asum:8 T1s:256 od:256 ot:256 oz:256 "
+      "sk:256 sk2:256 AS:16 npr:16 C1:256 C1t:256", f32, [])
+_decl("LC:48 PV:16 PS:512 D1:256 cw:256 sw:256 hf:256 dst:256 Ds:2,1024", f16, [])
+_decl("clkw:4112 Mk:256 sk8:2,1024 dd:144 d2:16,128 rst:1024 rowc:768 Zs:144 KB:2,32 K1:16 eqP:256 eqS:256 zl:256 "
+      "eqA:4096 eqB:4096 fC:4096 Y:4096 MN:4096 XG:4096 xs:4096 nk:256 oh:256 cmA:256 cmB:256 rC:512 FC:256 NG:256 "
+      "KTn:256 ysb:256 acr:256 cmD:256 eqn:256 one:256 sp:8,128 W2:32,2", b16, [])
+_decl("PLu:32 D1u:256 nlu:16 wu:16 idu:64", u16, [])
 _decl("tt:256 stt:256", u16, [NV])
-_decl("Df:256 Tf:256 Can:512 Q:768 sd:256 sT:256 sC:512 sz:256", f16, [NV])
-_l = "I In I4160n I17 I16 Ih I64 I64n I4096 I4096n I8192 I2080n I69n BO BO128n".split()
-SCRATCH["kb"] = ("sbuf", [128, len(_l), 128], b16)
-for _i, _n in enumerate(_l):
+_decl("Fin:512 Can:512 Q:768 sF:512 sC:512 sz:256", f16, [NV])
+KS = (("In", -1), ("I4160n", -4160), ("I17", 131072), ("I16", 65536), ("Ih", 0.5), ("I64", 64), ("I64n", -64), ("I4096", 4096),
+      ("I4096n", -4096), ("I8192", 8192), ("I2080n", -2080), ("I69n", -69632), ("I15", 1.5), ("I256", 256), ("BO128n", -128))
+SCRATCH["kb"] = ("sbuf", [128, len(KS) + 2, 128], b16)
+for _i, _n in enumerate(["I", "BO"] + [k[0] for k in KS]):
     ALIAS[_n] = ("kb", _i)
 for _i in range(8):
-    SCRATCH["ps%d" % _i] = ("psum", [128, 512], f32)
-BANKS = {"v": tuple(range(8)), "s": tuple(range(8)), "z": tuple(range(8)), "m": tuple(range(7, -1, -1))}
+    SCRATCH["ps%d" % _i] = ("psum", [128, 512] if _i < 7 else [128, 64, 8], f32)
+BANKS = {"v": tuple(range(7)), "m": tuple(range(6, -1, -1)), "c": (7,)}
 LOADS = ("tl", "dl", "z", "th", "clk", "st", "sc")
-OPT = dict(xs="S", dst="S", sw="S", cw="V", ys="S", hf="S", ps="GG", ny=8, nm=4, nx=8, cc=8, ck=8, mk=1, ww=0, join=0, d0="S", xv=(0,), yv=(),
-           spec=1, ds="Y", dup=1, ce=8, pA=1, pD=1, pT=1, pK=1, pB=1, pC=1, pZ=1)
-SEMAPHORES = ["sv", "ss", "sp", "sg", "so", "ls", "tp0", "tp1", "d00", "d01", "d10", "d11", "tq00", "tq01", "tq10", "tq11"] + ["l_" + n for n in LOADS]
-SEMAPHORES += ["a%d%d%s" % (t, h, k) for t in range(1, NV) for h in (0, 1) for k in "dtfzce"]
-CYC, PEC, OVV, OVS, WAKE, SELF, REMOTE, LOOK = 0.83, 0.43, 30.0, 40.0, 90.0, 90.0, 3500.0, 0.3
-GAT, SCA, PEM = 1.56, 3.8, 4.0
-ROUNDS, LOOKB = 2, 0.1
-PLAN = {'P': 21.7, 'mu': 1.5, 'SYA': (6.6, 6.2), 'SXGA': (12.6, 6.0), 'SfCC': (23.0, 3.9), 'VeqAA': (8.6, 3.3), 'VMNA': (10.2, 5.0), 'VeqBC': (24.8, 3.3), 'VscwD': (29.2, -0.3), 'VwuB': (22.4, -1), 'VsttC': (24.2, -0.5), 'VsdC': (29.7, 0), 'VsTC': (29.5, -2), 'SszC': (27.0, 0), 'VxsA': (19.0, 5), 'VD1uA': (15.7, -2.5), 'P~kbD': (25.8, 1.0), 'VohB': (16.3, 2.0), 'P~eqBC': (28.7, 3.3), 'VQB': (20.4, 1.0), 'VeqnC': (21.0, 1.0), 'P~kbA': (9.7, 2.0), 'P~dstB': (15.3, 0.5), 'P~fCC': (25.3, 1.2)}
+OPT = dict(scs=1, kn=2, ny=4, xp=(48, 96, 144, 192, 220), xv="SSSSSV", lq="YYYYSYY", oq=("yz",))
+SEMAPHORES = ["sv", "ss", "sp", "sg", "so", "ls", "tp", "tq0", "tq1", "d0", "d1"] + ["l_" + n for n in LOADS]
+SEMAPHORES += ["a%d%s" % (t, k) for t in range(1, NV) for k in "tefdz"]
+CYC, PEC, OVV, OVS, WAKE, SELF, REMOTE, LOOK, LOOKB, ROUNDS = 0.83, 0.40, 10.0, 50.0, 55.0, 70.0, 2300.0, 0.3, 0.1, 2
+GAT, SCA, PEM, PEG, LAT, ISSUE, RATE, LOCAL, START = 1.62, 3.8, 9.0, 17.0, 1.0, 250.0, 75.0, 700.0, 150.0
+PLAN = {'P': 23.5, 'mu': 3.4, 'VsFC': (23.1, -0.4), 'Gsk8': (16.6, -5.4), 'ScmBC': (23.6, 0.1), 'P~kbB': (2.0, 26.5), 'SysbB': (20.5, -3.5),
+        'VCanA': (-15.0, 4.4), 'VnuB': (15.3, 6.8), 'VC1C': (-4.9, 7.7), 'ST1sB4': (14.3, 1.9), 'Skb': (-17.8, 19.2), 'ScwB': (-8.3, -1.8),
+        'P~YB': (-10.9, 5.0), 'VsFC0': (18.9, 0.9), 'SXGA0': (-18.7, -3.3), 'VPVB': (5.5, 1.0), 'Gpidx': (-50.3, -3.0), 'Vone': (-51.2, -0.5),
+        'Vthn': (15.2, -3.5), 'Vq0': (2.9, -1.5), 'VswB4': (2.6, -0.5), 'VPVB4': (6.3, -1.8), 'VscwD4': (21.6, 8.7), 'VC1tC0': (-4.1, -2.4),
+        'VsttC': (-4.5, -0.2), 'Vclkw': (-20.4, 2.0), 'P~spC': (15.4, 0.0), 'Vtli': (-49.5, 2.0), 'Von32': (-21.3, 0.2), 'Gbo32': (-13.8, 1.5),
+        'Gboa': (-17.5, 0.5), 'Vrowc': (-4.8, 0.0), 'P~kbC0': (-12.3, -2.9), 'Vidu': (-10.3, 0.5), 'VeqSD': (3.9, 0.5)}
+PAIRS = [(q + y, q + (x ^ y)) for q in (0, 2) for x in (0, 1) for y in (0, 1)] + [(y, a) for y in range(4) for a in range(4) if y // 2 != a // 2]
 TEMP, PLACE = {}, {}
 
 
@@ -61,6 +66,8 @@ def psum(x):
 def get(T, x):
     if psum(x):
         bank, b0 = PLACE[x[0]][:2]
+        if TEMP[x[0]][0] == "c":
+            return T["ps%d" % bank][(slice(None),) + x[1]]
         a, b, st = (x[1][0] if x[1] else slice(None)).indices(128 * TEMP[x[0]][1])
         return T["ps%d" % bank][:, 128 * b0 + a:128 * b0 + b:st]
     return T[x[0]][(x[2:] or (slice(None),)) + x[1] + (slice(None),) * (len(SCRATCH[x[0]][1]) - 1 - len(x[1]))]
@@ -72,7 +79,7 @@ def half(x, i):
 
 def span(x):
     out = []
-    for d, n in enumerate([128 * TEMP[x[0]][1]] if psum(x) else SCRATCH[x[0]][1][1:]):
+    for d, n in enumerate(SCRATCH[x[0]][1][1:] if not psum(x) else [64, 8] if TEMP[x[0]][0] == "c" else [128 * TEMP[x[0]][1]]):
         i = x[1][d] if d < len(x[1]) else slice(None)
         if isinstance(i, int):
             out.append((i, i + 1, 1, 1))
@@ -99,15 +106,6 @@ def cover(p, q):
 
 def two(*xs):
     return all(not psum(x) and SCRATCH[x[0]][2] in (f16, b16, u16) for x in xs)
-
-
-def parts(name):
-    n = OPT[name]
-    return [(h, 3 - n, blk(h, 256 // n), blk(h, 16 // n)) for h in range(n)]
-
-
-def off(c, x):
-    return slice(c.start + x, c.stop + x)
 
 
 def program():
@@ -145,9 +143,9 @@ def program():
     def fill(o, v):
         add("V", (OVV, max(64, size(o) * (0.5 if two(o) else 1))), lambda g, T: g.vector.memset(get(T, o), v), [], [o])
 
-    def scan(o, a, b, op0=A.mult):
+    def scan(o, a, b):
         add("V", (OVV, max(64, size(o) * (0.5 if two(o, a, b) else 1))),
-            lambda g, T: g.vector.tensor_tensor_scan(get(T, o), get(T, a), get(T, b), 0.0, op0, A.max), [a, b], [o])
+            lambda g, T: g.vector.tensor_tensor_scan(get(T, o), get(T, a), get(T, b), 0.0, A.mult, A.max), [a, b], [o])
 
     def act(o, i, func, bias=0.0, scale=1.0, acc=None):
         def fn(g, T):
@@ -155,12 +153,12 @@ def program():
             return g.scalar.activation(get(T, o), get(T, i), func, bias=val(T, bias), scale=scale, **kw)
         add("S", (OVS, max(64, size(o))), fn, [i, bias], [o] + ([] if acc is None else [acc]))
 
-    def gat(e, o, win, offs, shift=None):
+    def gat(e, o, win, offs, shift=None, least=None):
         def fn(g, T):
             x = get(T, win).indirect(get(T, offs))
             if e == "S":
                 return g.scalar.activation(get(T, o), x, F.Copy, bias=shift or 0.0)
-            return g.vector.tensor_copy(get(T, o), x) if shift is None else g.vector.tensor_scalar(get(T, o), x, shift, None, A.add)
+            return g.vector.tensor_copy(get(T, o), x) if shift is None else g.vector.tensor_scalar(get(T, o), x, shift, least, A.add, A.max)
         add(e, (60, 0, size(o)), fn, [win, offs], [o])
 
     def mm(lst, *cuts):
@@ -175,7 +173,7 @@ def program():
                 x = g.tensor.matmul(get(T, o), get(T, l), get(T, r), a, b)
             return x
         d = sum(max(64, size(m[0])) * (4 if SCRATCH[m[1][0]][2] == f32 else 1) for m in lst)
-        add("P", (30, 0, 0, 0, len(lst), d), fn, [m[1] for m in lst] + [m[2] for m in lst], [m[0] for m in lst], open=not lst[-1][4])
+        add("P", (PEG, 0, 0, 0, len(lst), d), fn, [m[1] for m in lst] + [m[2] for m in lst], [m[0] for m in lst], open=not lst[-1][4])
 
     def group(lst, *cuts):
         mm([m + (i == 0, i == len(lst) - 1) for i, m in enumerate(lst)], *cuts)
@@ -183,389 +181,305 @@ def program():
     def chain(b, *terms):
         return [(R(b, *m[2:]), m[0], m[1], i == 0, i == len(terms) - 1) for i, m in enumerate(terms)]
 
-    def turned(buf, k, h0, n, x=0):
-        return [(R(buf, blk(x + h0 + i)), k, blk(i)) for i in range(n)]
+    def total(*terms):
+        b = tmp("m", 2)
+        mm(chain(b, *terms))
+        return R(b)
 
-    def load(q, name, o, src, dur):
-        add(q, (60,), lambda g, T: (g.sync if q == "Y" else g.scalar).dma_start(get(T, o), src(T)), [], [o], tok="l_" + name, lat=dur)
-    load("S", "clk", R("clkw", S_(16, 4112)), lambda T: T.clk[:, :], 5000)
-    load("Y", "tl", R("tli"), lambda T: T.tl[:, :], 2200)
-    load("Y", "dl", R("dli"), lambda T: T.dl[:, :], 2500)
-    load("Y", "z", R("zl"), lambda T: T.z0[:, :], 2700)
-    load("Y", "th", R("thi"), lambda T: T.th[:, :], 2800)
-    load("Y", "st", R("sti"), lambda T: T.st[:, :], 6500)
-    load("Y", "sc", R("sci"), lambda T: T.sc[:, :], 8000)
+    def turned(buf, k, x=0):
+        return [(R(buf, blk(x + i)), k, blk(i)) for i in (0, 1)]
+
+    def dma(q, pairs, r, w, tok, kib):
+        add(q, (len(pairs) * START,), lambda g, T: [(g.sync if q == "Y" else g.scalar).dma_start(o(T), i(T)) for o, i in pairs], r, w,
+            tok=tok, lat=1200 + 1024 * kib / LOCAL, nd=len(pairs))
+
+    def move(pairs, r, w, tok, kib):
+        dma("Y", [(lambda T, o=o: get(T, o), lambda T, i=i: get(T, i)) for o, i in pairs], r, w, tok, kib)
+
+    for name, o, src, kib in (("clk", R("clkw", S_(16, 4112)), "clk", 2048), ("tl", R("tli"), "tl", 128), ("dl", R("dli"), "dl", 128),
+                              ("z", R("zl"), "z0", 64), ("th", R("thi"), "th", 16), ("st", R("sti"), "st", 1024), ("sc", R("sci"), "sc", 1024)):
+        dma(OPT["lq"][LOADS.index(name)], [(lambda T, o=o: get(T, o), lambda T, src=src: T[src][:, :])], [], [o], "l_" + name, kib)
+
+    def out(name, buf, n):
+        dma("S" if name in OPT["oq"] else "Y", [(lambda T: T[name][:, :], lambda T: get(T, R(buf, S_(0, n))))], [R(buf, S_(0, n))], [], "so", n)
 
     def iota(o, pat, base, cm=0):
         kw = {} if SCRATCH[o[0]][2] == i32 else {"allow_small_or_imprecise_dtypes": True}
-        add("G", (130, 2 * size(o)), lambda g, T: g.iota(get(T, o), pat, base, cm, **kw), [R("turn")], [o])
+        add("G", (130, 2 * size(o)), lambda g, T: g.iota(get(T, o), pat, base, cm, **kw), [], [o])
 
     def aff(o, i, pat, op, base, cm, other=0.0):
-        alone = [R("turn")] * (len(o) > 2 and o[2].start > 0)
-        add("G", (170, 2 * size(o)), lambda g, T: g.affine_select(get(T, o), get(T, i), pat, op, other, base, cm), [i, R("turn")], [o] + alone)
+        add("G", (170, 2 * size(o)), lambda g, T: g.affine_select(get(T, o), get(T, i), pat, op, other, base, cm), [i], [o])
 
-    def shift(e, o, i, x):
-        return act(o, i, F.Copy, bias=x) if e == "S" else ts(o, i, x, A.add)
     fill(R("on32"), 1.0)
     iota(R("pidx"), [[0, 1]], 0, 1)
     aff(R("boa"), R("on32"), [[-16, 8], [0, 16]], A.is_ge, 0, 1)
     aff(R("bo32"), R("boa"), [[16, 8], [0, 16]], A.is_ge, 15, -1)
     aff(R("id32"), R("on32"), [[-1, 128]], A.is_equal, 0, 1)
-    iota(R("iq"), [[1, 16]], 0)
-    kn = 3 - OPT["pK"]
-    fill(R("rowc", S_(128 * kn, 1024)), 0.0)
-    iota(R("rowc", S_(0, 128 * kn)), [[0, 8 * kn], [-1, 16]], 16)
+    fill(R("rowc", S_(256, 768)), 0.0)
+    iota(R("rowc", S_(0, 256)), [[0, 16], [-1, 16]], 16)
     ts(R("pmi"), R("pidx"), 15, A.bitwise_and)
     cp(R("pmf"), R("pmi"))
     pm = R("pmf", S_(0, 1))
-    ts(R("P1"), R("iq", S_(0, 16)), pm, A.is_equal)
+    ts(R("Mk"), R("rowc", blk(0, 256)), pm, A.subtract, 0.0, A.is_le)
     act(R("BO"), R("bo32"), F.Copy)
     act(R("I"), R("id32"), F.Copy)
-    for j in range(16):
-        ts(R("bc", blk(j)), R("BO"), R("P1", S_(j, j + 1)), A.mult)
-    fill(R("clkw", S_(0, 16)), -1.0)
-    for n, src, k in (("In", "id32", -1), ("I4160n", "id32", -4160), ("I17", "id32", 131072), ("I16", "id32", 65536), ("Ih", "id32", 0.5),
-                      ("I64", "id32", 64), ("I64n", "id32", -64), ("I4096", "id32", 4096), ("I4096n", "id32", -4096), ("I8192", "id32", 8192),
-                      ("I2080n", "id32", -2080), ("I69n", "id32", -69632), ("BO128n", "bo32", -128)):
-        act(R(n), R(src), F.Copy, scale=float(k))
+    fill(R("clkw", S_(1, 16)), -1.0)
+    fill(R("clkw", S_(0, 1)), 0.0)
+    for n, k in KS:
+        act(R(n), R("bo32" if n[0] == "B" else "id32"), F.Copy, scale=float(k))
     BO8 = R("BO", S_(0, 128, 16))
-    if kn == 2:
+    if OPT["kn"] == 2:
         fill(R("KB"), 0.0)
-    for i in range(kn):
-        ts(R("KB", i, blk(i, 8)), BO8, 16.0, A.mult)
-        ts(R("KB", i, blk(kn + i, 8)), BO8, -2.0, A.mult)
+        for i in (0, 1):
+            ts(R("KB", i, blk(i, 8)), BO8, 16.0, A.mult)
+            ts(R("KB", i, blk(2 + i, 8)), BO8, -2.0, A.mult)
+    else:
+        ts(R("K1", blk(0, 8)), BO8, 16.0, A.mult)
+        ts(R("K1", blk(1, 8)), BO8, -2.0, A.mult)
     for i, x in enumerate((0.0, 2047.0, 4096.0)):
         fill(R("LC", blk(i, 16)), x)
     fill(R("Zs"), 0.0)
     cp(R("Zs", S_(15, 143, 16)), BO8)
-    iota(R("rst"), [[0, 64], [1, 16]], 0)
-    aff(R("rst"), R("rst"), [[0, 64], [1, 16]], A.is_equal, 0, 0, 1.0)
-    aff(R("dd"), R("bc"), [[1, 16], [0, 8], [-1, 16]], A.is_gt, 0, 0)
-    aff(R("dd"), R("dd"), [[0, 16], [-1, 128]], A.not_equal, 0, 1, -1.0)
+    fill(R("rst"), 1.0)
+    fill(R("rst", S_(0, 1024, 16)), 0.0)
+    aff(R("dd"), R("rowc", S_(512, 656)), [[-1, 144]], A.not_equal, 0, 1, 2.0)
+    for r in range(1, 16):
+        aff(R("d2", r), R("dd", S_(r, 128 + r)), [[-1, 128]], A.not_equal, 0, 1, -2.0)
     for i in (0, 1):
         aff(R("sk8", i, blk(0)), R("rowc", blk(3)), [[-16, 4], [0, 2], [-1, 16]], A.not_equal, 64 * i - 64, 1, -1.0)
         for n in (128, 256, 512):
             aff(R("sk8", i, S_(n, 2 * n)), R("sk8", i, S_(0, n)), [[0, n]], A.is_ge, 0, 0)
         aff(R("sk8", i), R("sk8", i), [[-1, 8], [-8, 8], [0, 16]], A.not_equal, -64 * i, 1, 1.0)
-    CST = (-32.0, 4322.0, -1015.5, -64.0, -1024.0, 32.5, 0.0156263, -0.5, 1.0, 1023.75, 1024.0)
-    for i, x in enumerate(CST):
-        if OPT["hf"] == "S" or i < 9:
-            fill(R("cst", S_(i, i + 1)), x)
-
-    def cst(x):
-        return R("cst", S_(CST.index(x), CST.index(x) + 1))
     ts(R("q0"), pm, 1024.0, A.add)
     act(R("Q", 0, blk(2, 256)), R("zl"), F.Copy)
-    spec = OPT["spec"]
     fill(R("one"), 1.0)
     cp(R("pf", S_(0, 1)), R("pidx"))
     for x, pat in enumerate(([[4, 4], [16, 8], [0, 4]], [[0, 4], [16, 8], [4, 4]])):
         iota(R("io", blk(x)), pat, 0)
         for b in range(4):
             ts(R("sp", 4 * x + b), R("io", blk(x)), float(b), A.add, R("pf", S_(0, 1)), A.is_equal)
-    aff(R("Wd"), R("one", S_(0, 32)), [[-1, 32]], A.is_equal, 0, 1)
+    Wd, Wt = R("W2", S_(0, 32), 0), R("W2", S_(0, 32), 1)
+    aff(Wd, R("one", S_(0, 32)), [[-1, 32]], A.is_equal, 0, 1)
     for jj in range(1, 4):
-        aff(R("Wd"), R("Wd"), [[-1, 32]], A.not_equal, -32 * jj, 1, 1.0)
-    aff(R("Wt"), R("one", S_(0, 32)), [[-4, 8], [-32, 4]], A.is_ge, 0, 1)
-    aff(R("Wt"), R("Wt"), [[4, 8], [32, 4]], A.is_ge, 3, -1)
-    ts(R("tm0"), R("tli"), 0.0, A.min, 2.0, A.mult)
-    tt(R("ts0"), R("tli"), R("tm0"), A.add)
-    ts(R("tt", 0), R("ts0"), 16.0, A.add)
-    ts(R("Tf", 0), R("tt", 0), -2063.0, A.add)
-    ts(R("Df", 0), R("dli"), -2047.0, A.add)
+        aff(Wd, Wd, [[-1, 32]], A.not_equal, -32 * jj, 1, 1.0)
+    aff(Wt, R("one", S_(0, 32)), [[-4, 8], [-32, 4]], A.is_ge, 0, 1)
+    aff(Wt, Wt, [[4, 8], [32, 4]], A.is_ge, 3, -1)
+
+    def lists(buf, t, x, i=None):
+        return R(buf, t, blk(x, 256) if i is None else blk(2 * x + i))
+    ts(R("tli"), R("tli"), 4095 - 2 ** 31, A.bitwise_and)
+    ts(lists("Fin", 0, 0), R("tli"), -2047.0, A.add, -2050.0, A.max)
+    ts(R("tt", 0), lists("Fin", 0, 0), 2063.0, A.add)
+    ts(lists("Fin", 0, 1), R("dli"), -2047.0, A.add)
     ts(R("thn"), R("thi"), -1.0, A.mult, -40.5, A.add)
     cp(R("nlim", S_(0, 1)), R("thn"))
-    for k in range(2):
-        c, b = blk(k, 512), tmp("s", 4)
-        ts(R(b), R("sti", c), 0.0, A.min, 2.0, A.mult)
-        tt(R("stw", c), R("sti", c), R(b), A.add)
-    cp(R("scw", S_(0, 1024)), R("sci"))
+    ts(R("sti"), R("sti"), 4095 - 2 ** 31, A.bitwise_and)
+    if OPT["scs"]:
+        iota(R("idi"), [[16, 64]], 0)
+        ts(R("idu"), R("idi"), pm, A.add)
+        for k in range(2):
+            gat("S", R("scw", blk(k, 512)), R("sci"), R("idu", blk(k, 32)))
+    else:
+        cp(R("scw", S_(0, 1024)), R("sci"))
 
     WIN = R("clkw")
-    I, In, I17, I4160n, BO, I2080n = R("I"), R("In"), R("I17"), R("I4160n"), R("BO"), R("I2080n")
+    I, In, I4160n, BO, I2080n, I4096, I64, NG, KTn = [R(n) for n in "I In I4160n BO I2080n I4096 I64 NG KTn".split()]
     sent = {}
 
-    def can(buf, t, c, x):
-        return R(buf, t, off(c, 256 * x))
+    def arrive(t, kind, x):
+        add("R", (0,), None, [], [x], tok="a%d%s" % (t, kind), after=sent[(t - 1, kind)], xl=0.0)
 
-    def arrive(t, h, kind, x):
-        j = sent[(t - 1, h, kind)]
-        add("R", (0,), None, [], [x], tok="a%d%d%s" % (t, h, kind), after=j, xl=ops[j]["xl"])
+    def send(t, kind, src, land):
+        sent[(t, kind)] = add("G", (ISSUE + 256 * size(src) / RATE,), None, [src], [], src=src, land=land, tok="a%d%s" % (t + 1, kind), by=256 * size(src))
 
-    def send(t, h, kind, src, land):
-        sent[(t, h, kind)] = add("G", (100,), None, [src], [], src=src, land=land, tok="a%d%d%s" % (t + 1, h, kind), xl=2.0 * (size(src) - 128))
+    def rows(buf, j, i):
+        return R(buf, blk(2 * j + i))
 
-    def rows(w, h, j, i=0):
-        return S_(2048 * h * (w == 128) + w * j + 128 * i, 2048 * h * (w == 128) + w * j + 128 * i + 128)
+    def spread(x, src, t):
+        if t:
+            return move([(R("Ds", x) + (blk(jj, 32),), src) for jj in range(4)], [src], [R("Ds", x)], "d%d" % x, 256)
+        for q in (0, 1):
+            b = tmp("v", 4)
+            mm([(R(b, blk(i, 256)), R("sp", 4 + 2 * q + i), src, True, True) for i in (0, 1)])
+            act(R("Ds", x, blk(q, 512)), R(b), F.Copy)
 
-    def spread(x, src, h, e):
-        w = size(src)
-        o = R("Ds", x, blk(h, 4 * w))
-        if e == "Y":
-            add("Y", (240,), lambda g, T: [g.sync.dma_start(get(T, o + (blk(jj, 32),)), get(T, src)) for jj in range(4)], [src], [o], tok="d%d%d" % (x, h), lat=2400)
-            return
-        for q in range(w // 128):
-            b, r = tmp("v", 4), 512 // w
-            mm([(R(b, blk(i, w)), R("sp", 4 + r * q + i), src, True, True) for i in range(r)])
-            shift(e, R("Ds", x, blk(h * w // 128 + q, 512)), R(b), 0.0)
+    def member(src, x, eq, pairs):
+        b = {}
+        for y, a in pairs:
+            for q in ([y // 2] if eq == "eqB" else [0, 1]):
+                if q not in b:
+                    b[q] = tmp("v", 4)
+                    mm([(R(b[q], blk(i, 256)), R("sp", 2 * q + i), src, True, True) for i in (0, 1)])
+            tt(R(eq, blk(4 * y + a, 256)), R("Ds", x, blk(a, 256)), R(b[y // 2], blk(y % 2, 256)), A.is_equal)
 
-    def member(src, x, eq, h):
-        w, r = size(src), OPT["dup"]
-        for q in range(w * r // 128):
-            b, nb = tmp("v", 4), 512 // (w * r)
-            mm([(R(b, blk(i, w)), R("sp", nb * q + i // r), src, True, True) for i in range(nb * r)])
-            for i in range(nb):
-                for a in range(0, 4, r):
-                    y = 16 * w * h + w * (4 * (nb * q + i) + a)
-                    tt(R(eq, S_(y, y + r * w)), R("Ds", x, S_(w * (4 * h + a), w * (4 * h + a + r))), R(b, blk(i, r * w)), A.is_equal)
+    def emptied(o, t, x, i):
+        return [(o, lists("Fin", t, x, i), I64), (o, lists("Can", t, x, i), R("I64n"))]
 
     def stageA(t):
+        Tf, Df = lists("Fin", t, 0), lists("Fin", t, 1)
         if t:
-            for h, n, c, _ in parts("pC"):
-                arrive(t, h, "t", R("tt", t, c))
-                arrive(t, h, "c", R("Can", t) if OPT["join"] else can("Can", t, c, 0))
-                if spec and not OPT["join"]:
-                    arrive(t, h, "e", can("Can", t, c, 1))
-            for h, n, c, _ in parts("pT"):
-                arrive(t, h, "f", R("Tf", t, c))
-            for h, n, c, _ in parts("pD"):
-                arrive(t, h, "d", R("Df", t, c))
-            for h, n, c, _ in parts("pZ"):
-                arrive(t, h, "z", R("Q", t, off(c, 512)))
-        n = OPT["ny"]
-        for hb in range(n):
-            gat("V" if hb in OPT["yv"] else "S", R("Y", blk(hb, 4096 // n)), WIN, R("tt", t, blk(hb, 256 // n)))
-        for h, n, c, _ in parts("pT"):
-            add("Y", (120,), lambda g, T, c=c: [g.sync.dma_start(get(T, half(R("PS", off(c, 256 * i)), 1 - i)), get(T, half(R("Tf", t, c), i))) for i in (0, 1)],
-                [R("Tf", t, c)], [R("PS", c), R("PS", off(c, 256))], tok="tp%d" % h, lat=2200)
+            arrive(t, "t", R("tt", t))
+            ts(lists("Can", t, 0), R("tt", t), -2063.0, A.add)
+            arrive(t, "e", lists("Can", t, 1))
+            arrive(t, "f", Tf)
+            arrive(t, "d", Df)
+            arrive(t, "z", R("Q", t, blk(2, 256)))
+        for q in range(OPT["ny"]):
+            gat("S", R("Y", blk(q, 4096 // OPT["ny"])), WIN, R("tt", t, blk(q, 256 // OPT["ny"])))
+        move([(half(R("PS", blk(i, 256)), 1 - i), half(Tf, i)) for i in (0, 1)], [Tf], [R("PS")], "tp", 64)
         for h in (0, 1):
-            b, n = tmp("z", 4), OPT["nm"] // 2
+            b = tmp("v", 4)
             mm([(R(b, S_(i, 512, 4)), I, R("Q", t, blk(4 + h)), True, True) for i in range(4)])
-            for hb in range(n):
+            for y in (0, 1):
                 for q in range(4):
-                    c = S_(2048 * h + 2048 // n * hb + q, 2048 * h + 2048 // n * (hb + 1), 4)
-                    tt(R("MN", c), R("Y", c), R(b, blk(hb, 512 // n)), A.min)
-        early = spec and t
-        for h, n, c, _ in parts("pD"):
-            spread(1, R("Df", t, c), h, "Y" if t else OPT["d0"])
-        for h, n, c, _ in parts("pA"):
-            w = 128 * n
-            if early:
-                spread(0, can("Can", t, c, 1), h, OPT["ds"])
-            member(can("Can", t, c, 0) if early else R("Tf", t, c), 0 if early else 1, "eqA", h)
-            b = tmp("m", 2 * n)
-            lst = [(R(b), I, R("rowc", S_(512, 512 + 2 * w)))]
-            for y in range(4):
-                for a in range(4):
-                    for i in range(n):
-                        e = R("eqA", rows(w, h, 4 * y + a, i))
-                        lst += [(R(b, S_(128 * i + a, 128 * i + 128, 4)), e, R("Wd")), (R(b, S_(w + 128 * i + y, w + 128 * i + 128, 4)), e, R("Wt"))]
-            cuts = list(range(1 + OPT["ce"], len(lst) + 1, OPT["ce"]))
-            for x, fin in enumerate(("Df", "Tf") if early else ()):
-                for i in range(n):
-                    o = R(b, blk(n * x + i))
-                    lst += [(o, R(fin, t, blk(h + i)), R("I64")), (o, can("Can", t, blk(h + i), 1 - x), R("I64n"))]
-            group(lst, *cuts)
-            act(R("cmD", c), R(b, blk(0, w)), F.Sign, bias=cst(-0.5))
-            act(R("cmA", c), R(b, blk(1, w)), F.Sign, bias=cst(-0.5))
-            pD = tmp("m", n)
-            mm(chain(pD, (I, R("Df", t, c)), *turned("cmD", I2080n, h, n)))
-            ts(R("D1", c), R(pD), -2080.0, A.add, -2112.0, A.max)
-            ts(R("D1u", c), R("D1", c), -2048.0, A.max, 2063.0, A.add)
-            ts(R("nk", c), R("D1", c), -2047.5, A.is_le, -0.5, A.add)
-        n = OPT["nx"]
-        for hb in range(n):
-            gat("V" if hb in OPT["xv"] else "S", R("XG", blk(hb, 4096 // n)), WIN, R("D1u", blk(hb, 256 // n)))
-        for hb in range(4):
-            scan(R("xs", blk(hb, 1024)), R("rst"), R("XG", blk(hb, 1024)))
+                    c = S_(2048 * h + 1024 * y + q, 2048 * h + 1024 * y + 1024, 4)
+                    tt(R("MN", c), R("Y", c), R(b, blk(y, 256)), A.min)
+        spread(1, Df, t)
+        if t:
+            spread(0, lists("Can", t, 1), t)
+        member(lists("Can", t, 0) if t else Tf, 0 if t else 1, "eqA", PAIRS)
+        b = tmp("c", 4)
+        lst = [(R(b, blk(i, 32), S_(a, 5 + y, 4 + y - a)), rows("eqA", 4 * y + a, i), R("W2")) for y, a in PAIRS for i in (0, 1)]
+        if t:
+            lst += [m for x in (0, 1) for i in (0, 1) for m in emptied(R(b, blk(i, 32), blk(x, 4)), t, 1 - x, i)]
+        group(lst, 8, 16, 24, 32)
+        act(R("cmD"), R(b, S_(0, 64), blk(0, 4)), F.Sign, bias=-0.5)
+        act(R("cmA"), R(b, S_(0, 64), blk(1, 4)), F.Sign, bias=-0.5)
+        ts(R("D1"), total((I, Df), *turned("cmD", I2080n)), -2080.0, A.add, -2112.0, A.max)
+        ts(R("nk"), R("D1"), -2047.5, A.is_le, -0.5, A.add)
+        ts(R("D1u"), R("D1"), -2048.0, A.max, 2063.0, A.add)
+        for a, y, e in zip((0,) + OPT["xp"], OPT["xp"] + (256,), OPT["xv"]):
+            gat(e, R("XG", S_(16 * a, 16 * y)), WIN, R("D1u", S_(a, y)))
+        for q in range(4):
+            scan(R("xs", blk(q, 1024)), R("rst"), R("XG", blk(q, 1024)))
 
     def stageB(t):
-        for h0, n, c, _ in parts("pK"):
+        Tf = lists("Fin", t, 0)
+        n = OPT["kn"]
+        for h in range(0, 2, n):
             b, w = tmp("m", 2 * n), 128 * n
-            kk, d = R(b, S_(0, w)), R(b, S_(w, 2 * w))
-            lst = [(R(b), I, R("rowc", S_(0, 2 * w)))] + [(R(b, blk(n + i)), R("Q", t, blk(4 + h0 + i)), BO) for i in range(n)]
+            kk, d, c = R(b, blk(0, w)), R(b, blk(1, w)), blk(h, w)
+            lst = [(kk, I, R("rowc", blk(0, w)))] + [(R(b, blk(n + i)), R("Q", t, blk(4 + h + i)), BO) for i in range(n)]
             for i in range(n):
-                x = 2048 * (h0 + i)
+                x, KB = 2048 * (h + i), R("KB", i) if n == 2 else R("K1")
                 lst += [(R(b, S_(w + 128 * i + j, w + 128 * i + 128, 16)), R("Y", S_(x + j, x + 2048, 16)), BO8) for j in range(16)]
-                lst += [(R(b, S_(j, 2 * w, 16)), R("MN", S_(x + j, x + 2048, 16)), R("KB", i, S_(0, 16 * n))) for q in range(4) for j in range(q, 16, 4)]
-            cuts = list(range(1 + n, len(lst), OPT["ck"]))
+                lst += [(R(b, S_(j, 2 * w, 16)), R("MN", S_(x + j, x + 2048, 16)), KB) for q in range(4) for j in range(q, 16, 4)]
+            cuts = list(range(1 + n, len(lst), 8))
             if t:
-                y = cuts[-OPT["mk"]]
-                cuts = [x + 2 * n * (x > y) for x in cuts] + [y + 2 * n]
-                for i in range(n):
-                    lst[y:y] = [(R(b, blk(i)), R("Tf", t, blk(h0 + i)), R("I64")), (R(b, blk(i)), can("Can", t, blk(h0 + i), 0), R("I64n"))]
-            group(lst, *sorted(cuts))
+                lst[cuts[-1]:cuts[-1]] = [m for i in range(n) for m in emptied(R(b, blk(n - 1 - i)), t, 0, h + n - 1 - i)]
+                cuts.append(cuts[-1] + 2 * n)
+            group(lst, *cuts)
             rs, back = R("rst", S_(0, w)), S_(c.stop - 1, c.start - 1 if c.start else None, -1)
             scan(R("sk", c), rs, kk)
             scan(R("sk2", back), rs, R("sk", back))
             tt(R("oh", c), R("sk2", c), kk, A.is_equal)
-            shift(OPT["dst"], R("dst", c), d, -2040.0)
-        for h, n, c, l in parts("pB"):
-            Tf, D1 = R("Tf", t, c), R("D1", c)
-            d = tmp("m", n)
-            mm([m for i in range(n) for m in chain(d, (R("dst", blk(h + i)), In, blk(i)), (R("cmA", blk(h + i)), I2080n, blk(i)))])
-            act(R("FC", c), R(d), F.Sign, bias=R("nlim", S_(t, t + 1)), scale=-1.0)
-            FC, XS = R("FC", c), R("Q", t, c)
-            o1, x, p = tmp("m", n), tmp("m", n), tmp("m", n)
-            mm([(R(o1, blk(i)), R("oh", blk(h + i)), I, True, True) for i in range(n)])
-            tt(R("Q", t, off(c, 256)), Tf, R(o1), A.mult)
-            mm(chain(x, (In, R("nk", c)), (R("I64"), FC), *turned("oh", R("I64"), h, n)))
-            shift(OPT["xs"], XS, R(x), 0.0)
-            L, w = tmp("m", 1), 8 * n
-            y = 32 + w
-            mm(chain(L, *([(R("Zs", S_(15 - r, 143 - r)), R("Q", t, S_(128 * h + r, 128 * h + 16 * y, 16)), S_(0, y)) for r in range(16)] +
-                          [(I, R("LC", S_(0, y)), S_(0, y))])))
-            X, E, U = R(L, S_(0, w)), R(L, S_(16, 16 + w)), R(L, S_(32, 32 + w))
-            both = blk(h, 2 * w)
-            lo, hi = S_(both.start, both.start + w), S_(both.start + w, both.stop)
-            ts(R("AS", l), X, -967.5, A.is_gt, 16384.0, A.mult)
-            tt(R("nu", lo), R("AS", l), E, A.add)
-            tt(R("nu", hi), R("nu", lo), U, A.max)
-            ts(R("npr", l), X, -968.0, A.is_equal, -1056.0, A.mult)
-            ts(R("nlu", l), E, 16.0, A.add)
-            ts(R("nv", both), R("nu", both), 1023, A.bitwise_and)
-            cp(R("wu", l), R("nv", hi))
-            gat(OPT["sw"], R("sw", c), R("stw"), R("wu", l), -2047.0)
-            gat(OPT["cw"], R("cw", c), R("scw", S_(0, 1024)), R("wu", l), -2047.0)
-            gat(OPT["ys"], R("ysb", c), WIN, R("nlu", l))
-            tt(R("PV", l), R("nv", lo), R("npr", l), A.add)
-            b = tmp("m", n)
-            mm(chain(b, (BO, XS), (R("BO128n"), FC)))
-            act(R("NG", c), R(b), F.Relu, bias=cst(4322.0), scale=-4.0)
-            act(R("NA", c), R(b), F.Relu, bias=cst(-1015.5))
-            mm(chain(p, (I, Tf), *(turned("cmA", I2080n, h, n) + turned("oh", I4160n, h, n))))
-            act(R("KTn", c), R(p), F.Sign, bias=cst(32.5), scale=-1.0)
-            act(R("T1s", c), R(p), F.Relu, bias=cst(-32.0))
-            if t + 1 < NV:
-                b, k = tmp("m", n), OPT["pB"] * t + h
-                mm(chain(b, (In, D1), (R("BO128n"), FC)))
-                act(R("acr", c), R(b), F.Relu, bias=cst(-64.0), scale=1.0 / 64, acc=R("asum", S_(k, k + 1)))
+            act(R("dst", c), d, F.Copy, bias=-2040.0)
+        d = tmp("m", 2)
+        mm([m for i in (0, 1) for m in chain(d, (R("dst", blk(i)), In, blk(i)), turned("cmA", I2080n)[i])])
+        act(R("FC"), R(d), F.Sign, bias=R("nlim", S_(t, t + 1)), scale=-1.0)
+        FC, XS, o1 = R("FC"), R("Q", t, blk(0, 256)), tmp("m", 2)
+        mm([(R(o1, blk(i)), R("oh", blk(i)), I, True, True) for i in (0, 1)])
+        tt(R("Q", t, blk(1, 256)), Tf, R(o1), A.mult)
+        cp(XS, total((In, R("nk")), (I64, FC), *turned("oh", I64)))
+        L = tmp("m", 1)
+        mm(chain(L, *([(R("Zs", S_(15 - r, 143 - r)), R("Q", t, S_(r, 768, 16)), S_(0, 48)) for r in range(16)] + [(I, R("LC"), S_(0, 48))])))
+        X, E, U = [R(L, blk(i, 16)) for i in range(3)]
+        lo, hi = blk(0, 16), blk(1, 16)
+        ts(R("AS"), X, -967.5, A.is_gt, 16384.0, A.mult)
+        tt(R("nu", lo), R("AS"), E, A.add)
+        tt(R("nu", hi), R("nu", lo), U, A.max)
+        ts(R("npr"), X, -968.0, A.is_equal, -1056.0, A.mult)
+        ts(R("nlu"), R("nu", lo), 16.0 - 16384.0, A.add)
+        ts(R("nv"), R("nu"), 1023, A.bitwise_and)
+        cp(R("wu"), R("nv", hi))
+        gat("V", R("sw"), R("sti"), R("wu"), -2047.0, -2050.0)
+        gat("S", R("cw"), R("scw", S_(0, 1024)), R("wu"), -2047.0)
+        gat("S", R("ysb"), WIN, R("nlu"))
+        tt(R("PV"), R("nv", lo), R("npr"), A.add)
+        ts(NG, total((BO, XS), (R("BO128n"), FC)), 1080.5, A.is_lt, 2.0, A.mult)
+        p = total((I, Tf), *(turned("cmA", I2080n) + turned("oh", I4160n)))
+        act(KTn, p, F.Sign, bias=32.5, scale=-1.0)
+        act(R("T1s"), p, F.Relu, bias=-32.0)
         if t + 1 < NV:
+            act(R("acr"), total((In, R("D1")), (R("BO128n"), FC)), F.Relu, bias=-64.0, scale=1.0 / 64, acc=R("asum", S_(t, t + 1)))
             a = tmp("m", 1)
-            mm(chain(a, *[(R("bo32"), R("asum", S_(i, i + 1)), S_(0, 1)) for i in range(OPT["pB"] * (t + 1))]))
-            cp(R("ai"), R(a, S_(0, 1)))
+            mm(chain(a, (R("bo32"), R("asum", S_(t, t + 1)), S_(0, 1))))
+            if t:
+                ts(R("ai"), R("a31"), R(a, S_(0, 1)), A.add)
+            else:
+                cp(R("ai"), R(a, S_(0, 1)))
             ts(R("a31"), R("ai"), 31, A.bitwise_and)
             ts(R("nlim", S_(t + 1, t + 2)), R("a31"), -8.0, A.mult, R("thn"), A.add)
 
-    def out(name, buf, c, lat=2500):
-        add("Y", (60,), lambda g, T: g.sync.dma_start(T[name][:, c], get(T, R(buf, c))), [R(buf, c)], [], tok="so", lat=lat)
-
     def stageC(t):
         last = t == NV - 1
-        for h, n, c, _ in parts("pC"):
-            NG = R("NG", c)
-            p0, p1, tc, dc = tmp("m", n), tmp("m", n), can("sC", t, c, 0), can("sC", t, c, 1)
-            mm(chain(p1, (I2080n, R("one", S_(0, 128 * n))), (I, R("Tf", t, c)), (I2080n, R("KTn", c)), (I4160n, NG)))
-            if spec and not last:
-                b = tmp("m", n)
-                mm(chain(b, (BO, R("Q", t, off(c, 256)))))
-                tt(R("eqn", c), R("sw", c), R(b), A.is_equal)
-            mm(chain(p0, (I17, NG), (R("I16"), R("KTn", c)), *[(R("I69n"), R("eqn", c))] * (spec and not last)))
-            tt(R("C1t", c), R("sw", c), R(p0), A.min)
-            tt(tc, R("C1t", c), R(p1), A.max)
-            if not last:
-                ts(R("stt", t, c), tc, -2063.0, A.max, 2063.0, A.add)
-                send(t, h, "t", R("stt", t, c), R("tt", t + 1, c))
-            if spec and not last:
-                p0, p1 = tmp("m", n), tmp("m", n)
-                mm(chain(p1, (I, R("D1", c)), (I4160n, NG)))
-                mm(chain(p0, (R("I4096"), NG), (R("I4096"), R("nk", c))))
-                tt(R("C1", c), R("cw", c), R(p0), A.min)
-                tt(dc, R("C1", c), R(p1), A.max)
-                if not OPT["join"]:
-                    send(t, h, "e", dc, can("Can", t + 1, c, 1))
-            if not last:
-                y = S_(0, 512) if OPT["join"] else c
-                send(t, h, "c", R("sC", t, y), R("Can", t + 1, y))
-        for h, n, c, _ in parts("pT"):
-            w = 128 * n
-            for i in (0, 1):
-                o, x = half(R("PS", off(c, 256 * i)), i), half(R("sw", c), i)
-                if OPT["ps"][i] == "G":
-                    aff(o, x, [[0, w]], A.is_ge, 0, 0)
-                elif OPT["ps"][i] == "Y":
-                    add("Y", (60,), lambda g, T, o=o, x=x: g.sync.dma_start(get(T, o), get(T, x)), [x], [o], tok="tq%d%d" % (h, i), lat=2200)
-                else:
-                    shift(OPT["ps"][i], o, x, 0.0)
-            r = 512 // w
-            for q in range(16 // r):
-                b = tmp("s", 4)
-                mm([(R(b, blk(i, w)), R("sk8", (r * q + i) // 8, blk((r * q + i) % 8)), R("PS", off(c, 256 * ((r * q + i) // 8))), True, True) for i in range(r)])
-                act(R("fC", S_(2048 * h + 512 * q, 2048 * h + 512 * q + 512)), R(b), F.Tanh, bias=cst(0.0156263), scale=16.0)
-            b = tmp("m", n)
-            mm([(R(b, S_(128 * i + 64 * (j // 8) + j % 8, 128 * i + 64 * (j // 8) + 64, 8)), R("fC", rows(w, h, j, i)), BO8, True, True)
-                for j in range(16) for i in range(n)], *range(OPT["cc"] * n, 16 * n, 4 * n))
-            act(R("rC", c), R(b), F.Copy, bias=-192.49, scale=-1.0)
-            act(R("rC", off(c, 256)), R(b), F.Copy, bias=193.0)
-            p = tmp("m", n)
-            mm(chain(p, (R("I8192"), R("NG", c)), (R("I4096n"), R("KTn", c)), *(turned("rC", R("I8192"), h, n) + turned("rC", R("I8192"), h, n, 2))))
-            fin = R("sT", t, c)
-            for x in ([c] if OPT["pT"] >= OPT["pC"] else [blk(0), blk(1)]):
-                tt(R("sT", t, x), can("sC", t, x, 0), R(p, off(x, -c.start)), A.min)
-            if last:
-                ts(R("ot", c), fin, 2047.0, A.add, -1.0, A.max)
-                out("yt", "ot", c)
-            else:
-                send(t, h, "f", fin, R("Tf", t + 1, c))
-        for h, n, c, _ in parts("pD"):
-            NG = R("NG", c)
-            member(R("cw", c), 1, "eqB", h)
-            b, w = tmp("m", n), 128 * n
-            lst = [m for y in range(4) for i in range(n) for m in
-                   chain(b, *[(R("eqB", rows(w, h, 4 * y + a, i)), R("Wt"), S_(128 * i + y, 128 * i + 128, 4)) for a in range(4)])]
-            mm(lst, *range(4 * n, 16 * n, 4 * n))
-            if spec and not last:
-                act(R("cmB", c), R(b), F.Relu, bias=cst(1.0), scale=-1.0)
-                p = tmp("m", n)
-                mm(chain(p, (R("I4096"), NG), (R("I4096n"), R("nk", c)), *turned("cmB", R("I4096"), h, n)))
-                for x in ([c] if OPT["pD"] >= OPT["pC"] else [blk(0), blk(1)]):
-                    tt(R("sd", t, x), can("sC", t, x, 1), R(p, off(x, -c.start)), A.min)
-            else:
-                act(R("cmB", c), R(b), F.Sign, scale=-1.0)
-                p0, p1 = tmp("m", n), tmp("m", n)
-                mm(chain(p1, (I, R("D1", c)), (I4160n, NG)))
-                mm(chain(p0, (R("I4096"), NG), (R("I4096"), R("nk", c)), *turned("cmB", R("I4096"), h, n)))
-                tt(R("C1", c), R("cw", c), R(p0), A.min)
-                tt(R("sd", t, c), R("C1", c), R(p1), A.max)
-            if last:
-                ts(R("od", c), R("sd", t, c), 2047.0, A.add, -1.0, A.max)
-                out("yd", "od", c)
-            else:
-                send(t, h, "d", R("sd", t, c), R("Df", t + 1, c))
-        for h, n, c, _ in parts("pZ"):
-            NG, Z, w = R("NG", c), R("Q", t, off(c, 512)), 128 * n
-            ys, c0, b, c3 = R("ysb", c), tmp("m", n), tmp("m", 2 * n), tmp("m", n)
-            zy = blk(h, 2 * w)
-            z0, z1 = R("zy", S_(zy.start, zy.start + w)), R("zy", S_(zy.start + w, zy.stop))
-            mm(chain(c0, (R("Ih"), ys), (I4160n, NG), (R("Ih"), R("xs", S_(16 * c.start + 15, 16 * c.stop, 16)))))
-            mm(chain(b, (I, Z, blk(0, w)), (I4160n, NG, blk(0, w))) + chain(b, (I, ys, blk(1, w)), (I4160n, R("NA", c), blk(1, w))))
-            if OPT["hf"] == "V":
-                ts(R("hf", c), R(c0), 1023.75, A.add, 1024.0, A.max)
-                act(R("zy", zy), R(b), F.Relu)
-            else:
-                act(R("hf", c), R(c0), F.Relu, bias=cst(1023.75))
-                act(z0, R(b, blk(0, w)), F.Relu, bias=cst(1024.0))
-                act(z1, R(b, blk(1, w)), F.Relu)
-            mm(chain(c3, (I, Z), (In, z0), (In, z1), (I, R("hf", c))))
-            act(R("oz", c) if last else R("sz", t, c), R(c3), F.Abs, bias=cst(-1024.0) if OPT["hf"] == "V" else 0.0)
-            if last:
-                out("yz", "oz", c)
-            else:
-                send(t, h, "z", R("sz", t, c), R("Q", t + 1, off(c, 512)))
+        tc, dc, sT, sd = [lists(b, t, x) for b in ("sC", "sF") for x in (0, 1)]
+        p1 = total((I2080n, R("one")), (I, lists("Fin", t, 0)), (I2080n, KTn), (I4160n, NG))
+        if not last:
+            tt(R("eqn"), R("sw"), total((BO, R("Q", t, blk(1, 256)))), A.is_equal)
+        tt(R("C1t"), R("sw"), total((R("I17"), NG), (R("I16"), KTn), *[(R("I69n"), R("eqn"))] * (not last)), A.min)
+        tt(tc, R("C1t"), p1, A.max)
+        if not last:
+            ts(R("stt", t), tc, -2062.0, A.max, 2063.0, A.add)
+            send(t, "t", R("stt", t), R("tt", t + 1))
+            p1 = total((I, R("D1")), (I4160n, NG))
+            tt(R("C1"), R("cw"), total((I4096, NG), (I4096, R("nk"))), A.min)
+            tt(dc, R("C1"), p1, A.max)
+            send(t, "e", dc, lists("Can", t + 1, 1))
+        for i in (0, 1):
+            o, x = half(R("PS", blk(i, 256)), i), half(R("sw"), i)
+            move([(o, x)], [x], [o], "tq%d" % i, 32)
+        for q in range(8):
+            b = tmp("v", 4)
+            mm([(R(b, blk(i, 256)), R("sk8", q // 4, blk(2 * (q % 4) + i)), R("PS", blk(q // 4, 256)), True, True) for i in (0, 1)])
+            act(R("fC", blk(q, 512)), R(b), F.Tanh, bias=0.0156263, scale=16.0)
+        b = tmp("m", 2)
+        mm([(R(b, S_(128 * i + 64 * (j // 8) + j % 8, 128 * i + 64 * (j // 8) + 64, 8)), rows("fC", j, i), BO8, True, True)
+            for j in range(16) for i in (0, 1)], 16, 24)
+        act(R("rC", blk(0, 256)), R(b), F.Copy, bias=-192.49, scale=-1.0)
+        act(R("rC", blk(1, 256)), R(b), F.Copy, bias=193.0)
+        tt(sT, tc, total((R("I8192"), NG), (R("I4096n"), KTn), *(turned("rC", R("I8192")) + turned("rC", R("I8192"), 2))), A.min)
+        if last:
+            ts(R("ot"), sT, 2047.0, A.add, -1.0, A.max)
+            out("yt", "ot", 256)
+        else:
+            send(t, "f", sT, lists("Fin", t + 1, 0))
+        member(R("cw"), 1, "eqB", sorted(PAIRS))
+        b = tmp("m", 2)
+        mm([m for y in range(4) for i in (0, 1) for m in
+            chain(b, *[(rows("eqB", 4 * y + a, i), Wt, S_(128 * i + y, 128 * i + 128, 4)) for a in range(4)])], 8, 16, 24)
+        if last:
+            act(R("cmB"), R(b), F.Sign, scale=-1.0)
+            p1 = total((I, R("D1")), (I4160n, NG))
+            tt(R("C1"), R("cw"), total((I4096, NG), (I4096, R("nk")), *turned("cmB", I4096)), A.min)
+            tt(sd, R("C1"), p1, A.max)
+            ts(R("od"), sd, 2047.0, A.add, -1.0, A.max)
+            out("yd", "od", 256)
+        else:
+            act(R("cmB"), R(b), F.Relu, bias=1.0, scale=-1.0)
+            tt(sd, dc, total((I4096, NG), (R("I4096n"), R("nk")), *turned("cmB", I4096)), A.min)
+            send(t, "d", sd, lists("Fin", t + 1, 1))
+        Z, ys = R("Q", t, blk(2, 256)), R("ysb")
+        ts(R("hf"), total((R("I15"), ys), (In, Z), (I4160n, NG), (R("Ih"), R("xs", S_(15, 4096, 16)))), 1535.75, A.add, 1024.0, A.max)
+        act(R("oz") if last else R("sz", t), total((I, Z), (In, ys), (R("I256"), NG), (I, R("hf"))), F.Abs, bias=-1536.0)
+        if last:
+            out("yz", "oz", 256)
+        else:
+            send(t, "z", R("sz", t), R("Q", t + 1, blk(2, 256)))
 
     def stageD(t):
-        b, PV = tmp("m", 2), R("PV")
-        mm([(R(b, S_(r, 256, 16)), R("dd", blk(r)), PV, True, True) for r in range(16)])
-        ts(R("eqP"), R(b), 0.0, A.is_equal)
-        c = tmp("m", 1)
-        mm(chain(c, (I, PV, S_(0, 16)), *[(R("I4096"), R("eqP", S_(r, 256, 16)), S_(0, 16)) for r in range(16)]))
+        b, c, PV = tmp("m", 2), tmp("m", 1), R("PV")
+        mm([(R(b, S_(r, 256, 16)), R("d2", r) if r else I, PV, True, True) for r in range(16)])
+        tt(R("eqP"), R("Mk"), R(b), A.is_equal)
+        scan(R("eqS"), R("rst", S_(0, 256)), R("eqP"))
+        mm(chain(c, (I, PV, S_(0, 16)), (I4096, R("eqS", S_(15, 256, 16)), S_(0, 16))))
         ts(R("PLu", S_(0, 32, 2)), R(c, S_(0, 16)), 1056.0, A.add, R("q0"), A.min)
         for c in range(16):
             o, offs, src = R("scw"), R("PLu", S_(2 * c, 2 * c + 1)), R("T1s", blk(c, 16))
             add("V", (60, 0, 0, 16), lambda g, T, o=o, offs=offs, src=src: g.vector.tensor_scalar(
                 get(T, o).indirect(get(T, offs)), get(T, src), 1.0, -1.0, A.mult, A.add), [offs, src], [o])
         if t == NV - 1:
-            out("ys", "scw", S_(0, 1024), 4500)
+            out("ys", "scw", 1024)
 
     for t in range(NV):
         for s, f in (("A", stageA), ("B", stageB), ("C", stageC), ("D", stageD)):
@@ -581,13 +495,12 @@ def depend(ops):
         for x, wr in [(x, False) for x in o["r"]] + [(x, True) for x in o["w"]]:
             sp = tuple(s[:3] for s in span(x))
             acc[(x[0], sp)] = acc.get((x[0], sp), False) or wr
-        rd = {(x[0], tuple(s[:3] for s in span(x))) for x in o["r"]}
         for (name, sp), wr in acc.items():
             for j, sj, wj in hist.get(name, ()):
                 if j != i and name in TEMP and o["e"] == ops[j]["e"] == "P":
                     seq.add(j)
                 elif j != i and (wj or wr) and meet(sp, sj):
-                    (seq if OPT["ww"] and (name, sp) not in rd and o["e"] == ops[j]["e"] in "VS" and "tok" not in ops[j] else pw).add(j)
+                    pw.add(j)
         for (name, sp), wr in acc.items():
             h = hist.setdefault(name, [])
             if wr:
@@ -602,17 +515,18 @@ def schedule(ops):
     pred, succ = [], [[] for _ in range(n)]
     for i, o in enumerate(ops):
         pred.append([(j, WAKE if ops[j]["e"] != o["e"] else SELF) for j in o["pw"]] + [(j, 0.0) for j in o["seq"]] +
-                    ([(o["after"], REMOTE + o["xl"])] if "after" in o else []))
+                    ([(o["after"], REMOTE)] if "after" in o else []))
         for j, l in pred[i]:
             succ[j].append((i, l))
-    fin = [o["d"] + o.get("lat", 0.0) for o in ops]
+    fin = [o["d"] + LAT * o.get("lat", 0.0) for o in ops]
     steps, key = {}, [None] * n
     for i, o in enumerate(ops):
-        if o["n"] in PLAN:
-            steps.setdefault((o["n"], int(o["g"][1])), []).append(i)
+        if o["n"] in PLAN or o["n"] + o["g"][1:] in PLAN:
+            steps.setdefault((o["n"], int(o["g"][1:] or 0)), []).append(i)
     for (name, t), l in steps.items():
+        a, b = PLAN.get(name + str(t)) or PLAN[name]
         for k, i in enumerate(l):
-            key[i] = 1000 * (t * PLAN["P"] + PLAN[name][0] + PLAN[name][1] * k / max(1, len(l) - 1))
+            key[i] = 1000 * (t * PLAN["P"] + a + b * k / max(1, len(l) - 1))
     for i in range(n - 1, -1, -1):
         if key[i] is None:
             key[i] = min([key[k] - PLAN["mu"] * (fin[i] + l) for k, l in succ[i]] or [1000 * PLAN["P"] * (int(ops[i]["g"][1:] or 0) + 1.3)])

import math
from concourse.mybir import AluOpType, ActivationFunctionType

A, F = AluOpType, ActivationFunctionType
NV = 5
f32, f16, b16, i32, u16 = "float32", "float16", "bfloat16", "int32", "uint16"
SCRATCH, ALIAS = {}, {}


def _decl(text, d, lead):
    for w in text.split():
        n, s = w.split(":")
        SCRATCH[n] = ("sbuf", [128] + lead + [int(x) for x in s.split(",")], d)


_decl("tli:256 dli:256 thi:1 sci:1024 sti:1024 pidx:1 pmi:1 ai:1 a31:1 nu:32 nv:32 idi:64", i32, [])
_decl("scw:1040 pmf:1 on32:128 boa:128 bo32:128 id32:128 io:256 pf:8 q0:1 thn:1 nlim:8 asum:8 T1s:256 od:256 ot:256 oz:256 "
      "sk:256 sk2:256 AS:16 npr:16 C1:256 C1t:256", f32, [])
_decl("LC:48 PV:16 PS:512 D1:256 cw:256 sw:256 hf:256 dst:256 Ds:2,1024", f16, [])
_decl("clkw:4112 Mk:256 sk8:2,1024 dd:144 d2:16,128 rst:1024 rowc:768 Zs:144 KB:2,32 K1:16 eqP:256 eqS:256 zl:256 "
      "eqA:4096 eqB:4096 fC:4096 Y:4096 MN:4096 XG:4096 xs:4096 nk:256 oh:256 cmA:256 cmB:256 rC:512 FC:256 NG:256 "
      "KTn:256 ysb:256 acr:256 cmD:256 eqn:256 one:256 sp:8,128 W2:32,2", b16, [])
_decl("PLu:32 D1u:256 nlu:16 wu:16 idu:64", u16, [])
_decl("tt:256 stt:256", u16, [NV])
_decl("Fin:512 Can:512 Q:768 sF:512 sC:512 sz:256", f16, [NV])
KS = (("In", -1), ("I4160n", -4160), ("I17", 131072), ("I16", 65536), ("Ih", 0.5), ("I64", 64), ("I64n", -64), ("I4096", 4096),
      ("I4096n", -4096), ("I8192", 8192), ("I2080n", -2080), ("I69n", -69632), ("I15", 1.5), ("I256", 256), ("BO128n", -128))
SCRATCH["kb"] = ("sbuf", [128, len(KS) + 2, 128], b16)
for _i, _n in enumerate(["I", "BO"] + [k[0] for k in KS]):
    ALIAS[_n] = ("kb", _i)
for _i in range(8):
    SCRATCH["ps%d" % _i] = ("psum", [128, 512] if _i < 7 else [128, 64, 8], f32)
BANKS = {"v": tuple(range(7)), "m": tuple(range(6, -1, -1)), "c": (7,)}
LOADS = ("tl", "dl", "z", "th", "clk", "st", "sc")
OPT = dict(scs=1, kn=2, ny=4, xp=(48, 96, 144, 192, 220), xv="SSSSSV", lq="YYYYSYY", oq=("yz",))
SEMAPHORES = ["sv", "ss", "sp", "sg", "so", "ls", "tp", "tq0", "tq1", "d0", "d1"] + ["l_" + n for n in LOADS]
SEMAPHORES += ["a%d%s" % (t, k) for t in range(1, NV) for k in "tefdz"]
CYC, PEC, OVV, OVS, WAKE, SELF, REMOTE, LOOK, LOOKB, ROUNDS = 0.83, 0.40, 10.0, 50.0, 55.0, 70.0, 2300.0, 0.3, 0.1, 2
GAT, SCA, PEM, PEG, LAT, ISSUE, RATE, LOCAL, START = 1.62, 3.8, 9.0, 17.0, 1.0, 250.0, 75.0, 700.0, 150.0
PLAN = {'P': 23.5, 'mu': 3.4, 'VsFC': (23.1, -0.4), 'Gsk8': (16.6, -5.4), 'ScmBC': (23.6, 0.1), 'P~kbB': (2.0, 26.5), 'SysbB': (20.5, -3.5),
        'VCanA': (-15.0, 4.4), 'VnuB': (15.3, 6.8), 'VC1C': (-4.9, 7.7), 'ST1sB4': (14.3, 1.9), 'Skb': (-17.8, 19.2), 'ScwB': (-8.3, -1.8),
        'P~YB': (-10.9, 5.0), 'VsFC0': (18.9, 0.9), 'SXGA0': (-18.7, -3.3), 'VPVB': (5.5, 1.0), 'Gpidx': (-50.3, -3.0), 'Vone': (-51.2, -0.5),
        'Vthn': (15.2, -3.5), 'Vq0': (2.9, -1.5), 'VswB4': (2.6, -0.5), 'VPVB4': (6.3, -1.8), 'VscwD4': (21.6, 8.7), 'VC1tC0': (-4.1, -2.4),
        'VsttC': (-4.5, -0.2), 'Vclkw': (-20.4, 2.0), 'P~spC': (15.4, 0.0), 'Vtli': (-49.5, 2.0), 'Von32': (-21.3, 0.2), 'Gbo32': (-13.8, 1.5),
        'Gboa': (-17.5, 0.5), 'Vrowc': (-4.8, 0.0), 'P~kbC0': (-12.3, -2.9), 'Vidu': (-10.3, 0.5), 'VeqSD': (3.9, 0.5)}
PAIRS = [(q + y, q + (x ^ y)) for q in (0, 2) for x in (0, 1) for y in (0, 1)] + [(y, a) for y in range(4) for a in range(4) if y // 2 != a // 2]
TEMP, PLACE = {}, {}


def R(name, *ix):
    return (ALIAS[name][0], (ALIAS[name][1],) + ix) if name in ALIAS else (name, ix)


def S_(a, b, st=None):
    return slice(a, b, st)


def blk(i, n=128):
    return slice(n * i, n * i + n)


def psum(x):
    return x[0] in TEMP


def get(T, x):
    if psum(x):
        bank, b0 = PLACE[x[0]][:2]
        if TEMP[x[0]][0] == "c":
            return T["ps%d" % bank][(slice(None),) + x[1]]
        a, b, st = (x[1][0] if x[1] else slice(None)).indices(128 * TEMP[x[0]][1])
        return T["ps%d" % bank][:, 128 * b0 + a:128 * b0 + b:st]
    return T[x[0]][(x[2:] or (slice(None),)) + x[1] + (slice(None),) * (len(SCRATCH[x[0]][1]) - 1 - len(x[1]))]


def half(x, i):
    return x + (blk(i, 64),)


def span(x):
    out = []
    for d, n in enumerate(SCRATCH[x[0]][1][1:] if not psum(x) else [64, 8] if TEMP[x[0]][0] == "c" else [128 * TEMP[x[0]][1]]):
        i = x[1][d] if d < len(x[1]) else slice(None)
        if isinstance(i, int):
            out.append((i, i + 1, 1, 1))
        else:
            r = range(*i.indices(n))
            out.append((min(r[0], r[-1]), max(r[0], r[-1]) + 1, abs(r.step), len(r)))
    return out


def size(x):
    n = 1
    for s in span(x):
        n *= s[3]
    return n


def meet(p, q):
    return all(a[0] < b[1] and b[0] < a[1] and (a[0] - b[0]) % math.gcd(a[2], b[2]) == 0 for a, b in zip(p, q))


def cover(p, q):
    return all(a[0] <= b[0] and b[1] <= a[1] and b[2] % a[2] == 0 and (a[0] - b[0]) % a[2] == 0 for a, b in zip(p, q))


def two(*xs):
    return all(not psum(x) and SCRATCH[x[0]][2] in (f16, b16, u16) for x in xs)


def program():
    ops, lab = [], [""]

    def tmp(role, n):
        name = "~%d" % len(TEMP)
        TEMP[name] = (role, n)
        return name

    def add(e, c, fn, r, w, **kw):
        c = c + (0,) * (6 - len(c))
        d = c[0] + CYC * (c[1] + GAT * c[2] + SCA * c[3]) + PEM * c[4] + PEC * c[5]
        r = [x for x in r if isinstance(x, tuple)]
        name = "" if not w else "~" + r[0][0] if psum(w[0]) else w[0][0]
        ops.append(dict(kw, g=lab[0], n=e + name + lab[0][:1], e=e, c=c, d=d, fn=fn, r=r, w=w))
        return len(ops) - 1

    def val(T, x):
        return get(T, x) if isinstance(x, tuple) else x

    def ts(o, i, s1, op0, s2=None, op1=None):
        def fn(g, T):
            a = (get(T, o), get(T, i), val(T, s1), val(T, s2), op0)
            return g.vector.tensor_scalar(*(a if op1 is None else a + (op1,)))
        add("V", (OVV, max(64, size(o) * (0.5 if two(o, i) else 1))), fn, [i, s1, s2], [o])

    def tt(o, a, b, op):
        add("V", (OVV, max(64, size(o) * (1 if psum(a) or psum(b) else 2))),
            lambda g, T: g.vector.tensor_tensor(get(T, o), get(T, a), get(T, b), op), [a, b], [o])

    def cp(o, i):
        add("V", (OVV, max(64, size(o) * (0.5 if two(o, i) else 1))), lambda g, T: g.vector.tensor_copy(get(T, o), get(T, i)), [i], [o])

    def fill(o, v):
        add("V", (OVV, max(64, size(o) * (0.5 if two(o) else 1))), lambda g, T: g.vector.memset(get(T, o), v), [], [o])

    def scan(o, a, b):
        add("V", (OVV, max(64, size(o) * (0.5 if two(o, a, b) else 1))),
            lambda g, T: g.vector.tensor_tensor_scan(get(T, o), get(T, a), get(T, b), 0.0, A.mult, A.max), [a, b], [o])

    def act(o, i, func, bias=0.0, scale=1.0, acc=None):
        def fn(g, T):
            kw = {} if acc is None else {"accum_out": get(T, acc)}
            return g.scalar.activation(get(T, o), get(T, i), func, bias=val(T, bias), scale=scale, **kw)
        add("S", (OVS, max(64, size(o))), fn, [i, bias], [o] + ([] if acc is None else [acc]))

    def gat(e, o, win, offs, shift=None, least=None):
        def fn(g, T):
            x = get(T, win).indirect(get(T, offs))
            if e == "S":
                return g.scalar.activation(get(T, o), x, F.Copy, bias=shift or 0.0)
            return g.vector.tensor_copy(get(T, o), x) if shift is None else g.vector.tensor_scalar(get(T, o), x, shift, least, A.add, A.max)
        add(e, (60, 0, size(o)), fn, [win, offs], [o])

    def mm(lst, *cuts):
        cuts = [c for c in cuts if 0 < c < len(lst)]
        if cuts:
            mm(lst[:cuts[0]])
            return mm(lst[cuts[0]:], *[c - cuts[0] for c in cuts[1:]])

        def fn(g, T):
            x = None
            for o, l, r, a, b in lst:
                x = g.tensor.matmul(get(T, o), get(T, l), get(T, r), a, b)
            return x
        d = sum(max(64, size(m[0])) * (4 if SCRATCH[m[1][0]][2] == f32 else 1) for m in lst)
        add("P", (PEG, 0, 0, 0, len(lst), d), fn, [m[1] for m in lst] + [m[2] for m in lst], [m[0] for m in lst], open=not lst[-1][4])

    def group(lst, *cuts):
        mm([m + (i == 0, i == len(lst) - 1) for i, m in enumerate(lst)], *cuts)

    def chain(b, *terms):
        return [(R(b, *m[2:]), m[0], m[1], i == 0, i == len(terms) - 1) for i, m in enumerate(terms)]

    def total(*terms):
        b = tmp("m", 2)
        mm(chain(b, *terms))
        return R(b)

    def turned(buf, k, x=0):
        return [(R(buf, blk(x + i)), k, blk(i)) for i in (0, 1)]

    def dma(q, pairs, r, w, tok, kib):
        add(q, (len(pairs) * START,), lambda g, T: [(g.sync if q == "Y" else g.scalar).dma_start(o(T), i(T)) for o, i in pairs], r, w,
            tok=tok, lat=1200 + 1024 * kib / LOCAL, nd=len(pairs))

    def move(pairs, r, w, tok, kib):
        dma("Y", [(lambda T, o=o: get(T, o), lambda T, i=i: get(T, i)) for o, i in pairs], r, w, tok, kib)

    for name, o, src, kib in (("clk", R("clkw", S_(16, 4112)), "clk", 2048), ("tl", R("tli"), "tl", 128), ("dl", R("dli"), "dl", 128),
                              ("z", R("zl"), "z0", 64), ("th", R("thi"), "th", 16), ("st", R("sti"), "st", 1024), ("sc", R("sci"), "sc", 1024)):
        dma(OPT["lq"][LOADS.index(name)], [(lambda T, o=o: get(T, o), lambda T, src=src: T[src][:, :])], [], [o], "l_" + name, kib)

    def out(name, buf, n):
        dma("S" if name in OPT["oq"] else "Y", [(lambda T: T[name][:, :], lambda T: get(T, R(buf, S_(0, n))))], [R(buf, S_(0, n))], [], "so", n)

    def iota(o, pat, base, cm=0):
        kw = {} if SCRATCH[o[0]][2] == i32 else {"allow_small_or_imprecise_dtypes": True}
        add("G", (130, 2 * size(o)), lambda g, T: g.iota(get(T, o), pat, base, cm, **kw), [], [o])

    def aff(o, i, pat, op, base, cm, other=0.0):
        add("G", (170, 2 * size(o)), lambda g, T: g.affine_select(get(T, o), get(T, i), pat, op, other, base, cm), [i], [o])

    fill(R("on32"), 1.0)
    iota(R("pidx"), [[0, 1]], 0, 1)
    aff(R("boa"), R("on32"), [[-16, 8], [0, 16]], A.is_ge, 0, 1)
    aff(R("bo32"), R("boa"), [[16, 8], [0, 16]], A.is_ge, 15, -1)
    aff(R("id32"), R("on32"), [[-1, 128]], A.is_equal, 0, 1)
    fill(R("rowc", S_(256, 768)), 0.0)
    iota(R("rowc", S_(0, 256)), [[0, 16], [-1, 16]], 16)
    ts(R("pmi"), R("pidx"), 15, A.bitwise_and)
    cp(R("pmf"), R("pmi"))
    pm = R("pmf", S_(0, 1))
    ts(R("Mk"), R("rowc", blk(0, 256)), pm, A.subtract, 0.0, A.is_le)
    act(R("BO"), R("bo32"), F.Copy)
    act(R("I"), R("id32"), F.Copy)
    fill(R("clkw", S_(1, 16)), -1.0)
    fill(R("clkw", S_(0, 1)), 0.0)
    for n, k in KS:
        act(R(n), R("bo32" if n[0] == "B" else "id32"), F.Copy, scale=float(k))
    BO8 = R("BO", S_(0, 128, 16))
    if OPT["kn"] == 2:
        fill(R("KB"), 0.0)
        for i in (0, 1):
            ts(R("KB", i, blk(i, 8)), BO8, 16.0, A.mult)
            ts(R("KB", i, blk(2 + i, 8)), BO8, -2.0, A.mult)
    else:
        ts(R("K1", blk(0, 8)), BO8, 16.0, A.mult)
        ts(R("K1", blk(1, 8)), BO8, -2.0, A.mult)
    for i, x in enumerate((0.0, 2047.0, 4096.0)):
        fill(R("LC", blk(i, 16)), x)
    fill(R("Zs"), 0.0)
    cp(R("Zs", S_(15, 143, 16)), BO8)
    fill(R("rst"), 1.0)
    fill(R("rst", S_(0, 1024, 16)), 0.0)
    aff(R("dd"), R("rowc", S_(512, 656)), [[-1, 144]], A.not_equal, 0, 1, 2.0)
    for r in range(1, 16):
        aff(R("d2", r), R("dd", S_(r, 128 + r)), [[-1, 128]], A.not_equal, 0, 1, -2.0)
    for i in (0, 1):
        aff(R("sk8", i, blk(0)), R("rowc", blk(3)), [[-16, 4], [0, 2], [-1, 16]], A.not_equal, 64 * i - 64, 1, -1.0)
        for n in (128, 256, 512):
            aff(R("sk8", i, S_(n, 2 * n)), R("sk8", i, S_(0, n)), [[0, n]], A.is_ge, 0, 0)
        aff(R("sk8", i), R("sk8", i), [[-1, 8], [-8, 8], [0, 16]], A.not_equal, -64 * i, 1, 1.0)
    ts(R("q0"), pm, 1024.0, A.add)
    act(R("Q", 0, blk(2, 256)), R("zl"), F.Copy)
    fill(R("one"), 1.0)
    cp(R("pf", S_(0, 1)), R("pidx"))
    for x, pat in enumerate(([[4, 4], [16, 8], [0, 4]], [[0, 4], [16, 8], [4, 4]])):
        iota(R("io", blk(x)), pat, 0)
        for b in range(4):
            ts(R("sp", 4 * x + b), R("io", blk(x)), float(b), A.add, R("pf", S_(0, 1)), A.is_equal)
    Wd, Wt = R("W2", S_(0, 32), 0), R("W2", S_(0, 32), 1)
    aff(Wd, R("one", S_(0, 32)), [[-1, 32]], A.is_equal, 0, 1)
    for jj in range(1, 4):
        aff(Wd, Wd, [[-1, 32]], A.not_equal, -32 * jj, 1, 1.0)
    aff(Wt, R("one", S_(0, 32)), [[-4, 8], [-32, 4]], A.is_ge, 0, 1)
    aff(Wt, Wt, [[4, 8], [32, 4]], A.is_ge, 3, -1)

    def lists(buf, t, x, i=None):
        return R(buf, t, blk(x, 256) if i is None else blk(2 * x + i))
    ts(R("tli"), R("tli"), 4095 - 2 ** 31, A.bitwise_and)
    ts(lists("Fin", 0, 0), R("tli"), -2047.0, A.add, -2050.0, A.max)
    ts(R("tt", 0), lists("Fin", 0, 0), 2063.0, A.add)
    ts(lists("Fin", 0, 1), R("dli"), -2047.0, A.add)
    ts(R("thn"), R("thi"), -1.0, A.mult, -40.5, A.add)
    cp(R("nlim", S_(0, 1)), R("thn"))
    ts(R("sti"), R("sti"), 4095 - 2 ** 31, A.bitwise_and)
    if OPT["scs"]:
        iota(R("idi"), [[16, 64]], 0)
        ts(R("idu"), R("idi"), pm, A.add)
        for k in range(2):
            gat("S", R("scw", blk(k, 512)), R("sci"), R("idu", blk(k, 32)))
    else:
        cp(R("scw", S_(0, 1024)), R("sci"))

    WIN = R("clkw")
    I, In, I4160n, BO, I2080n, I4096, I64, NG, KTn = [R(n) for n in "I In I4160n BO I2080n I4096 I64 NG KTn".split()]
    sent = {}

    def arrive(t, kind, x):
        add("R", (0,), None, [], [x], tok="a%d%s" % (t, kind), after=sent[(t - 1, kind)], xl=0.0)

    def send(t, kind, src, land):
        sent[(t, kind)] = add("G", (ISSUE + 256 * size(src) / RATE,), None, [src], [], src=src, land=land, tok="a%d%s" % (t + 1, kind), by=256 * size(src))

    def rows(buf, j, i):
        return R(buf, blk(2 * j + i))

    def spread(x, src, t):
        if t:
            return move([(R("Ds", x) + (blk(jj, 32),), src) for jj in range(4)], [src], [R("Ds", x)], "d%d" % x, 256)
        for q in (0, 1):
            b = tmp("v", 4)
            mm([(R(b, blk(i, 256)), R("sp", 4 + 2 * q + i), src, True, True) for i in (0, 1)])
            act(R("Ds", x, blk(q, 512)), R(b), F.Copy)

    def member(src, x, eq, pairs):
        b = {}
        for y, a in pairs:
            for q in ([y // 2] if eq == "eqB" else [0, 1]):
                if q not in b:
                    b[q] = tmp("v", 4)
                    mm([(R(b[q], blk(i, 256)), R("sp", 2 * q + i), src, True, True) for i in (0, 1)])
            tt(R(eq, blk(4 * y + a, 256)), R("Ds", x, blk(a, 256)), R(b[y // 2], blk(y % 2, 256)), A.is_equal)

    def emptied(o, t, x, i):
        return [(o, lists("Fin", t, x, i), I64), (o, lists("Can", t, x, i), R("I64n"))]

    def stageA(t):
        Tf, Df = lists("Fin", t, 0), lists("Fin", t, 1)
        if t:
            arrive(t, "t", R("tt", t))
            ts(lists("Can", t, 0), R("tt", t), -2063.0, A.add)
            arrive(t, "e", lists("Can", t, 1))
            arrive(t, "f", Tf)
            arrive(t, "d", Df)
            arrive(t, "z", R("Q", t, blk(2, 256)))
        for q in range(OPT["ny"]):
            gat("S", R("Y", blk(q, 4096 // OPT["ny"])), WIN, R("tt", t, blk(q, 256 // OPT["ny"])))
        move([(half(R("PS", blk(i, 256)), 1 - i), half(Tf, i)) for i in (0, 1)], [Tf], [R("PS")], "tp", 64)
        for h in (0, 1):
            b = tmp("v", 4)
            mm([(R(b, S_(i, 512, 4)), I, R("Q", t, blk(4 + h)), True, True) for i in range(4)])
            for y in (0, 1):
                for q in range(4):
                    c = S_(2048 * h + 1024 * y + q, 2048 * h + 1024 * y + 1024, 4)
                    tt(R("MN", c), R("Y", c), R(b, blk(y, 256)), A.min)
        spread(1, Df, t)
        if t:
            spread(0, lists("Can", t, 1), t)
        member(lists("Can", t, 0) if t else Tf, 0 if t else 1, "eqA", PAIRS)
        b = tmp("c", 4)
        lst = [(R(b, blk(i, 32), S_(a, 5 + y, 4 + y - a)), rows("eqA", 4 * y + a, i), R("W2")) for y, a in PAIRS for i in (0, 1)]
        if t:
            lst += [m for x in (0, 1) for i in (0, 1) for m in emptied(R(b, blk(i, 32), blk(x, 4)), t, 1 - x, i)]
        group(lst, 8, 16, 24, 32)
        act(R("cmD"), R(b, S_(0, 64), blk(0, 4)), F.Sign, bias=-0.5)
        act(R("cmA"), R(b, S_(0, 64), blk(1, 4)), F.Sign, bias=-0.5)
        ts(R("D1"), total((I, Df), *turned("cmD", I2080n)), -2080.0, A.add, -2112.0, A.max)
        ts(R("nk"), R("D1"), -2047.5, A.is_le, -0.5, A.add)
        ts(R("D1u"), R("D1"), -2048.0, A.max, 2063.0, A.add)
        for a, y, e in zip((0,) + OPT["xp"], OPT["xp"] + (256,), OPT["xv"]):
            gat(e, R("XG", S_(16 * a, 16 * y)), WIN, R("D1u", S_(a, y)))
        for q in range(4):
            scan(R("xs", blk(q, 1024)), R("rst"), R("XG", blk(q, 1024)))

    def stageB(t):
        Tf = lists("Fin", t, 0)
        n = OPT["kn"]
        for h in range(0, 2, n):
            b, w = tmp("m", 2 * n), 128 * n
            kk, d, c = R(b, blk(0, w)), R(b, blk(1, w)), blk(h, w)
            lst = [(kk, I, R("rowc", blk(0, w)))] + [(R(b, blk(n + i)), R("Q", t, blk(4 + h + i)), BO) for i in range(n)]
            for i in range(n):
                x, KB = 2048 * (h + i), R("KB", i) if n == 2 else R("K1")
                lst += [(R(b, S_(w + 128 * i + j, w + 128 * i + 128, 16)), R("Y", S_(x + j, x + 2048, 16)), BO8) for j in range(16)]
                lst += [(R(b, S_(j, 2 * w, 16)), R("MN", S_(x + j, x + 2048, 16)), KB) for q in range(4) for j in range(q, 16, 4)]
            cuts = list(range(1 + n, len(lst), 8))
            if t:
                lst[cuts[-1]:cuts[-1]] = [m for i in range(n) for m in emptied(R(b, blk(n - 1 - i)), t, 0, h + n - 1 - i)]
                cuts.append(cuts[-1] + 2 * n)
            group(lst, *cuts)
            rs, back = R("rst", S_(0, w)), S_(c.stop - 1, c.start - 1 if c.start else None, -1)
            scan(R("sk", c), rs, kk)
            scan(R("sk2", back), rs, R("sk", back))
            tt(R("oh", c), R("sk2", c), kk, A.is_equal)
            act(R("dst", c), d, F.Copy, bias=-2040.0)
        d = tmp("m", 2)
        mm([m for i in (0, 1) for m in chain(d, (R("dst", blk(i)), In, blk(i)), turned("cmA", I2080n)[i])])
        act(R("FC"), R(d), F.Sign, bias=R("nlim", S_(t, t + 1)), scale=-1.0)
        FC, XS, o1 = R("FC"), R("Q", t, blk(0, 256)), tmp("m", 2)
        mm([(R(o1, blk(i)), R("oh", blk(i)), I, True, True) for i in (0, 1)])
        tt(R("Q", t, blk(1, 256)), Tf, R(o1), A.mult)
        cp(XS, total((In, R("nk")), (I64, FC), *turned("oh", I64)))
        L = tmp("m", 1)
        mm(chain(L, *([(R("Zs", S_(15 - r, 143 - r)), R("Q", t, S_(r, 768, 16)), S_(0, 48)) for r in range(16)] + [(I, R("LC"), S_(0, 48))])))
        X, E, U = [R(L, blk(i, 16)) for i in range(3)]
        lo, hi = blk(0, 16), blk(1, 16)
        ts(R("AS"), X, -967.5, A.is_gt, 16384.0, A.mult)
        tt(R("nu", lo), R("AS"), E, A.add)
        tt(R("nu", hi), R("nu", lo), U, A.max)
        ts(R("npr"), X, -968.0, A.is_equal, -1056.0, A.mult)
        ts(R("nlu"), R("nu", lo), 16.0 - 16384.0, A.add)
        ts(R("nv"), R("nu"), 1023, A.bitwise_and)
        cp(R("wu"), R("nv", hi))
        gat("V", R("sw"), R("sti"), R("wu"), -2047.0, -2050.0)
        gat("S", R("cw"), R("scw", S_(0, 1024)), R("wu"), -2047.0)
        gat("S", R("ysb"), WIN, R("nlu"))
        tt(R("PV"), R("nv", lo), R("npr"), A.add)
        ts(NG, total((BO, XS), (R("BO128n"), FC)), 1080.5, A.is_lt, 2.0, A.mult)
        p = total((I, Tf), *(turned("cmA", I2080n) + turned("oh", I4160n)))
        act(KTn, p, F.Sign, bias=32.5, scale=-1.0)
        act(R("T1s"), p, F.Relu, bias=-32.0)
        if t + 1 < NV:
            act(R("acr"), total((In, R("D1")), (R("BO128n"), FC)), F.Relu, bias=-64.0, scale=1.0 / 64, acc=R("asum", S_(t, t + 1)))
            a = tmp("m", 1)
            mm(chain(a, (R("bo32"), R("asum", S_(t, t + 1)), S_(0, 1))))
            if t:
                ts(R("ai"), R("a31"), R(a, S_(0, 1)), A.add)
            else:
                cp(R("ai"), R(a, S_(0, 1)))
            ts(R("a31"), R("ai"), 31, A.bitwise_and)
            ts(R("nlim", S_(t + 1, t + 2)), R("a31"), -8.0, A.mult, R("thn"), A.add)

    def stageC(t):
        last = t == NV - 1
        tc, dc, sT, sd = [lists(b, t, x) for b in ("sC", "sF") for x in (0, 1)]
        p1 = total((I2080n, R("one")), (I, lists("Fin", t, 0)), (I2080n, KTn), (I4160n, NG))
        if not last:
            tt(R("eqn"), R("sw"), total((BO, R("Q", t, blk(1, 256)))), A.is_equal)
        tt(R("C1t"), R("sw"), total((R("I17"), NG), (R("I16"), KTn), *[(R("I69n"), R("eqn"))] * (not last)), A.min)
        tt(tc, R("C1t"), p1, A.max)
        if not last:
            ts(R("stt", t), tc, -2062.0, A.max, 2063.0, A.add)
            send(t, "t", R("stt", t), R("tt", t + 1))
            p1 = total((I, R("D1")), (I4160n, NG))
            tt(R("C1"), R("cw"), total((I4096, NG), (I4096, R("nk"))), A.min)
            tt(dc, R("C1"), p1, A.max)
            send(t, "e", dc, lists("Can", t + 1, 1))
        for i in (0, 1):
            o, x = half(R("PS", blk(i, 256)), i), half(R("sw"), i)
            move([(o, x)], [x], [o], "tq%d" % i, 32)
        for q in range(8):
            b = tmp("v", 4)
            mm([(R(b, blk(i, 256)), R("sk8", q // 4, blk(2 * (q % 4) + i)), R("PS", blk(q // 4, 256)), True, True) for i in (0, 1)])
            act(R("fC", blk(q, 512)), R(b), F.Tanh, bias=0.0156263, scale=16.0)
        b = tmp("m", 2)
        mm([(R(b, S_(128 * i + 64 * (j // 8) + j % 8, 128 * i + 64 * (j // 8) + 64, 8)), rows("fC", j, i), BO8, True, True)
            for j in range(16) for i in (0, 1)], 16, 24)
        act(R("rC", blk(0, 256)), R(b), F.Copy, bias=-192.49, scale=-1.0)
        act(R("rC", blk(1, 256)), R(b), F.Copy, bias=193.0)
        tt(sT, tc, total((R("I8192"), NG), (R("I4096n"), KTn), *(turned("rC", R("I8192")) + turned("rC", R("I8192"), 2))), A.min)
        if last:
            ts(R("ot"), sT, 2047.0, A.add, -1.0, A.max)
            out("yt", "ot", 256)
        else:
            send(t, "f", sT, lists("Fin", t + 1, 0))
        member(R("cw"), 1, "eqB", sorted(PAIRS))
        b = tmp("m", 2)
        mm([m for y in range(4) for i in (0, 1) for m in
            chain(b, *[(rows("eqB", 4 * y + a, i), Wt, S_(128 * i + y, 128 * i + 128, 4)) for a in range(4)])], 8, 16, 24)
        if last:
            act(R("cmB"), R(b), F.Sign, scale=-1.0)
            p1 = total((I, R("D1")), (I4160n, NG))
            tt(R("C1"), R("cw"), total((I4096, NG), (I4096, R("nk")), *turned("cmB", I4096)), A.min)
            tt(sd, R("C1"), p1, A.max)
            ts(R("od"), sd, 2047.0, A.add, -1.0, A.max)
            out("yd", "od", 256)
        else:
            act(R("cmB"), R(b), F.Relu, bias=1.0, scale=-1.0)
            tt(sd, dc, total((I4096, NG), (R("I4096n"), R("nk")), *turned("cmB", I4096)), A.min)
            send(t, "d", sd, lists("Fin", t + 1, 1))
        Z, ys = R("Q", t, blk(2, 256)), R("ysb")
        ts(R("hf"), total((R("I15"), ys), (In, Z), (I4160n, NG), (R("Ih"), R("xs", S_(15, 4096, 16)))), 1535.75, A.add, 1024.0, A.max)
        act(R("oz") if last else R("sz", t), total((I, Z), (In, ys), (R("I256"), NG), (I, R("hf"))), F.Abs, bias=-1536.0)
        if last:
            out("yz", "oz", 256)
        else:
            send(t, "z", R("sz", t), R("Q", t + 1, blk(2, 256)))

    def stageD(t):
        b, c, PV = tmp("m", 2), tmp("m", 1), R("PV")
        mm([(R(b, S_(r, 256, 16)), R("d2", r) if r else I, PV, True, True) for r in range(16)])
        tt(R("eqP"), R("Mk"), R(b), A.is_equal)
        scan(R("eqS"), R("rst", S_(0, 256)), R("eqP"))
        mm(chain(c, (I, PV, S_(0, 16)), (I4096, R("eqS", S_(15, 256, 16)), S_(0, 16))))
        ts(R("PLu", S_(0, 32, 2)), R(c, S_(0, 16)), 1056.0, A.add, R("q0"), A.min)
        for c in range(16):
            o, offs, src = R("scw"), R("PLu", S_(2 * c, 2 * c + 1)), R("T1s", blk(c, 16))
            add("V", (60, 0, 0, 16), lambda g, T, o=o, offs=offs, src=src: g.vector.tensor_scalar(
                get(T, o).indirect(get(T, offs)), get(T, src), 1.0, -1.0, A.mult, A.add), [offs, src], [o])
        if t == NV - 1:
            out("ys", "scw", 1024)

    for t in range(NV):
        for s, f in (("A", stageA), ("B", stageB), ("C", stageC), ("D", stageD)):
            lab[0] = s + str(t)
            f(t)
    return ops


def depend(ops):
    hist = {}
    for i, o in enumerate(ops):
        pw, seq, acc = set(), set(), {}
        for x, wr in [(x, False) for x in o["r"]] + [(x, True) for x in o["w"]]:
            sp = tuple(s[:3] for s in span(x))
            acc[(x[0], sp)] = acc.get((x[0], sp), False) or wr
        for (name, sp), wr in acc.items():
            for j, sj, wj in hist.get(name, ()):
                if j != i and name in TEMP and o["e"] == ops[j]["e"] == "P":
                    seq.add(j)
                elif j != i and (wj or wr) and meet(sp, sj):
                    pw.add(j)
        for (name, sp), wr in acc.items():
            h = hist.setdefault(name, [])
            if wr:
                h[:] = [y for y in h if y[0] == i or not cover(sp, y[1])]
            h.append((i, sp, wr))
        o["pw"], o["seq"] = pw, seq
        o["t"] = sorted({x[0] for x in o["r"] + o["w"] if psum(x)})


def schedule(ops):
    n = len(ops)
    pred, succ = [], [[] for _ in range(n)]
    for i, o in enumerate(ops):
        pred.append([(j, WAKE if ops[j]["e"] != o["e"] else SELF) for j in o["pw"]] + [(j, 0.0) for j in o["seq"]] +
                    ([(o["after"], REMOTE)] if "after" in o else []))
        for j, l in pred[i]:
            succ[j].append((i, l))
    fin = [o["d"] + LAT * o.get("lat", 0.0) for o in ops]
    steps, key = {}, [None] * n
    for i, o in enumerate(ops):
        if o["n"] in PLAN or o["n"] + o["g"][1:] in PLAN:
            steps.setdefault((o["n"], int(o["g"][1:] or 0)), []).append(i)
    for (name, t), l in steps.items():
        a, b = PLAN.get(name + str(t)) or PLAN[name]
        for k, i in enumerate(l):
            key[i] = 1000 * (t * PLAN["P"] + a + b * k / max(1, len(l) - 1))
    for i in range(n - 1, -1, -1):
        if key[i] is None:
            key[i] = min([key[k] - PLAN["mu"] * (fin[i] + l) for k, l in succ[i]] or [1000 * PLAN["P"] * (int(ops[i]["g"][1:] or 0) + 1.3)])
    best = forward(ops, pred, succ, fin, [-a for a in key])
    for _ in range(ROUNDS - 1):
        best = forward(ops, pred, succ, fin, backward(ops, pred, succ, fin, best[2]))
    PLACE.update(best[4])
    for i, o in enumerate(ops):
        o["s"], o["pw"] = best[2][i] - fin[i], o["pw"] | best[3][i]
    return best[1]


def pick(ops, st, pri, look):
    a = min(st, key=lambda j: st[j] + ops[j]["d"])
    same = [j for j in st if ops[j]["e"] == ops[a]["e"]]
    lo = min(st[j] for j in same)
    return max((j for j in same if st[j] <= lo + look * (st[a] + ops[a]["d"] - lo)), key=lambda j: pri[j])


def backward(ops, pred, succ, fin, pri):
    cnt, rdy, free, out = [len(x) for x in succ], [0.0] * len(ops), {}, [0.0] * len(ops)
    ready = [i for i in range(len(ops)) if cnt[i] == 0]
    while ready:
        st = {i: max(rdy[i] + fin[i] - ops[i]["d"], free.get(ops[i]["e"], 0.0)) for i in ready}
        i = pick(ops, st, pri, LOOKB)
        ready.remove(i)
        out[i] = st[i] + ops[i]["d"]
        if ops[i]["e"] != "R":
            free[ops[i]["e"]] = out[i]
        for k, l in pred[i]:
            cnt[k] -= 1
            rdy[k] = max(rdy[k], out[i] + l)
            if cnt[k] == 0:
                ready.append(k)
    return out


def forward(ops, pred, succ, fin, pri):
    n = len(ops)
    cnt, users, PLACE, more = [len(x) for x in pred], {}, {}, {}
    for o in ops:
        for x in o["t"]:
            users[x] = users.get(x, 0) + 1
    rdy, free, order, end = [0.0] * n, {}, [], {}
    last = [{} for _ in range(8)]
    lock = [None] * 8
    held = [[None] * 4 for _ in range(8)]
    past = [[{} for _ in range(4)] for _ in range(8)]

    def start(i):
        o = ops[i]
        s, new, pw = max(rdy[i], free.get(o["e"], 0.0)), {}, set()
        for x in o["t"]:
            if x in PLACE:
                opts = [PLACE[x]]
            else:
                role, m = TEMP[x]
                opts = [(b, a) for b in BANKS[role] for a in range(0, 5 - m, m) if all(held[b][c] is None for c in range(a, a + m))]
            best = None
            for b, a in opts:
                if o["e"] == "P" and lock[b] not in (None, x):
                    continue
                w = {j for e, j in last[b].items() if e != o["e"]}
                if x not in PLACE:
                    w |= {j for c in range(a, a + TEMP[x][1]) for j in past[b][c].values()}
                s1 = max([s] + [end[j] + WAKE for j in w])
                if best is None or s1 < best[0]:
                    best = (s1, (b, a), w)
            if best is None:
                return None
            s, new[x] = best[0], best[1]
            pw |= best[2]
        return s, new, pw
    ready = [i for i in range(n) if cnt[i] == 0]
    while ready:
        st = {i: start(i) for i in ready}
        can = [i for i in ready if st[i]]
        if not can:
            return 1e30, order, [end.get(i, 1e9) for i in range(n)]
        i = pick(ops, {j: st[j][0] for j in can}, pri, LOOK)
        ready.remove(i)
        o = ops[i]
        s, new, more[i] = st[i]
        end[i] = s + fin[i]
        for x, (b, a) in new.items():
            PLACE[x] = (b, a)
            users[x] -= 1
            last[b][o["e"]] = i
            if o["e"] == "P":
                lock[b] = x if o["open"] else None
            for c in range(a, a + TEMP[x][1]):
                held[b][c] = x if users[x] else None
                past[b][c][o["e"]] = i
        if o["e"] != "R":
            free[o["e"]] = s + o["d"]
        order.append(i)
        for k, l in succ[i]:
            cnt[k] -= 1
            rdy[k] = max(rdy[k], end[i] + l)
            if cnt[k] == 0:
                ready.append(k)
    return max(end.values()), order, end, more, PLACE


CACHE = []


def rank_program(g, core, T, topo):
    rank = T.rank_of(core)
    if rank is None:
        return
    dst = T.cores[(rank + 1) % len(T.cores)]
    rid, pid = topo.addr(dst)[:2]
    mask, nout = topo.mask(core, dst), len(topo.engines(core, dst))
    nin = len(topo.engines(T.cores[rank - 1], core))
    if not CACHE:
        ops = program()
        depend(ops)
        CACHE.extend((ops, schedule(ops)))
    ops, order = CACHE
    queue = {"V": g.vector, "S": g.scalar, "P": g.tensor, "G": g, "Y": g.sync}
    sem = {"V": "sv", "S": "ss", "P": "sp", "G": "sg"}
    known, vc, tok, total = {e: {} for e in queue}, {}, {}, {"ls": 0}
    for i in order:
        o = ops[i]
        e = o["e"]
        if e == "R":
            tok[i], vc[i] = (o["tok"], nin), {}
            total[o["tok"]] = nin
            continue
        kn, need = known[e], {}
        for j in o["pw"]:
            need[tok[j][0]] = max(need.get(tok[j][0], 0), tok[j][1])
        for j in sorted(o["pw"], reverse=True):
            s = tok[j][0]
            if kn.get(s, 0) < need[s]:
                queue[e].wait_ge(T.sem[s], need[s])
                kn[s] = need[s]
            for a in vc[j]:
                kn[a] = max(kn.get(a, 0), vc[j][a])
        if "land" in o:
            g.remote_dma(out_ap=get(T, o["land"]), in_ap=get(T, o["src"]), remote_sem=T.sem[o["tok"]], local_sem=T.sem["ls"],
                         pid=pid, routing_id=rid, dma_engine_mask=mask)
            total["ls"] += nout
            continue
        x = o["fn"](g, T)
        s, n = (o["tok"], 16) if "tok" in o else (sem[e], 1)
        for y in x if isinstance(x, list) else [x]:
            total[s] = total.get(s, 0) + n
            y.then_inc(T.sem[s], n)
        tok[i], vc[i] = (s, total[s]), dict(kn)
    for s in total:
        if total[s]:
            g.wait_ge(T.sem[s], total[s])
